import numpy as np
import ml_dtypes


def mxq(x, axis, fmt="e4m3"):
    dtype, down = {"e4m3": (ml_dtypes.float8_e4m3fn, 7), "e5m2": (ml_dtypes.float8_e5m2, 14)}[fmt]
    v = np.moveaxis(np.asarray(x, np.float32).astype(ml_dtypes.bfloat16).astype(np.float64), axis, -1)
    blocks = v.reshape(v.shape[:-1] + (-1, 32))
    amax = np.abs(blocks).max(-1, keepdims=True)
    byte = np.maximum(np.where(amax > 0, np.frexp(amax)[1] - 1 + 127, 0) - down, 1)
    scale = np.exp2(byte - 127.0)
    codes = (blocks / scale).astype(np.float32).astype(dtype).astype(np.float64)
    return np.moveaxis((codes * scale).reshape(v.shape), -1, axis)


WIDE = False


def mx_kscale(k):
    if not WIDE:
        return np.ones(k)
    levels = np.array([10, -10, 5, -5, 0])
    if k % 512:
        return np.exp2(np.random.permutation(np.resize(levels, k // 32))).repeat(32)
    a = np.empty((k // 512, 16))
    for p in range(k // 512):
        a[p, :8] = np.random.permutation(np.resize(levels, 8))
        for g in range(8):
            far = levels[np.abs(levels - a[p, g]) >= 10]
            a[p, g + 8] = far[np.random.randint(len(far))]
    return np.exp2(a.ravel()).repeat(32)


def f64(x):
    return np.asarray(x).astype(np.float64)


def striped(idx):
    return np.tile(idx.reshape(-1, 16).T, (8, 1)).astype(np.uint16)


def unstriped(offs):
    return offs[:16].T.reshape(-1).astype(np.int64)


E2M1 = np.array([0.0, 0.5, 1.0, 1.5, 2.0, 3.0, 4.0, 6.0, -0.0, -0.5, -1.0, -1.5, -2.0, -3.0, -4.0, -6.0])


def pack_weight(w, fmt):
    k, n = w.shape
    w = f64(np.asarray(w, np.float32).astype(ml_dtypes.bfloat16)).reshape(k // 32, 32, n)
    amax = np.abs(w).max(1)
    if fmt == "e4m3":
        byte = np.frexp(amax)[1] - 1 + 127 - 7
    else:
        mant, ex = np.frexp(amax / 6.0)
        byte = np.where(mant > 0.5, ex, ex - 1) + 127
    byte = np.clip(np.where(amax > 0, byte, 1), 1, 254)
    scaled = (w * np.exp2(127.0 - byte)[:, None, :]).reshape(k, n).astype(np.float32)
    by_word = np.ascontiguousarray(scaled.reshape(k // 512, 128, 4, n).transpose(0, 1, 3, 2))
    if fmt == "e4m3":
        words = by_word.astype(ml_dtypes.float8_e4m3fn).view(np.uint8)
    else:
        c = by_word.astype(ml_dtypes.float4_e2m1fn).view(np.uint8) & 0xF
        words = (c[..., 0::2] | (c[..., 1::2] << 4)).reshape(k // 512, 128, 2 * n)
    return np.ascontiguousarray(words), np.ascontiguousarray(byte.astype(np.uint8).reshape(k // 512, 16, n))


def unpack_weight(words, scales, fmt):
    g, _, n = scales.shape
    words = np.ascontiguousarray(words).reshape(g, 128, n, -1)
    if fmt == "e4m3":
        vals = words.view(ml_dtypes.float8_e4m3fn).astype(np.float64)
    else:
        nib = np.empty((g, 128, n, 4), np.uint8)
        nib[..., 0::2] = words & 0xF
        nib[..., 1::2] = words >> 4
        vals = E2M1[nib]
    vals = vals * np.repeat(np.exp2(scales.astype(np.float64) - 127.0), 8, axis=1)[..., None]
    return vals.transpose(0, 1, 3, 2).reshape(g * 512, n)


def gelu(v):
    return 0.5 * v * (1.0 + np.tanh(np.sqrt(2.0 / np.pi) * (v + 0.044715 * v**3)))


K, T, S, H, T2, P, N = 512, 4096, 1024, 1024, 2048, 1024, 512

def setup_inputs():
    n = np.random.standard_normal
    s = mx_kscale(K)[:, None]
    u = mx_kscale(H)[:, None]
    tab_words, tab_scales = pack_weight(n((K, T)) * s, "e4m3")
    w2_words, w2_scales = pack_weight(1.5 * n((H, N)) / np.sqrt(H) / u, "e2m1")
    return {
        "tab_words": tab_words, "tab_scales": tab_scales,
        "offs": striped(np.random.permutation(T)[:S]),
        "offs2": striped(np.random.permutation(T2)[:S]),
        "offs3": striped(np.random.permutation(T2)[:P]),
        "offs4": striped(np.random.permutation(T2)[:P]),
        "w1": (n((K, H)) / np.sqrt(K) / s * u.T).astype(np.float32),
        "wgs": np.exp(0.3 * n((128, S))).astype(np.float32),
        "page0": (n((H, T2)) * u).astype(np.float32),
        "rate": (np.exp(0.3 * n(H)) / u[:, 0]).astype(np.float32),
        "w2_words": w2_words, "w2_scales": w2_scales,
        "w3": (1.5 * n((H, N)) / np.sqrt(H) / u).astype(np.float32),
    }

def reference(tab_words, tab_scales, offs, offs2, offs3, offs4, w1, wgs, page0, rate, w2_words, w2_scales, w3):
    v = unpack_weight(tab_words, tab_scales, "e4m3")[:, unstriped(offs)]
    h = mxq(f64(w1), 0, "e4m3").T @ v
    page = f64(page0).copy()
    page[:, unstriped(offs2)] = np.tile(f64(wgs), (H // 128, 1)) * h
    x1 = page[:, unstriped(offs3)]
    x2 = page[:, unstriped(offs4)]
    z = x1 * (1.0 / (1.0 + np.exp(-f64(rate)[:, None] * x2)))
    zq = mxq(z, 0, "e4m3")
    y1 = unpack_weight(w2_words, w2_scales, "e2m1").T @ zq
    y2 = mxq(f64(w3), 0, "e4m3").T @ zq
    return y1 * np.tanh(y2)

@@ -1,0 +1,308 @@
+from contextlib import ExitStack
+
+import concourse.mybir as mybir
+
+K, T, S, H, T2, PAIRS, N = 512, 4096, 1024, 1024, 2048, 1024, 512
+FLOPS = 2 * K * H * S + 2 * 2 * H * N * PAIRS
+
+F32 = mybir.dt.float32
+BF16 = mybir.dt.bfloat16
+I32 = mybir.dt.int32
+U32 = mybir.dt.uint32
+U16 = mybir.dt.uint16
+U8 = mybir.dt.uint8
+FP8X4 = mybir.dt.float8_e4m3fn_x4
+FP4X4 = mybir.dt.float4_e2m1fn_x4
+MULT = mybir.AluOpType.mult
+SIGMOID = mybir.ActivationFunctionType.Sigmoid
+TANH = mybir.ActivationFunctionType.Tanh
+
+P = 128
+PACK = 4
+PASS = P * PACK
+BANK = 512
+CHUNK = 256
+CHUNKS = PAIRS // CHUNK
+TILES = H // P
+
+
+def list_slice(offsets, start, stop):
+    return offsets[:, start // 16 : stop // 16]
+
+
+def tile_list_hero_villain_reads_kernel(
+    tc, tab_words, tab_scales, offs, offs2, offs3, offs4, w1, wgs, page0, rate, w2_words, w2_scales, w3, out
+):
+    nc = tc.nc
+    with ExitStack() as ctx:
+        lists = ctx.enter_context(tc.tile_pool(name="lists", bufs=1))
+        keep = ctx.enter_context(tc.tile_pool(name="keep", bufs=1))
+        ring = ctx.enter_context(tc.tile_pool(name="ring", bufs=2))
+        psum = ctx.enter_context(tc.psum_pool(name="psum", bufs=1))
+
+        def held(shape, dtype, name, tag=None):
+            return keep.tile(shape, dtype, name=name, tag=tag or name, align_bytes=64)
+
+        def bank(index, name):
+            return psum.tile([P, BANK], F32, name=name, tag="bank%d" % index)
+
+        table_scales = held([P, T], U8, "table_scales")
+        nc.vector.memset(table_scales[:].bitcast(I32), 0)
+        w2_plane = held([P, 2, N], U8, "w2_plane")
+        nc.vector.memset(w2_plane[:].rearrange("p a c -> p (a c)").bitcast(I32), 0)
+
+        def load_list(src, name):
+            tile = lists.tile([P, S // 16], U16, name=name)
+            nc.sync.dma_start(tile[:], src)
+            return tile
+
+        def load_w1(b):
+            raw = held([P, PACK, PASS], F32, "w1_raw%d" % b)
+            nc.sync.dma_start(raw[:], w1[:, PASS * b : PASS * (b + 1)].rearrange("(p j) c -> p j c", j=PACK))
+            return raw
+
+        def load_weight_rows(t):
+            tile = held([P, S], F32, "wgs%d" % t)
+            rows = wgs.rearrange("(q t) j -> t q j", t=PACK)[t]
+            for q in range(4):
+                nc.sync.dma_start(tile[32 * q : 32 * (q + 1), :], rows)
+            return tile
+
+        def load_page(u):
+            b, t = divmod(u, PACK)
+            tile = held([P, T2], F32, "page%d" % u)
+            nc.sync.dma_start(tile[:], page0.rearrange("(b p t) c -> b t p c", p=P, t=PACK)[b, t])
+            return tile
+
+        picks = load_list(offs, "picks")
+        w1_raw = [load_w1(0)]
+        for q in range(4):
+            nc.sync.dma_start(
+                table_scales[32 * q : 32 * q + 4, :].bitcast(I32), tab_scales[0, 4 * q : 4 * q + 4, :].bitcast(I32)
+            )
+        table_words = held([P, T], U32, "table_words")
+        nc.sync.dma_start(table_words[:].bitcast(I32), tab_words[0].rearrange("p n t -> p (n t)").bitcast(I32))
+        slots = load_list(offs2, "slots")
+        wg = [load_weight_rows(0)]
+        pages = [load_page(0)]
+        villains = load_list(offs4, "villains")
+        heroes = load_list(offs3, "heroes")
+        rates = held([P, 2, PACK], F32, "rates")
+        nc.sync.dma_start(rates[:], rate.rearrange("(b p t) -> p b t", p=P, t=PACK))
+        for t in range(1, PACK):
+            wg.append(load_weight_rows(t))
+            pages.append(load_page(t))
+            if t == 1:
+                w1_raw.append(load_w1(1))
+
+        v_scales = held([P, S], U8, "v_scales")
+        nc.vector.tensor_copy(v_scales[:], table_scales[:].indirect(picks[:]))
+
+        def quantise_w1(b, tag):
+            staged = held([P, PACK, P, PACK], BF16, "w1_staged%d" % b, tag)
+            nc.scalar.copy(
+                staged[:].rearrange("p t m j -> p m t j"), w1_raw[b][:].rearrange("p j (m t) -> p m t j", t=PACK)
+            )
+            codes = held([P, PASS], U32, "w1_codes%d" % b)
+            scales = held([P, PASS], U8, "w1_scales%d" % b)
+            nc.vector.quantize_mx(
+                out=codes[:].bitcast(FP8X4), scales=scales[:], in_=staged[:].rearrange("p t m j -> p (t m j)")
+            )
+            return codes, scales
+
+        w1_q = [quantise_w1(0, "w1_staged0")]
+        v_words = [held([P, BANK], U32, "v_words%d" % c) for c in range(2)]
+        for c in range(2):
+            nc.vector.tensor_copy(
+                v_words[c][:], table_words[:].indirect(list_slice(picks, BANK * c, BANK * (c + 1)))
+            )
+
+        w3_raw = held([P, 2, PACK, N], F32, "w3_raw", "table_words")
+        for a in range(2):
+            nc.sync.dma_start(w3_raw[:, a], w3[PASS * a : PASS * (a + 1), :].rearrange("(p j) n -> p j n", j=PACK))
+        for u in range(PACK, TILES):
+            pages.append(load_page(u))
+        w2_codes = held([P, 2, 2 * N], U8, "w2_codes")
+        nc.sync.dma_start(w2_codes[:].bitcast(I32), w2_words.rearrange("a p c -> p a c").bitcast(I32))
+        for q in range(4):
+            nc.sync.dma_start(
+                w2_plane[32 * q : 32 * q + 4, :, :].bitcast(I32),
+                w2_scales[:, 4 * q : 4 * q + 4, :].rearrange("a r c -> r a c").bitcast(I32),
+            )
+
+        lanes = held([P, (TILES + 1) * S], F32, "lanes")
+
+        def lane(i):
+            return lanes[:, S * i : S * (i + 1)]
+
+        def make_h(u):
+            b, t = divmod(u, PACK)
+            codes, scales = w1_q[b]
+            for c in range(2):
+                acc = bank((2 * u + c) % 4, "h_acc")
+                nc.tensor.matmul_mx(
+                    out=acc[:],
+                    lhsT=codes[:, P * t : P * (t + 1)].bitcast(FP8X4),
+                    lhsT_scale=scales[:, P * t : P * (t + 1)],
+                    rhs=v_words[c][:].bitcast(FP8X4),
+                    rhs_scale=v_scales[:, BANK * c : BANK * (c + 1)],
+                    start=True,
+                    stop=True,
+                )
+                nc.scalar.copy(lane(u)[:, BANK * c : BANK * (c + 1)], acc[:])
+
+        def scatter(u, start, stop):
+            nc.vector.tensor_tensor(
+                pages[u][:].indirect(list_slice(slots, start, stop)),
+                lane(u)[:, start:stop],
+                wg[u % PACK][:, start:stop],
+                MULT,
+            )
+
+        gates = {}
+
+        def make_gate(u, start, stop):
+            b, t = divmod(u, PACK)
+            if start == 0:
+                gates[u] = held([P, PAIRS], F32, "gate%d" % u, "gate%d" % t)
+            gate = gates[u][:, start:stop]
+            nc.vector.tensor_copy(gate, pages[u][:].indirect(list_slice(villains, start, stop)))
+            nc.scalar.activation(gate, gate, SIGMOID, scale=rates[:, b, t : t + 1])
+
+        def read_hero(u, start, stop, z):
+            nc.vector.tensor_tensor(
+                z, pages[u][:].indirect(list_slice(heroes, start, stop)), gates[u][:, start:stop], MULT
+            )
+
+        def interleave(staged, planes):
+            nc.scalar.copy(
+                staged.rearrange("p (c i) t -> p c t i", i=4), planes.rearrange("p t (c i) -> p c t i", i=4)
+            )
+
+        def quantise(staged, width, name):
+            codes = held([P, width], U32, name + "_codes")
+            scales = held([P, width], U8, name + "_scales")
+            nc.vector.quantize_mx(
+                out=codes[:].bitcast(FP8X4), scales=scales[:], in_=staged.rearrange("p m t -> p (m t)")
+            )
+            return codes, scales
+
+        def quantise_w3(a, tag):
+            staged = held([P, N, PACK], BF16, "w3_staged%d" % a, tag)
+            interleave(staged[:], w3_raw[:, a])
+            return quantise(staged[:], N, "w3_%d" % a)
+
+        w3_q = []
+        sums = {}
+
+        def multiply(c, b, z_codes, z_scales):
+            if b == 0:
+                first = 4 * ((c + 1) % 2)
+                sums[c] = [bank(first + i, "y_acc") for i in range(4)]
+            for half in range(2):
+                y2, y1 = sums[c][2 * half], sums[c][2 * half + 1]
+                for i in range(2):
+                    n = 2 * half + i
+                    nc.tensor.matmul_mx(
+                        out=y2[:, CHUNK * i : CHUNK * (i + 1)],
+                        lhsT=w3_q[b][0][:, P * n : P * (n + 1)].bitcast(FP8X4),
+                        lhsT_scale=w3_q[b][1][:, P * n : P * (n + 1)],
+                        rhs=z_codes.bitcast(FP8X4),
+                        rhs_scale=z_scales,
+                        start=(b == 0 and i == 0),
+                        stop=(b == 1 and i == 1),
+                    )
+                for i in range(2):
+                    n = 2 * half + i
+                    for s in range(2):
+                        nc.tensor.matmul_mx(
+                            out=y1[:, CHUNK * i + P * s : CHUNK * i + P * (s + 1)],
+                            lhsT=w2_codes[:, b, 2 * P * n : 2 * P * (n + 1)].bitcast(FP4X4),
+                            lhsT_scale=w2_plane[:, b, P * n : P * (n + 1)],
+                            rhs=z_codes[:, P * s : P * (s + 1)].bitcast(FP8X4),
+                            rhs_scale=z_scales[:, P * s : P * (s + 1)],
+                            start=(b == 0 and i == 0 and s == 0),
+                            stop=(b == 1 and i == 1 and s == 1),
+                        )
+
+        def finish(c):
+            for half in range(2):
+                y2, y1 = sums[c][2 * half], sums[c][2 * half + 1]
+                squashed = ring.tile([P, BANK], F32, name="squashed")
+                nc.scalar.activation(squashed[:], y2[:], TANH)
+                result = ring.tile([P, BANK], F32, name="result", bufs=4)
+                nc.vector.tensor_tensor(result[:], y1[:], squashed[:], MULT)
+                nc.sync.dma_start(
+                    out[2 * P * half : 2 * P * (half + 1), CHUNK * c : CHUNK * (c + 1)].rearrange(
+                        "(i p) m -> p i m", p=P
+                    ),
+                    result[:].rearrange("p (i m) -> p i m", i=2),
+                )
+
+        for u in range(PACK):
+            make_h(u)
+        scatter(0, 0, BANK)
+        scatter(0, BANK, S)
+        make_gate(0, 0, PAIRS)
+        for u in range(1, PACK + 1):
+            scatter(u, 0, S)
+            read_hero(u - 1, 0, PAIRS, lane(u))
+            if u < PACK:
+                make_gate(u, 0, PAIRS)
+            if u == 1:
+                w1_q.append(quantise_w1(1, "gate0"))
+                for later in range(PACK, TILES):
+                    make_h(later)
+            elif u < PACK:
+                w3_q.append(quantise_w3(u - 2, "gate%d" % (u - 1)))
+        make_gate(PACK, 0, PAIRS)
+        z0_staged = held([P, PAIRS, PACK], BF16, "z0_staged", "w1_raw0")
+        interleave(z0_staged[:], lanes[:, S : 5 * S].rearrange("p (t m) -> p t m", t=PACK))
+        z0_codes, z0_scales = quantise(z0_staged[:], PAIRS, "z0")
+
+        def first_pass(c):
+            cols = slice(CHUNK * c, CHUNK * (c + 1))
+            multiply(c, 0, z0_codes[:, cols], z0_scales[:, cols])
+
+        first_pass(0)
+        first_pass(1)
+
+        planes0 = lanes[:, 5 * S : 9 * S].rearrange("p (t m) -> p t m", t=PACK)[:, :, 0:CHUNK]
+        for u in range(PACK + 1, TILES):
+            scatter(u, 0, S)
+            read_hero(u - 1, 0, CHUNK, planes0[:, u - 1 - PACK, :])
+            if u < TILES - 1:
+                make_gate(u, 0, PAIRS)
+        last = TILES - 1
+        make_gate(last, 0, CHUNK)
+        make_gate(last, CHUNK, PAIRS)
+
+        def chunk_planes(c):
+            if c == 2:
+                start = last * S + CHUNK
+                return lanes[:, start : start + PACK * CHUNK].rearrange("p (t m) -> p t m", t=PACK)
+            tile = held([P, PACK, CHUNK], F32, "planes%d" % c, "wgs%d" % (PACK - 1))
+            return tile[:]
+
+        def second_pass(c, planes):
+            staged = ring.tile([P, CHUNK, PACK], BF16, name="z1_staged", align_bytes=64)
+            interleave(staged[:], planes)
+            codes, scales = quantise(staged[:], CHUNK, "z1_%d" % c)
+            multiply(c, 1, codes[:], scales[:])
+
+        planes = planes0
+        read_hero(last, 0, CHUNK, planes0[:, PACK - 1, :])
+        for c in range(1, CHUNKS + 1):
+            previous = planes
+            if c < CHUNKS:
+                planes = chunk_planes(c)
+                for t in range(PACK - 1):
+                    read_hero(PACK + t, CHUNK * c, CHUNK * (c + 1), planes[:, t, :])
+            second_pass(c - 1, previous)
+            if c < CHUNKS:
+                read_hero(last, CHUNK * c, CHUNK * (c + 1), planes[:, PACK - 1, :])
+            if c >= 2:
+                finish(c - 2)
+                if c < CHUNKS:
+                    first_pass(c)
+        finish(CHUNKS - 1)

@@ -22,7 +22,10 @@ PACK = 4
 PASS = P * PACK
 BANK = 512
 CHUNK = 256
-CHUNKS = PAIRS // CHUNK
+WIDTHS = (256, 256, 256, 128, 128)
+STARTS = (0, 256, 512, 768, 896)
+FIRST_BANK = (4, 0, 4, 0, 2)
+CHUNKS = len(WIDTHS)
 TILES = H // P
 
 
@@ -61,12 +64,12 @@ def tile_list_hero_villain_reads_kernel(
             nc.sync.dma_start(raw[:], w1[:, PASS * b : PASS * (b + 1)].rearrange("(p j) c -> p j c", j=PACK))
             return raw
 
-        def load_weight_rows(t):
-            tile = held([P, S], F32, "wgs%d" % t)
+        wg = [held([P, S], F32, "wgs%d" % t) for t in range(PACK)]
+
+        def load_weight_rows(t, start, stop):
             rows = wgs.rearrange("(q t) j -> t q j", t=PACK)[t]
-            for q in range(4):
-                nc.sync.dma_start(tile[32 * q : 32 * (q + 1), :], rows)
-            return tile
+            for q in (0, 2, 1, 3):
+                nc.sync.dma_start(wg[t][32 * q : 32 * (q + 1), start:stop], rows[:, start:stop])
 
         def load_page(u):
             b, t = divmod(u, PACK)
@@ -74,8 +77,8 @@ def tile_list_hero_villain_reads_kernel(
             nc.sync.dma_start(tile[:], page0.rearrange("(b p t) c -> b t p c", p=P, t=PACK)[b, t])
             return tile
 
-        picks = load_list(offs, "picks")
         w1_raw = [load_w1(0)]
+        picks = load_list(offs, "picks")
         for q in range(4):
             nc.sync.dma_start(
                 table_scales[32 * q : 32 * q + 4, :].bitcast(I32), tab_scales[0, 4 * q : 4 * q + 4, :].bitcast(I32)
@@ -83,14 +86,15 @@ def tile_list_hero_villain_reads_kernel(
         table_words = held([P, T], U32, "table_words")
         nc.sync.dma_start(table_words[:].bitcast(I32), tab_words[0].rearrange("p n t -> p (n t)").bitcast(I32))
         slots = load_list(offs2, "slots")
-        wg = [load_weight_rows(0)]
+        load_weight_rows(0, 0, BANK)
         pages = [load_page(0)]
+        load_weight_rows(0, BANK, S)
         villains = load_list(offs4, "villains")
         heroes = load_list(offs3, "heroes")
         rates = held([P, 2, PACK], F32, "rates")
         nc.sync.dma_start(rates[:], rate.rearrange("(b p t) -> p b t", p=P, t=PACK))
         for t in range(1, PACK):
-            wg.append(load_weight_rows(t))
+            load_weight_rows(t, 0, S)
             pages.append(load_page(t))
             if t == 1:
                 w1_raw.append(load_w1(1))
@@ -196,47 +200,48 @@ def tile_list_hero_villain_reads_kernel(
         sums = {}
 
         def multiply(c, b, z_codes, z_scales):
+            width = WIDTHS[c]
+            per_bank = BANK // width
             if b == 0:
-                first = 4 * ((c + 1) % 2)
-                sums[c] = [bank(first + i, "y_acc") for i in range(4)]
-            for half in range(2):
-                y2, y1 = sums[c][2 * half], sums[c][2 * half + 1]
-                for i in range(2):
-                    n = 2 * half + i
+                sums[c] = [bank(FIRST_BANK[c] + i, "y_acc") for i in range(2 * PACK // per_bank)]
+            for g in range(PACK // per_bank):
+                y2, y1 = sums[c][2 * g], sums[c][2 * g + 1]
+                for i in range(per_bank):
+                    n = per_bank * g + i
                     nc.tensor.matmul_mx(
-                        out=y2[:, CHUNK * i : CHUNK * (i + 1)],
+                        out=y2[:, width * i : width * (i + 1)],
                         lhsT=w3_q[b][0][:, P * n : P * (n + 1)].bitcast(FP8X4),
                         lhsT_scale=w3_q[b][1][:, P * n : P * (n + 1)],
                         rhs=z_codes.bitcast(FP8X4),
                         rhs_scale=z_scales,
                         start=(b == 0 and i == 0),
-                        stop=(b == 1 and i == 1),
+                        stop=(b == 1 and i == per_bank - 1),
                     )
-                for i in range(2):
-                    n = 2 * half + i
-                    for s in range(2):
-                        nc.tensor.matmul_mx(
-                            out=y1[:, CHUNK * i + P * s : CHUNK * i + P * (s + 1)],
-                            lhsT=w2_codes[:, b, 2 * P * n : 2 * P * (n + 1)].bitcast(FP4X4),
-                            lhsT_scale=w2_plane[:, b, P * n : P * (n + 1)],
-                            rhs=z_codes[:, P * s : P * (s + 1)].bitcast(FP8X4),
-                            rhs_scale=z_scales[:, P * s : P * (s + 1)],
-                            start=(b == 0 and i == 0 and s == 0),
-                            stop=(b == 1 and i == 1 and s == 1),
-                        )
+                for i in range(BANK // P):
+                    n, s = divmod(BANK // P * g + i, width // P)
+                    nc.tensor.matmul_mx(
+                        out=y1[:, P * i : P * (i + 1)],
+                        lhsT=w2_codes[:, b, 2 * P * n : 2 * P * (n + 1)].bitcast(FP4X4),
+                        lhsT_scale=w2_plane[:, b, P * n : P * (n + 1)],
+                        rhs=z_codes[:, P * s : P * (s + 1)].bitcast(FP8X4),
+                        rhs_scale=z_scales[:, P * s : P * (s + 1)],
+                        start=(b == 0 and i == 0),
+                        stop=(b == 1 and i == BANK // P - 1),
+                    )
 
         def finish(c):
-            for half in range(2):
-                y2, y1 = sums[c][2 * half], sums[c][2 * half + 1]
+            width = WIDTHS[c]
+            per_bank = BANK // width
+            for g in range(PACK // per_bank):
+                y2, y1 = sums[c][2 * g], sums[c][2 * g + 1]
                 squashed = ring.tile([P, BANK], F32, name="squashed")
                 nc.scalar.activation(squashed[:], y2[:], TANH)
                 result = ring.tile([P, BANK], F32, name="result", bufs=4)
                 nc.vector.tensor_tensor(result[:], y1[:], squashed[:], MULT)
+                rows = slice(P * per_bank * g, P * per_bank * (g + 1))
                 nc.sync.dma_start(
-                    out[2 * P * half : 2 * P * (half + 1), CHUNK * c : CHUNK * (c + 1)].rearrange(
-                        "(i p) m -> p i m", p=P
-                    ),
-                    result[:].rearrange("p (i m) -> p i m", i=2),
+                    out[rows, STARTS[c] : STARTS[c] + width].rearrange("(i p) m -> p i m", p=P),
+                    result[:].rearrange("p (i m) -> p i m", i=per_bank),
                 )
 
         for u in range(PACK):
@@ -257,11 +262,13 @@ def tile_list_hero_villain_reads_kernel(
                 w3_q.append(quantise_w3(u - 2, "gate%d" % (u - 1)))
         make_gate(PACK, 0, PAIRS)
         z0_staged = held([P, PAIRS, PACK], BF16, "z0_staged", "w1_raw0")
-        interleave(z0_staged[:], lanes[:, S : 5 * S].rearrange("p (t m) -> p t m", t=PACK))
+        z0 = lanes[:, S : 5 * S].rearrange("p (t m) -> p t m", t=PACK)
+        for start in range(0, PAIRS, CHUNK):
+            interleave(z0_staged[:, start : start + CHUNK, :], z0[:, :, start : start + CHUNK])
         z0_codes, z0_scales = quantise(z0_staged[:], PAIRS, "z0")
 
         def first_pass(c):
-            cols = slice(CHUNK * c, CHUNK * (c + 1))
+            cols = slice(STARTS[c], STARTS[c] + WIDTHS[c])
             multiply(c, 0, z0_codes[:, cols], z0_scales[:, cols])
 
         first_pass(0)
@@ -281,13 +288,15 @@ def tile_list_hero_villain_reads_kernel(
             if c == 2:
                 start = last * S + CHUNK
                 return lanes[:, start : start + PACK * CHUNK].rearrange("p (t m) -> p t m", t=PACK)
-            tile = held([P, PACK, CHUNK], F32, "planes%d" % c, "wgs%d" % (PACK - 1))
+            if c == 4:
+                return planes0[:, :, 0 : WIDTHS[c]]
+            tile = held([P, PACK, WIDTHS[c]], F32, "planes%d" % c, "wgs%d" % (PACK - 1))
             return tile[:]
 
         def second_pass(c, planes):
-            staged = ring.tile([P, CHUNK, PACK], BF16, name="z1_staged", align_bytes=64)
+            staged = ring.tile([P, WIDTHS[c], PACK], BF16, name="z1_staged", align_bytes=64)
             interleave(staged[:], planes)
-            codes, scales = quantise(staged[:], CHUNK, "z1_%d" % c)
+            codes, scales = quantise(staged[:], WIDTHS[c], "z1_%d" % c)
             multiply(c, 1, codes[:], scales[:])
 
         planes = planes0
@@ -297,10 +306,10 @@ def tile_list_hero_villain_reads_kernel(
             if c < CHUNKS:
                 planes = chunk_planes(c)
                 for t in range(PACK - 1):
-                    read_hero(PACK + t, CHUNK * c, CHUNK * (c + 1), planes[:, t, :])
+                    read_hero(PACK + t, STARTS[c], STARTS[c] + WIDTHS[c], planes[:, t, :])
             second_pass(c - 1, previous)
             if c < CHUNKS:
-                read_hero(last, CHUNK * c, CHUNK * (c + 1), planes[:, PACK - 1, :])
+                read_hero(last, STARTS[c], STARTS[c] + WIDTHS[c], planes[:, PACK - 1, :])
             if c >= 2:
                 finish(c - 2)
                 if c < CHUNKS:

@@ -102,19 +102,23 @@ def tile_list_hero_villain_reads_kernel(
         v_scales = held([P, S], U8, "v_scales")
         nc.vector.tensor_copy(v_scales[:], table_scales[:].indirect(picks[:]))
 
-        def quantise_w1(b, tag):
-            staged = held([P, PACK, P, PACK], BF16, "w1_staged%d" % b, tag)
+        def stage_w1(b):
+            staged = held([P, PACK, P, PACK], BF16, "w1_staged%d" % b, "staged")
             nc.scalar.copy(
                 staged[:].rearrange("p t m j -> p m t j"), w1_raw[b][:].rearrange("p j (m t) -> p m t j", t=PACK)
             )
-            codes = held([P, PASS], U32, "w1_codes%d" % b)
-            scales = held([P, PASS], U8, "w1_scales%d" % b)
+            return staged[:].rearrange("p t m j -> p (t m) j")
+
+        def quantise(staged, name, tag=None):
+            width = staged.shape[1]
+            codes = held([P, width], U32, name + "_codes", tag)
+            scales = held([P, width], U8, name + "_scales")
             nc.vector.quantize_mx(
-                out=codes[:].bitcast(FP8X4), scales=scales[:], in_=staged[:].rearrange("p t m j -> p (t m j)")
+                out=codes[:].bitcast(FP8X4), scales=scales[:], in_=staged.rearrange("p m t -> p (m t)")
             )
             return codes, scales
 
-        w1_q = [quantise_w1(0, "w1_staged0")]
+        w1_q = [quantise(stage_w1(0), "w1_0")]
         v_words = [held([P, BANK], U32, "v_words%d" % c) for c in range(2)]
         for c in range(2):
             nc.vector.tensor_copy(
@@ -183,18 +187,10 @@ def tile_list_hero_villain_reads_kernel(
                 staged.rearrange("p (c i) t -> p c t i", i=4), planes.rearrange("p t (c i) -> p c t i", i=4)
             )
 
-        def quantise(staged, width, name):
-            codes = held([P, width], U32, name + "_codes")
-            scales = held([P, width], U8, name + "_scales")
-            nc.vector.quantize_mx(
-                out=codes[:].bitcast(FP8X4), scales=scales[:], in_=staged.rearrange("p m t -> p (m t)")
-            )
-            return codes, scales
-
-        def quantise_w3(a, tag):
+        def stage_w3(a, tag):
             staged = held([P, N, PACK], BF16, "w3_staged%d" % a, tag)
             interleave(staged[:], w3_raw[:, a])
-            return quantise(staged[:], N, "w3_%d" % a)
+            return staged[:]
 
         w3_q = []
         sums = {}
@@ -234,38 +230,48 @@ def tile_list_hero_villain_reads_kernel(
             per_bank = BANK // width
             for g in range(PACK // per_bank):
                 y2, y1 = sums[c][2 * g], sums[c][2 * g + 1]
-                squashed = ring.tile([P, BANK], F32, name="squashed")
+                squashed = held([P, BANK], F32, "squashed%d_%d" % (c, g), "squashed%d" % (sum(PACK * w // BANK for w in WIDTHS[:c]) + g))
                 nc.scalar.activation(squashed[:], y2[:], TANH)
-                result = ring.tile([P, BANK], F32, name="result", bufs=4)
-                nc.vector.tensor_tensor(result[:], y1[:], squashed[:], MULT)
-                rows = slice(P * per_bank * g, P * per_bank * (g + 1))
-                nc.sync.dma_start(
-                    out[rows, STARTS[c] : STARTS[c] + width].rearrange("(i p) m -> p i m", p=P),
-                    result[:].rearrange("p (i m) -> p i m", i=per_bank),
-                )
+                for pair in range(per_bank // 2):
+                    cols = slice(2 * width * pair, 2 * width * (pair + 1))
+                    result = ring.tile([P, 2 * width], F32, name="result", bufs=4)
+                    nc.vector.tensor_tensor(result[:], y1[:, cols], squashed[:, cols], MULT)
+                    row = P * (per_bank * g + 2 * pair)
+                    nc.sync.dma_start(
+                        out[row : row + 2 * P, STARTS[c] : STARTS[c] + width].rearrange("(i p) m -> p i m", p=P),
+                        result[:].rearrange("p (i m) -> p i m", i=2),
+                    )
 
         for u in range(PACK):
             make_h(u)
         scatter(0, 0, BANK)
         scatter(0, BANK, S)
         make_gate(0, 0, PAIRS)
+        w1_staged = stage_w1(1)
         for u in range(1, PACK + 1):
             scatter(u, 0, S)
             read_hero(u - 1, 0, PAIRS, lane(u))
-            if u < PACK:
-                make_gate(u, 0, PAIRS)
-            if u == 1:
-                w1_q.append(quantise_w1(1, "gate0"))
+            make_gate(u, 0, PAIRS)
+            if u == 2:
+                w1_q.append(quantise(w1_staged, "w1_1", "gate1"))
                 for later in range(PACK, TILES):
                     make_h(later)
-            elif u < PACK:
-                w3_q.append(quantise_w3(u - 2, "gate%d" % (u - 1)))
-        make_gate(PACK, 0, PAIRS)
+                w3_staged = [stage_w3(0, "staged"), stage_w3(1, "w3_staged1")]
+        w3_q.append(quantise(w3_staged[0], "w3_0", "wgs0"))
         z0_staged = held([P, PAIRS, PACK], BF16, "z0_staged", "w1_raw0")
         z0 = lanes[:, S : 5 * S].rearrange("p (t m) -> p t m", t=PACK)
         for start in range(0, PAIRS, CHUNK):
             interleave(z0_staged[:, start : start + CHUNK, :], z0[:, :, start : start + CHUNK])
-        z0_codes, z0_scales = quantise(z0_staged[:], PAIRS, "z0")
+
+        planes0 = lanes[:, 5 * S : 9 * S].rearrange("p (t m) -> p t m", t=PACK)[:, :, 0:CHUNK]
+        last = TILES - 1
+        for u in range(PACK + 1, last):
+            scatter(u, 0, S)
+            read_hero(u - 1, 0, CHUNK, planes0[:, u - 1 - PACK, :])
+            make_gate(u, 0, PAIRS)
+            if u == PACK + 1:
+                w3_q.append(quantise(w3_staged[1], "w3_1", "wgs1"))
+        z0_codes, z0_scales = quantise(z0_staged[:], "z0", "wgs2")
 
         def first_pass(c):
             cols = slice(STARTS[c], STARTS[c] + WIDTHS[c])
@@ -273,45 +279,38 @@ def tile_list_hero_villain_reads_kernel(
 
         first_pass(0)
         first_pass(1)
-
-        planes0 = lanes[:, 5 * S : 9 * S].rearrange("p (t m) -> p t m", t=PACK)[:, :, 0:CHUNK]
-        for u in range(PACK + 1, TILES):
-            scatter(u, 0, S)
-            read_hero(u - 1, 0, CHUNK, planes0[:, u - 1 - PACK, :])
-            if u < TILES - 1:
-                make_gate(u, 0, PAIRS)
-        last = TILES - 1
+        scatter(last, 0, S)
         make_gate(last, 0, CHUNK)
+        read_hero(last - 1, 0, CHUNK, planes0[:, PACK - 2, :])
+        read_hero(last, 0, CHUNK, planes0[:, PACK - 1, :])
         make_gate(last, CHUNK, PAIRS)
 
-        def chunk_planes(c):
-            if c == 2:
-                start = last * S + CHUNK
-                return lanes[:, start : start + PACK * CHUNK].rearrange("p (t m) -> p t m", t=PACK)
-            if c == 4:
-                return planes0[:, :, 0 : WIDTHS[c]]
-            tile = held([P, PACK, WIDTHS[c]], F32, "planes%d" % c, "wgs%d" % (PACK - 1))
-            return tile[:]
+        def read_chunk(c, tag):
+            planes = held([P, PACK, WIDTHS[c]], F32, "planes%d" % c, tag)
+            for t in range(PACK):
+                read_hero(PACK + t, STARTS[c], STARTS[c] + WIDTHS[c], planes[:, t, :])
+            return planes[:]
 
         def second_pass(c, planes):
-            staged = ring.tile([P, WIDTHS[c], PACK], BF16, name="z1_staged", align_bytes=64)
+            staged = held([P, WIDTHS[c], PACK], BF16, "z1_staged%d" % c)
             interleave(staged[:], planes)
-            codes, scales = quantise(staged[:], WIDTHS[c], "z1_%d" % c)
+            codes, scales = quantise(staged[:], "z1_%d" % c)
             multiply(c, 1, codes[:], scales[:])
 
-        planes = planes0
-        read_hero(last, 0, CHUNK, planes0[:, PACK - 1, :])
-        for c in range(1, CHUNKS + 1):
-            previous = planes
-            if c < CHUNKS:
-                planes = chunk_planes(c)
-                for t in range(PACK - 1):
-                    read_hero(PACK + t, STARTS[c], STARTS[c] + WIDTHS[c], planes[:, t, :])
-            second_pass(c - 1, previous)
-            if c < CHUNKS:
-                read_hero(last, STARTS[c], STARTS[c] + WIDTHS[c], planes[:, PACK - 1, :])
-            if c >= 2:
-                finish(c - 2)
-                if c < CHUNKS:
-                    first_pass(c)
-        finish(CHUNKS - 1)
+        planes1 = read_chunk(1, "wgs3")
+        second_pass(0, planes0)
+        planes2 = read_chunk(2, "z1_staged0")
+        second_pass(1, planes1)
+        finish(0)
+        first_pass(2)
+        planes3 = read_chunk(3, "squashed1")
+        second_pass(2, planes2)
+        finish(1)
+        first_pass(3)
+        first_pass(4)
+        planes4 = read_chunk(4, "squashed2")
+        second_pass(3, planes3)
+        second_pass(4, planes4)
+        finish(2)
+        finish(3)
+        finish(4)

@@ -40,7 +40,6 @@ def tile_list_hero_villain_reads_kernel(
     with ExitStack() as ctx:
         lists = ctx.enter_context(tc.tile_pool(name="lists", bufs=1))
         keep = ctx.enter_context(tc.tile_pool(name="keep", bufs=1))
-        ring = ctx.enter_context(tc.tile_pool(name="ring", bufs=2))
         psum = ctx.enter_context(tc.psum_pool(name="psum", bufs=1))
 
         def held(shape, dtype, name, tag=None):
@@ -51,6 +50,8 @@ def tile_list_hero_villain_reads_kernel(
 
         table_scales = held([P, T], U8, "table_scales")
         nc.vector.memset(table_scales[:].bitcast(I32), 0)
+        v_scales = held([P, S], U8, "v_scales")
+        nc.vector.memset(v_scales[:].bitcast(I32), 0)
         w2_plane = held([P, 2, N], U8, "w2_plane")
         nc.vector.memset(w2_plane[:].rearrange("p a c -> p (a c)").bitcast(I32), 0)
 
@@ -79,15 +80,12 @@ def tile_list_hero_villain_reads_kernel(
 
         w1_raw = [load_w1(0)]
         picks = load_list(offs, "picks")
-        for q in range(4):
-            nc.sync.dma_start(
-                table_scales[32 * q : 32 * q + 4, :].bitcast(I32), tab_scales[0, 4 * q : 4 * q + 4, :].bitcast(I32)
-            )
+        nc.sync.dma_start(table_scales[0:P:8, :].bitcast(I32), tab_scales[0].bitcast(I32))
         table_words = held([P, T], U32, "table_words")
         nc.sync.dma_start(table_words[:].bitcast(I32), tab_words[0].rearrange("p n t -> p (n t)").bitcast(I32))
+        pages = [load_page(0)]
         slots = load_list(offs2, "slots")
         load_weight_rows(0, 0, BANK)
-        pages = [load_page(0)]
         load_weight_rows(0, BANK, S)
         villains = load_list(offs4, "villains")
         heroes = load_list(offs3, "heroes")
@@ -99,8 +97,8 @@ def tile_list_hero_villain_reads_kernel(
             if t == 1:
                 w1_raw.append(load_w1(1))
 
-        v_scales = held([P, S], U8, "v_scales")
-        nc.vector.tensor_copy(v_scales[:], table_scales[:].indirect(picks[:]))
+        picked_scales = held([P, S], U8, "picked_scales")
+        nc.vector.tensor_copy(picked_scales[:], table_scales[:].indirect(picks[:]))
 
         def stage_w1(b):
             staged = held([P, PACK, P, PACK], BF16, "w1_staged%d" % b, "staged")
@@ -119,6 +117,8 @@ def tile_list_hero_villain_reads_kernel(
             return codes, scales
 
         w1_q = [quantise(stage_w1(0), "w1_0")]
+        for r in range(4):
+            nc.scalar.dma_start(v_scales[r:P:32, :].bitcast(I32), picked_scales[8 * r : P : 32, :].bitcast(I32))
         v_words = [held([P, BANK], U32, "v_words%d" % c) for c in range(2)]
         for c in range(2):
             nc.vector.tensor_copy(
@@ -234,12 +234,14 @@ def tile_list_hero_villain_reads_kernel(
                 nc.scalar.activation(squashed[:], y2[:], TANH)
                 for pair in range(per_bank // 2):
                     cols = slice(2 * width * pair, 2 * width * (pair + 1))
-                    result = ring.tile([P, 2 * width], F32, name="result", bufs=4)
-                    nc.vector.tensor_tensor(result[:], y1[:, cols], squashed[:, cols], MULT)
-                    row = P * (per_bank * g + 2 * pair)
+                    n = per_bank * g + 2 * pair
+                    place = PACK * STARTS[c] + width * n
+                    result = results[:, place : place + 2 * width]
+                    nc.vector.tensor_tensor(result, y1[:, cols], squashed[:, cols], MULT)
+                    row = P * n
                     nc.sync.dma_start(
                         out[row : row + 2 * P, STARTS[c] : STARTS[c] + width].rearrange("(i p) m -> p i m", p=P),
-                        result[:].rearrange("p (i m) -> p i m", i=2),
+                        result.rearrange("p (i m) -> p i m", i=2),
                     )
 
         for u in range(PACK):
@@ -297,6 +299,7 @@ def tile_list_hero_villain_reads_kernel(
             codes, scales = quantise(staged[:], "z1_%d" % c)
             multiply(c, 1, codes[:], scales[:])
 
+        results = held([P, PACK * PAIRS], F32, "results", "table_words")
         planes1 = read_chunk(1, "wgs3")
         second_pass(0, planes0)
         planes2 = read_chunk(2, "z1_staged0")

@@ -81,12 +81,12 @@ def tile_list_hero_villain_reads_kernel(
         w1_raw = [load_w1(0)]
         picks = load_list(offs, "picks")
         nc.sync.dma_start(table_scales[0:P:8, :].bitcast(I32), tab_scales[0].bitcast(I32))
+        load_weight_rows(0, 0, CHUNK)
         table_words = held([P, T], U32, "table_words")
         nc.sync.dma_start(table_words[:].bitcast(I32), tab_words[0].rearrange("p n t -> p (n t)").bitcast(I32))
         pages = [load_page(0)]
         slots = load_list(offs2, "slots")
-        load_weight_rows(0, 0, BANK)
-        load_weight_rows(0, BANK, S)
+        load_weight_rows(0, CHUNK, S)
         villains = load_list(offs4, "villains")
         heroes = load_list(offs3, "heroes")
         rates = held([P, 2, PACK], F32, "rates")
@@ -157,7 +157,11 @@ def tile_list_hero_villain_reads_kernel(
                     start=True,
                     stop=True,
                 )
-                nc.scalar.copy(lane(u)[:, BANK * c : BANK * (c + 1)], acc[:])
+                piece = CHUNK if (u, c) == (0, 0) else BANK
+                for start in range(0, BANK, piece):
+                    nc.scalar.copy(
+                        lane(u)[:, BANK * c + start : BANK * c + start + piece], acc[:, start : start + piece]
+                    )
 
         def scatter(u, start, stop):
             nc.vector.tensor_tensor(
@@ -246,8 +250,8 @@ def tile_list_hero_villain_reads_kernel(
 
         for u in range(PACK):
             make_h(u)
-        scatter(0, 0, BANK)
-        scatter(0, BANK, S)
+        scatter(0, 0, CHUNK)
+        scatter(0, CHUNK, S)
         make_gate(0, 0, PAIRS)
         w1_staged = stage_w1(1)
         for u in range(1, PACK + 1):

@@ -50,8 +50,9 @@ def tile_list_hero_villain_reads_kernel(
 
         table_scales = held([P, T], U8, "table_scales")
         nc.vector.memset(table_scales[:].bitcast(I32), 0)
-        v_scales = held([P, S], U8, "v_scales")
-        nc.vector.memset(v_scales[:].bitcast(I32), 0)
+        v_scales = [held([P, BANK], U8, "v_scales%d" % c) for c in range(2)]
+        for c in range(2):
+            nc.vector.memset(v_scales[c][:].bitcast(I32), 0)
         w2_plane = held([P, 2, N], U8, "w2_plane")
         nc.vector.memset(w2_plane[:].rearrange("p a c -> p (a c)").bitcast(I32), 0)
 
@@ -60,52 +61,31 @@ def tile_list_hero_villain_reads_kernel(
             nc.sync.dma_start(tile[:], src)
             return tile
 
-        def load_w1(b):
-            raw = held([P, PACK, PASS], F32, "w1_raw%d" % b)
-            nc.sync.dma_start(raw[:], w1[:, PASS * b : PASS * (b + 1)].rearrange("(p j) c -> p j c", j=PACK))
+        def load_w1(start, stop):
+            raw = held([P, PACK, stop - start], F32, "w1_raw%d" % start)
+            nc.sync.dma_start(raw[:], w1[:, start:stop].rearrange("(p j) c -> p j c", j=PACK))
             return raw
 
-        wg = [held([P, S], F32, "wgs%d" % t) for t in range(PACK)]
-
-        def load_weight_rows(t, start, stop):
+        def load_dealt_weights(t):
+            tile = held([P, S], F32, "wgs_dealt%d" % t)
             rows = wgs.rearrange("(q t) j -> t q j", t=PACK)[t]
             for q in (0, 2, 1, 3):
-                nc.sync.dma_start(wg[t][32 * q : 32 * (q + 1), start:stop], rows[:, start:stop])
-
-        def load_page(u):
-            b, t = divmod(u, PACK)
-            tile = held([P, T2], F32, "page%d" % u)
-            nc.sync.dma_start(tile[:], page0.rearrange("(b p t) c -> b t p c", p=P, t=PACK)[b, t])
+                nc.sync.dma_start(tile[32 * q : 32 * (q + 1), :], rows)
             return tile
 
-        w1_raw = [load_w1(0)]
-        picks = load_list(offs, "picks")
-        nc.sync.dma_start(table_scales[0:P:8, :].bitcast(I32), tab_scales[0].bitcast(I32))
-        load_weight_rows(0, 0, CHUNK)
-        table_words = held([P, T], U32, "table_words")
-        nc.sync.dma_start(table_words[:].bitcast(I32), tab_words[0].rearrange("p n t -> p (n t)").bitcast(I32))
-        pages = [load_page(0)]
-        slots = load_list(offs2, "slots")
-        load_weight_rows(0, CHUNK, S)
-        villains = load_list(offs4, "villains")
-        heroes = load_list(offs3, "heroes")
-        rates = held([P, 2, PACK], F32, "rates")
-        nc.sync.dma_start(rates[:], rate.rearrange("(b p t) -> p b t", p=P, t=PACK))
-        for t in range(1, PACK):
-            load_weight_rows(t, 0, S)
-            pages.append(load_page(t))
-            if t == 1:
-                w1_raw.append(load_w1(1))
+        def load_page(u):
+            tile = held([P, T2], F32, "page%d" % u)
+            if u < PACK:
+                rows = page0[P * u : P * (u + 1), :]
+            else:
+                rows = page0[PASS:, :].rearrange("(p t) c -> t p c", t=PACK)[u - PACK]
+            nc.sync.dma_start(tile[:], rows)
+            return tile
 
-        picked_scales = held([P, S], U8, "picked_scales")
-        nc.vector.tensor_copy(picked_scales[:], table_scales[:].indirect(picks[:]))
-
-        def stage_w1(b):
-            staged = held([P, PACK, P, PACK], BF16, "w1_staged%d" % b, "staged")
+        def interleave(staged, planes):
             nc.scalar.copy(
-                staged[:].rearrange("p t m j -> p m t j"), w1_raw[b][:].rearrange("p j (m t) -> p m t j", t=PACK)
+                staged.rearrange("p (c i) t -> p c t i", i=4), planes.rearrange("p t (c i) -> p c t i", i=4)
             )
-            return staged[:].rearrange("p t m j -> p (t m) j")
 
         def quantise(staged, name, tag=None):
             width = staged.shape[1]
@@ -116,20 +96,108 @@ def tile_list_hero_villain_reads_kernel(
             )
             return codes, scales
 
-        w1_q = [quantise(stage_w1(0), "w1_0")]
-        for r in range(4):
-            nc.scalar.dma_start(v_scales[r:P:32, :].bitcast(I32), picked_scales[8 * r : P : 32, :].bitcast(I32))
+        w1_q = {}
+
+        def prepare_w1(raw, start, stop):
+            staged = held([P, stop - start, PACK], BF16, "w1_staged%d" % start)
+            if start < PASS:
+                interleave(staged[:], raw[:])
+            else:
+                nc.scalar.copy(
+                    staged[:].rearrange("p (t m) j -> p m t j", t=PACK),
+                    raw[:].rearrange("p j (m t) -> p m t j", t=PACK),
+                )
+            codes, scales = quantise(staged[:], "w1_%d" % start)
+            for u in range(start // P, stop // P):
+                cols = slice(P * u - start, P * (u + 1) - start)
+                w1_q[u] = (codes[:, cols], scales[:, cols])
+
+        def pick_scales(c):
+            picked = held([P, BANK], U8, "picked_scales%d" % c)
+            nc.vector.tensor_copy(picked[:], table_scales[:].indirect(list_slice(picks, BANK * c, BANK * (c + 1))))
+            return picked
+
+        def move_scales(c, picked):
+            for r in range(4):
+                nc.sync.dma_start(v_scales[c][r:P:32, :].bitcast(I32), picked[8 * r : P : 32, :].bitcast(I32))
+
+        raw_first = load_w1(0, P)
+        picks = load_list(offs, "picks")
+        slots = load_list(offs2, "slots")
+        plain_weights = held([P, S], F32, "wgs_plain")
+        nc.sync.dma_start(plain_weights[:, 0:BANK], wgs[:, 0:BANK])
+        nc.sync.dma_start(table_scales[0:P:8, :].bitcast(I32), tab_scales[0].bitcast(I32))
+        table_words = held([P, T], U32, "table_words")
+        nc.sync.dma_start(table_words[:].bitcast(I32), tab_words[0].rearrange("p n t -> p (n t)").bitcast(I32))
+        picked = [pick_scales(0)]
+        move_scales(0, picked[0])
+        prepare_w1(raw_first, 0, P)
+        picked.append(pick_scales(1))
+        pages = [load_page(0)]
+        move_scales(1, picked[1])
+        raw_next = load_w1(P, 2 * P)
+        raw_pair = load_w1(2 * P, PASS)
+        nc.sync.dma_start(plain_weights[:, BANK:S], wgs[:, BANK:S])
         v_words = [held([P, BANK], U32, "v_words%d" % c) for c in range(2)]
         for c in range(2):
             nc.vector.tensor_copy(
                 v_words[c][:], table_words[:].indirect(list_slice(picks, BANK * c, BANK * (c + 1)))
             )
 
+        lanes = {}
+
+        def make_h(u, tag):
+            codes, scales = w1_q[u]
+            lanes[u] = held([P, S], F32, "lane%d" % u, tag)
+            pieces = ((0, CHUNK), (CHUNK, BANK), (BANK, S)) if u == 0 else ((0, BANK), (BANK, S))
+            for start, stop in pieces:
+                c, at = divmod(start, BANK)
+                acc = bank(h_count[0] % 4, "h_acc")
+                h_count[0] = h_count[0] + 1
+                nc.tensor.matmul_mx(
+                    out=acc[:, 0 : stop - start],
+                    lhsT=codes.bitcast(FP8X4),
+                    lhsT_scale=scales,
+                    rhs=v_words[c][:, at : at + stop - start].bitcast(FP8X4),
+                    rhs_scale=v_scales[c][:, at : at + stop - start],
+                    start=True,
+                    stop=True,
+                )
+                nc.scalar.copy(lanes[u][:, start:stop], acc[:, 0 : stop - start])
+
+        h_count = [0]
+
+        def scatter(u, start, stop, weights):
+            nc.vector.tensor_tensor(
+                pages[u][:].indirect(list_slice(slots, start, stop)),
+                lanes[u][:, start:stop],
+                weights[:, start:stop],
+                MULT,
+            )
+
+        make_h(0, "lane0")
+        scatter(0, 0, BANK, plain_weights)
+        prepare_w1(raw_next, P, 2 * P)
+        scatter(0, BANK, S, plain_weights)
+        prepare_w1(raw_pair, 2 * P, PASS)
+        pages.append(load_page(1))
+        raw_second = load_w1(PASS, H)
+        prepare_w1(raw_second, PASS, H)
+        for u in range(2, PACK):
+            pages.append(load_page(u))
         w3_raw = held([P, 2, PACK, N], F32, "w3_raw", "table_words")
         for a in range(2):
             nc.sync.dma_start(w3_raw[:, a], w3[PASS * a : PASS * (a + 1), :].rearrange("(p j) n -> p j n", j=PACK))
-        for u in range(PACK, TILES):
-            pages.append(load_page(u))
+        dealt = [load_dealt_weights(0)]
+        pages.append(load_page(PACK))
+        villains = load_list(offs4, "villains")
+        rates = [held([P, PACK], F32, "rates%d" % b) for b in range(2)]
+        with nc.allow_non_contiguous_dma(reason="one rate a partition"):
+            nc.sync.dma_start(rates[0][:], rate[0:PASS].rearrange("(u p) -> p u", p=P))
+        nc.sync.dma_start(rates[1][:], rate[PASS:H].rearrange("(p t) -> p t", t=PACK))
+        for t in range(1, PACK):
+            dealt.append(load_dealt_weights(t))
+            pages.append(load_page(PACK + t))
         w2_codes = held([P, 2, 2 * N], U8, "w2_codes")
         nc.sync.dma_start(w2_codes[:].bitcast(I32), w2_words.rearrange("a p c -> p a c").bitcast(I32))
         for q in range(4):
@@ -137,66 +205,46 @@ def tile_list_hero_villain_reads_kernel(
                 w2_plane[32 * q : 32 * q + 4, :, :].bitcast(I32),
                 w2_scales[:, 4 * q : 4 * q + 4, :].rearrange("a r c -> r a c").bitcast(I32),
             )
+        heroes = load_list(offs3, "heroes")
 
-        lanes = held([P, (TILES + 1) * S], F32, "lanes")
+        for u in range(1, PACK):
+            make_h(u, "lane%d" % (u % 3))
+            scatter(u, 0, S, plain_weights)
+        make_h(PACK, "lane%d" % (PACK % 3))
+        scatter(PACK, 0, S, dealt[0])
 
-        def lane(i):
-            return lanes[:, S * i : S * (i + 1)]
-
-        def make_h(u):
+        def make_gate(u, gate):
             b, t = divmod(u, PACK)
-            codes, scales = w1_q[b]
-            for c in range(2):
-                acc = bank((2 * u + c) % 4, "h_acc")
-                nc.tensor.matmul_mx(
-                    out=acc[:],
-                    lhsT=codes[:, P * t : P * (t + 1)].bitcast(FP8X4),
-                    lhsT_scale=scales[:, P * t : P * (t + 1)],
-                    rhs=v_words[c][:].bitcast(FP8X4),
-                    rhs_scale=v_scales[:, BANK * c : BANK * (c + 1)],
-                    start=True,
-                    stop=True,
-                )
-                piece = CHUNK if (u, c) == (0, 0) else BANK
-                for start in range(0, BANK, piece):
-                    nc.scalar.copy(
-                        lane(u)[:, BANK * c + start : BANK * c + start + piece], acc[:, start : start + piece]
-                    )
+            nc.vector.tensor_copy(gate, pages[u][:].indirect(villains[:]))
+            nc.scalar.activation(gate, gate, SIGMOID, scale=rates[b][:, t : t + 1])
 
-        def scatter(u, start, stop):
+        def read_hero(u, start, stop, gate, z):
             nc.vector.tensor_tensor(
-                pages[u][:].indirect(list_slice(slots, start, stop)),
-                lane(u)[:, start:stop],
-                wg[u % PACK][:, start:stop],
-                MULT,
+                z, pages[u][:].indirect(list_slice(heroes, start, stop)), gate[:, start:stop], MULT
             )
 
-        gates = {}
-
-        def make_gate(u, start, stop):
-            b, t = divmod(u, PACK)
-            if start == 0:
-                gates[u] = held([P, PAIRS], F32, "gate%d" % u, "gate%d" % t)
-            gate = gates[u][:, start:stop]
-            nc.vector.tensor_copy(gate, pages[u][:].indirect(list_slice(villains, start, stop)))
-            nc.scalar.activation(gate, gate, SIGMOID, scale=rates[:, b, t : t + 1])
-
-        def read_hero(u, start, stop, z):
-            nc.vector.tensor_tensor(
-                z, pages[u][:].indirect(list_slice(heroes, start, stop)), gates[u][:, start:stop], MULT
-            )
-
-        def interleave(staged, planes):
-            nc.scalar.copy(
-                staged.rearrange("p (c i) t -> p c t i", i=4), planes.rearrange("p t (c i) -> p c t i", i=4)
-            )
-
-        def stage_w3(a, tag):
-            staged = held([P, N, PACK], BF16, "w3_staged%d" % a, tag)
-            interleave(staged[:], w3_raw[:, a])
-            return staged[:]
-
+        gates = [held([P, PAIRS], F32, "gate%d" % u) for u in range(PACK)]
+        for u in range(PACK):
+            make_gate(u, gates[u][:])
+        z0_rows = held([P, PACK, PAIRS], F32, "z0_rows")
+        z0_planes = held([P, PACK, PAIRS], F32, "z0_planes")
+        for u in range(PACK):
+            read_hero(u, 0, PAIRS, gates[u][:], z0_rows[:, u, :])
+            for t in range(PACK):
+                nc.sync.dma_start(z0_planes[32 * u : 32 * (u + 1), t, :], z0_rows[t:P:PACK, u, :])
+        for u in range(PACK + 1, TILES):
+            make_h(u, "gate%d" % (u - PACK - 1))
+            scatter(u, 0, S, dealt[u - PACK])
+        w3_staged = held([P, 2, N, PACK], BF16, "w3_staged", "w1_raw%d" % PASS)
         w3_q = []
+        for a in range(2):
+            interleave(w3_staged[:, a], w3_raw[:, a])
+            w3_q.append(quantise(w3_staged[:, a], "w3_%d" % a))
+        z0_staged = held([P, PAIRS, PACK], BF16, "z0_staged")
+        for start in range(0, PAIRS, CHUNK):
+            interleave(z0_staged[:, start : start + CHUNK, :], z0_planes[:, :, start : start + CHUNK])
+        z0_codes, z0_scales = quantise(z0_staged[:], "z0")
+
         sums = {}
 
         def multiply(c, b, z_codes, z_scales):
@@ -234,7 +282,7 @@ def tile_list_hero_villain_reads_kernel(
             per_bank = BANK // width
             for g in range(PACK // per_bank):
                 y2, y1 = sums[c][2 * g], sums[c][2 * g + 1]
-                squashed = held([P, BANK], F32, "squashed%d_%d" % (c, g), "squashed%d" % (sum(PACK * w // BANK for w in WIDTHS[:c]) + g))
+                squashed = held([P, BANK], F32, "squashed%d_%d" % (c, g), squash_tags[PACK * STARTS[c] // BANK + g])
                 nc.scalar.activation(squashed[:], y2[:], TANH)
                 for pair in range(per_bank // 2):
                     cols = slice(2 * width * pair, 2 * width * (pair + 1))
@@ -248,74 +296,45 @@ def tile_list_hero_villain_reads_kernel(
                         result.rearrange("p (i m) -> p i m", i=2),
                     )
 
-        for u in range(PACK):
-            make_h(u)
-        scatter(0, 0, CHUNK)
-        scatter(0, CHUNK, S)
-        make_gate(0, 0, PAIRS)
-        w1_staged = stage_w1(1)
-        for u in range(1, PACK + 1):
-            scatter(u, 0, S)
-            read_hero(u - 1, 0, PAIRS, lane(u))
-            make_gate(u, 0, PAIRS)
-            if u == 2:
-                w1_q.append(quantise(w1_staged, "w1_1", "gate1"))
-                for later in range(PACK, TILES):
-                    make_h(later)
-                w3_staged = [stage_w3(0, "staged"), stage_w3(1, "w3_staged1")]
-        w3_q.append(quantise(w3_staged[0], "w3_0", "wgs0"))
-        z0_staged = held([P, PAIRS, PACK], BF16, "z0_staged", "w1_raw0")
-        z0 = lanes[:, S : 5 * S].rearrange("p (t m) -> p t m", t=PACK)
-        for start in range(0, PAIRS, CHUNK):
-            interleave(z0_staged[:, start : start + CHUNK, :], z0[:, :, start : start + CHUNK])
-
-        planes0 = lanes[:, 5 * S : 9 * S].rearrange("p (t m) -> p t m", t=PACK)[:, :, 0:CHUNK]
-        last = TILES - 1
-        for u in range(PACK + 1, last):
-            scatter(u, 0, S)
-            read_hero(u - 1, 0, CHUNK, planes0[:, u - 1 - PACK, :])
-            make_gate(u, 0, PAIRS)
-            if u == PACK + 1:
-                w3_q.append(quantise(w3_staged[1], "w3_1", "wgs1"))
-        z0_codes, z0_scales = quantise(z0_staged[:], "z0", "wgs2")
-
         def first_pass(c):
             cols = slice(STARTS[c], STARTS[c] + WIDTHS[c])
             multiply(c, 0, z0_codes[:, cols], z0_scales[:, cols])
 
+        late_gates = held([P, PACK, PAIRS], F32, "late_gates", "z0_planes")
+        for t in range(PACK):
+            make_gate(PACK + t, late_gates[:, t, :])
         first_pass(0)
         first_pass(1)
-        scatter(last, 0, S)
-        make_gate(last, 0, CHUNK)
-        read_hero(last - 1, 0, CHUNK, planes0[:, PACK - 2, :])
-        read_hero(last, 0, CHUNK, planes0[:, PACK - 1, :])
-        make_gate(last, CHUNK, PAIRS)
 
         def read_chunk(c, tag):
             planes = held([P, PACK, WIDTHS[c]], F32, "planes%d" % c, tag)
             for t in range(PACK):
-                read_hero(PACK + t, STARTS[c], STARTS[c] + WIDTHS[c], planes[:, t, :])
+                read_hero(PACK + t, STARTS[c], STARTS[c] + WIDTHS[c], late_gates[:, t, :], planes[:, t, :])
             return planes[:]
 
+        staging_tags = ("w1_raw0", "w1_raw128", "w1_raw256", "w1_staged0", "w1_staged128")
+
         def second_pass(c, planes):
-            staged = held([P, WIDTHS[c], PACK], BF16, "z1_staged%d" % c)
+            staged = held([P, WIDTHS[c], PACK], BF16, "z1_staged%d" % c, staging_tags[c])
             interleave(staged[:], planes)
             codes, scales = quantise(staged[:], "z1_%d" % c)
             multiply(c, 1, codes[:], scales[:])
 
         results = held([P, PACK * PAIRS], F32, "results", "table_words")
-        planes1 = read_chunk(1, "wgs3")
+        squash_tags = ["wgs_dealt%d" % t for t in range(PACK)] + ["gate%d" % t for t in range(PACK)]
+        planes0 = read_chunk(0, "lane0")
+        planes1 = read_chunk(1, "lane1")
         second_pass(0, planes0)
-        planes2 = read_chunk(2, "z1_staged0")
+        planes2 = read_chunk(2, staging_tags[0])
         second_pass(1, planes1)
         finish(0)
         first_pass(2)
-        planes3 = read_chunk(3, "squashed1")
+        planes3 = read_chunk(3, squash_tags[1])
         second_pass(2, planes2)
         finish(1)
         first_pass(3)
         first_pass(4)
-        planes4 = read_chunk(4, "squashed2")
+        planes4 = read_chunk(4, squash_tags[2])
         second_pass(3, planes3)
         second_pass(4, planes4)
         finish(2)

@@ -22,6 +22,7 @@ PACK = 4
 PASS = P * PACK
 BANK = 512
 CHUNK = 256
+LEAD = 1024
 WIDTHS = (256, 256, 256, 128, 128)
 STARTS = (0, 256, 512, 768, 896)
 FIRST_BANK = (4, 0, 4, 0, 2)
@@ -124,11 +125,13 @@ def tile_list_hero_villain_reads_kernel(
         raw_first = load_w1(0, P)
         picks = load_list(offs, "picks")
         slots = load_list(offs2, "slots")
+        table_words = held([P, T], U32, "table_words")
+        words = tab_words[0].rearrange("p n t -> p (n t)").bitcast(I32)
+        nc.sync.dma_start(table_words[:, 0:LEAD].bitcast(I32), words[:, 0:LEAD])
+        nc.sync.dma_start(table_scales[0:P:8, :].bitcast(I32), tab_scales[0].bitcast(I32))
+        nc.sync.dma_start(table_words[:, LEAD:T].bitcast(I32), words[:, LEAD:T])
         plain_weights = held([P, S], F32, "wgs_plain")
         nc.sync.dma_start(plain_weights[:, 0:BANK], wgs[:, 0:BANK])
-        nc.sync.dma_start(table_scales[0:P:8, :].bitcast(I32), tab_scales[0].bitcast(I32))
-        table_words = held([P, T], U32, "table_words")
-        nc.sync.dma_start(table_words[:].bitcast(I32), tab_words[0].rearrange("p n t -> p (n t)").bitcast(I32))
         picked = [pick_scales(0)]
         move_scales(0, picked[0])
         prepare_w1(raw_first, 0, P)
@@ -325,7 +328,7 @@ def tile_list_hero_villain_reads_kernel(
         planes0 = read_chunk(0, "lane0")
         planes1 = read_chunk(1, "lane1")
         second_pass(0, planes0)
-        planes2 = read_chunk(2, staging_tags[0])
+        planes2 = read_chunk(2, "lane0")
         second_pass(1, planes1)
         finish(0)
         first_pass(2)

@@ -20,14 +20,17 @@ TANH = mybir.ActivationFunctionType.Tanh
 P = 128
 PACK = 4
 PASS = P * PACK
+TILES = H // P
 BANK = 512
-CHUNK = 256
-LEAD = 1024
+HALF = S // 2
+QUARTER = S // 4
+LEAD = T // 4
+H_BANKS = 4
+H_BUFFERS = 3
 WIDTHS = (256, 256, 256, 128, 128)
 STARTS = (0, 256, 512, 768, 896)
-FIRST_BANK = (4, 0, 4, 0, 2)
 CHUNKS = len(WIDTHS)
-TILES = H // P
+BANKS = ((4, 5, 6, 7), (0, 1, 2, 3), (4, 5, 6, 7), (0, 2), (1, 3))
 
 
 def list_slice(offsets, start, stop):
@@ -51,11 +54,11 @@ def tile_list_hero_villain_reads_kernel(
 
         table_scales = held([P, T], U8, "table_scales")
         nc.vector.memset(table_scales[:].bitcast(I32), 0)
-        v_scales = [held([P, BANK], U8, "v_scales%d" % c) for c in range(2)]
+        v_scales = [held([P, HALF], U8, "v_scales%d" % c) for c in range(2)]
         for c in range(2):
             nc.vector.memset(v_scales[c][:].bitcast(I32), 0)
-        w2_plane = held([P, 2, N], U8, "w2_plane")
-        nc.vector.memset(w2_plane[:].rearrange("p a c -> p (a c)").bitcast(I32), 0)
+        w2_scale_rows = held([P, 2, N], U8, "w2_scale_rows")
+        nc.vector.memset(w2_scale_rows[:].rearrange("p a c -> p (a c)").bitcast(I32), 0)
 
         def load_list(src, name):
             tile = lists.tile([P, S // 16], U16, name=name)
@@ -83,14 +86,12 @@ def tile_list_hero_villain_reads_kernel(
             nc.sync.dma_start(tile[:], rows)
             return tile
 
-        def interleave(staged, planes):
-            nc.scalar.copy(
-                staged.rearrange("p (c i) t -> p c t i", i=4), planes.rearrange("p t (c i) -> p c t i", i=4)
-            )
+        def interleave(staged, rows):
+            nc.scalar.copy(staged.rearrange("p (c i) t -> p c t i", i=4), rows.rearrange("p t (c i) -> p c t i", i=4))
 
-        def quantise(staged, name, tag=None):
+        def quantise(staged, name):
             width = staged.shape[1]
-            codes = held([P, width], U32, name + "_codes", tag)
+            codes = held([P, width], U32, name + "_codes")
             scales = held([P, width], U8, name + "_scales")
             nc.vector.quantize_mx(
                 out=codes[:].bitcast(FP8X4), scales=scales[:], in_=staged.rearrange("p m t -> p (m t)")
@@ -114,15 +115,15 @@ def tile_list_hero_villain_reads_kernel(
                 w1_q[u] = (codes[:, cols], scales[:, cols])
 
         def pick_scales(c):
-            picked = held([P, BANK], U8, "picked_scales%d" % c)
-            nc.vector.tensor_copy(picked[:], table_scales[:].indirect(list_slice(picks, BANK * c, BANK * (c + 1))))
+            picked = held([P, HALF], U8, "picked_scales%d" % c)
+            nc.vector.tensor_copy(picked[:], table_scales[:].indirect(list_slice(picks, HALF * c, HALF * (c + 1))))
             return picked
 
         def move_scales(c, picked):
             for r in range(4):
                 nc.sync.dma_start(v_scales[c][r:P:32, :].bitcast(I32), picked[8 * r : P : 32, :].bitcast(I32))
 
-        raw_first = load_w1(0, P)
+        w1_tile0 = load_w1(0, P)
         picks = load_list(offs, "picks")
         slots = load_list(offs2, "slots")
         table_words = held([P, T], U32, "table_words")
@@ -131,32 +132,31 @@ def tile_list_hero_villain_reads_kernel(
         nc.sync.dma_start(table_scales[0:P:8, :].bitcast(I32), tab_scales[0].bitcast(I32))
         nc.sync.dma_start(table_words[:, LEAD:T].bitcast(I32), words[:, LEAD:T])
         plain_weights = held([P, S], F32, "wgs_plain")
-        nc.sync.dma_start(plain_weights[:, 0:BANK], wgs[:, 0:BANK])
+        nc.sync.dma_start(plain_weights[:, 0:HALF], wgs[:, 0:HALF])
         picked = [pick_scales(0)]
         move_scales(0, picked[0])
-        prepare_w1(raw_first, 0, P)
+        prepare_w1(w1_tile0, 0, P)
         picked.append(pick_scales(1))
         pages = [load_page(0)]
         move_scales(1, picked[1])
-        raw_next = load_w1(P, 2 * P)
-        raw_pair = load_w1(2 * P, PASS)
-        nc.sync.dma_start(plain_weights[:, BANK:S], wgs[:, BANK:S])
-        v_words = [held([P, BANK], U32, "v_words%d" % c) for c in range(2)]
+        w1_tile1 = load_w1(P, 2 * P)
+        w1_tiles23 = load_w1(2 * P, PASS)
+        nc.sync.dma_start(plain_weights[:, HALF:S], wgs[:, HALF:S])
+        v_words = [held([P, HALF], U32, "v_words%d" % c) for c in range(2)]
         for c in range(2):
-            nc.vector.tensor_copy(
-                v_words[c][:], table_words[:].indirect(list_slice(picks, BANK * c, BANK * (c + 1)))
-            )
+            nc.vector.tensor_copy(v_words[c][:], table_words[:].indirect(list_slice(picks, HALF * c, HALF * (c + 1))))
 
-        lanes = {}
+        h_rows = {}
+        h_products = []
 
         def make_h(u, tag):
             codes, scales = w1_q[u]
-            lanes[u] = held([P, S], F32, "lane%d" % u, tag)
-            pieces = ((0, CHUNK), (CHUNK, BANK), (BANK, S)) if u == 0 else ((0, BANK), (BANK, S))
+            h_rows[u] = held([P, S], F32, "h%d" % u, tag)
+            pieces = ((0, QUARTER), (QUARTER, HALF), (HALF, S)) if u == 0 else ((0, HALF), (HALF, S))
             for start, stop in pieces:
-                c, at = divmod(start, BANK)
-                acc = bank(h_count[0] % 4, "h_acc")
-                h_count[0] = h_count[0] + 1
+                c, at = divmod(start, HALF)
+                acc = bank(len(h_products) % H_BANKS, "h_acc")
+                h_products.append(acc)
                 nc.tensor.matmul_mx(
                     out=acc[:, 0 : stop - start],
                     lhsT=codes.bitcast(FP8X4),
@@ -166,136 +166,135 @@ def tile_list_hero_villain_reads_kernel(
                     start=True,
                     stop=True,
                 )
-                nc.scalar.copy(lanes[u][:, start:stop], acc[:, 0 : stop - start])
-
-        h_count = [0]
+                nc.scalar.copy(h_rows[u][:, start:stop], acc[:, 0 : stop - start])
 
         def scatter(u, start, stop, weights):
             nc.vector.tensor_tensor(
                 pages[u][:].indirect(list_slice(slots, start, stop)),
-                lanes[u][:, start:stop],
+                h_rows[u][:, start:stop],
                 weights[:, start:stop],
                 MULT,
             )
 
-        make_h(0, "lane0")
-        scatter(0, 0, BANK, plain_weights)
-        prepare_w1(raw_next, P, 2 * P)
-        scatter(0, BANK, S, plain_weights)
-        prepare_w1(raw_pair, 2 * P, PASS)
+        make_h(0, "h_buffer0")
+        scatter(0, 0, HALF, plain_weights)
+        prepare_w1(w1_tile1, P, 2 * P)
+        scatter(0, HALF, S, plain_weights)
+        prepare_w1(w1_tiles23, 2 * P, PASS)
+
         pages.append(load_page(1))
-        raw_second = load_w1(PASS, H)
-        prepare_w1(raw_second, PASS, H)
+        prepare_w1(load_w1(PASS, H), PASS, H)
         for u in range(2, PACK):
             pages.append(load_page(u))
         w3_raw = held([P, 2, PACK, N], F32, "w3_raw", "table_words")
         for a in range(2):
             nc.sync.dma_start(w3_raw[:, a], w3[PASS * a : PASS * (a + 1), :].rearrange("(p j) n -> p j n", j=PACK))
-        dealt = [load_dealt_weights(0)]
+        dealt_weights = [load_dealt_weights(0)]
         pages.append(load_page(PACK))
         villains = load_list(offs4, "villains")
-        rates = [held([P, PACK], F32, "rates%d" % b) for b in range(2)]
+        rates = [held([P, PACK], F32, "rates%d" % a) for a in range(2)]
         with nc.allow_non_contiguous_dma(reason="one rate a partition"):
             nc.sync.dma_start(rates[0][:], rate[0:PASS].rearrange("(u p) -> p u", p=P))
         nc.sync.dma_start(rates[1][:], rate[PASS:H].rearrange("(p t) -> p t", t=PACK))
         for t in range(1, PACK):
-            dealt.append(load_dealt_weights(t))
+            dealt_weights.append(load_dealt_weights(t))
             pages.append(load_page(PACK + t))
         w2_codes = held([P, 2, 2 * N], U8, "w2_codes")
         nc.sync.dma_start(w2_codes[:].bitcast(I32), w2_words.rearrange("a p c -> p a c").bitcast(I32))
         for q in range(4):
             nc.sync.dma_start(
-                w2_plane[32 * q : 32 * q + 4, :, :].bitcast(I32),
+                w2_scale_rows[32 * q : 32 * q + 4, :, :].bitcast(I32),
                 w2_scales[:, 4 * q : 4 * q + 4, :].rearrange("a r c -> r a c").bitcast(I32),
             )
         heroes = load_list(offs3, "heroes")
 
-        for u in range(1, PACK):
-            make_h(u, "lane%d" % (u % 3))
-            scatter(u, 0, S, plain_weights)
-        make_h(PACK, "lane%d" % (PACK % 3))
-        scatter(PACK, 0, S, dealt[0])
+        for u in range(1, PACK + 1):
+            make_h(u, "h_buffer%d" % (u % H_BUFFERS))
+            scatter(u, 0, S, plain_weights if u < PACK else dealt_weights[0])
 
         def make_gate(u, gate):
-            b, t = divmod(u, PACK)
+            a, t = divmod(u, PACK)
             nc.vector.tensor_copy(gate, pages[u][:].indirect(villains[:]))
-            nc.scalar.activation(gate, gate, SIGMOID, scale=rates[b][:, t : t + 1])
+            nc.scalar.activation(gate, gate, SIGMOID, scale=rates[a][:, t : t + 1])
 
         def read_hero(u, start, stop, gate, z):
-            nc.vector.tensor_tensor(
-                z, pages[u][:].indirect(list_slice(heroes, start, stop)), gate[:, start:stop], MULT
-            )
+            nc.vector.tensor_tensor(z, pages[u][:].indirect(list_slice(heroes, start, stop)), gate[:, start:stop], MULT)
 
         gates = [held([P, PAIRS], F32, "gate%d" % u) for u in range(PACK)]
         for u in range(PACK):
             make_gate(u, gates[u][:])
-        z0_rows = held([P, PACK, PAIRS], F32, "z0_rows")
-        z0_planes = held([P, PACK, PAIRS], F32, "z0_planes")
+        z0_plain = held([P, PACK, PAIRS], F32, "z0_plain")
+        z0_dealt = held([P, PACK, PAIRS], F32, "z0_dealt")
         for u in range(PACK):
-            read_hero(u, 0, PAIRS, gates[u][:], z0_rows[:, u, :])
+            read_hero(u, 0, PAIRS, gates[u][:], z0_plain[:, u, :])
             for t in range(PACK):
-                nc.sync.dma_start(z0_planes[32 * u : 32 * (u + 1), t, :], z0_rows[t:P:PACK, u, :])
+                nc.sync.dma_start(z0_dealt[32 * u : 32 * (u + 1), t, :], z0_plain[t:P:PACK, u, :])
+
         for u in range(PACK + 1, TILES):
             make_h(u, "gate%d" % (u - PACK - 1))
-            scatter(u, 0, S, dealt[u - PACK])
+            scatter(u, 0, S, dealt_weights[u - PACK])
         w3_staged = held([P, 2, N, PACK], BF16, "w3_staged", "w1_raw%d" % PASS)
-        w3_q = []
         for a in range(2):
             interleave(w3_staged[:, a], w3_raw[:, a])
-            w3_q.append(quantise(w3_staged[:, a], "w3_%d" % a))
+        w3_codes, w3_scales = quantise(w3_staged[:].rearrange("p a n t -> p (a n) t"), "w3")
         z0_staged = held([P, PAIRS, PACK], BF16, "z0_staged")
-        for start in range(0, PAIRS, CHUNK):
-            interleave(z0_staged[:, start : start + CHUNK, :], z0_planes[:, :, start : start + CHUNK])
-        z0_codes, z0_scales = quantise(z0_staged[:], "z0")
+        for start in range(0, PAIRS, QUARTER):
+            interleave(z0_staged[:, start : start + QUARTER, :], z0_dealt[:, :, start : start + QUARTER])
 
         sums = {}
 
-        def multiply(c, b, z_codes, z_scales):
+        def multiply(c, a, z_codes, z_scales):
             width = WIDTHS[c]
             per_bank = BANK // width
-            if b == 0:
-                sums[c] = [bank(FIRST_BANK[c] + i, "y_acc") for i in range(2 * PACK // per_bank)]
-            for g in range(PACK // per_bank):
+            if a == 0:
+                sums[c] = [bank(index, "y_acc") for index in BANKS[c]]
+            for g in range(N // P // per_bank):
                 y2, y1 = sums[c][2 * g], sums[c][2 * g + 1]
                 for i in range(per_bank):
-                    n = per_bank * g + i
+                    cols = slice(N * a + P * (per_bank * g + i), N * a + P * (per_bank * g + i + 1))
                     nc.tensor.matmul_mx(
                         out=y2[:, width * i : width * (i + 1)],
-                        lhsT=w3_q[b][0][:, P * n : P * (n + 1)].bitcast(FP8X4),
-                        lhsT_scale=w3_q[b][1][:, P * n : P * (n + 1)],
+                        lhsT=w3_codes[:, cols].bitcast(FP8X4),
+                        lhsT_scale=w3_scales[:, cols],
                         rhs=z_codes.bitcast(FP8X4),
                         rhs_scale=z_scales,
-                        start=(b == 0 and i == 0),
-                        stop=(b == 1 and i == per_bank - 1),
+                        start=(a == 0 and i == 0),
+                        stop=(a == 1 and i == per_bank - 1),
                     )
                 for i in range(BANK // P):
                     n, s = divmod(BANK // P * g + i, width // P)
                     nc.tensor.matmul_mx(
                         out=y1[:, P * i : P * (i + 1)],
-                        lhsT=w2_codes[:, b, 2 * P * n : 2 * P * (n + 1)].bitcast(FP4X4),
-                        lhsT_scale=w2_plane[:, b, P * n : P * (n + 1)],
+                        lhsT=w2_codes[:, a, 2 * P * n : 2 * P * (n + 1)].bitcast(FP4X4),
+                        lhsT_scale=w2_scale_rows[:, a, P * n : P * (n + 1)],
                         rhs=z_codes[:, P * s : P * (s + 1)].bitcast(FP8X4),
                         rhs_scale=z_scales[:, P * s : P * (s + 1)],
-                        start=(b == 0 and i == 0),
-                        stop=(b == 1 and i == BANK // P - 1),
+                        start=(a == 0 and i == 0),
+                        stop=(a == 1 and i == BANK // P - 1),
                     )
+
+        tanh_tags = ["wgs_dealt%d" % t for t in range(PACK)] + ["gate%d" % u for u in range(PACK)]
+        tanhs = {}
+
+        def squash(c):
+            for g in range(N // P * WIDTHS[c] // BANK):
+                tile = held([P, BANK], F32, "tanh%d_%d" % (c, g), tanh_tags[N // P * STARTS[c] // BANK + g])
+                nc.scalar.activation(tile[:], sums[c][2 * g][:], TANH)
+                tanhs[c, g] = tile
 
         def finish(c):
             width = WIDTHS[c]
             per_bank = BANK // width
-            for g in range(PACK // per_bank):
-                y2, y1 = sums[c][2 * g], sums[c][2 * g + 1]
-                squashed = held([P, BANK], F32, "squashed%d_%d" % (c, g), squash_tags[PACK * STARTS[c] // BANK + g])
-                nc.scalar.activation(squashed[:], y2[:], TANH)
-                for pair in range(per_bank // 2):
-                    cols = slice(2 * width * pair, 2 * width * (pair + 1))
-                    n = per_bank * g + 2 * pair
-                    place = PACK * STARTS[c] + width * n
+            for g in range(N // P // per_bank):
+                y1 = sums[c][2 * g + 1]
+                for two in range(per_bank // 2):
+                    cols = slice(2 * width * two, 2 * width * (two + 1))
+                    n = per_bank * g + 2 * two
+                    place = N // P * STARTS[c] + width * n
                     result = results[:, place : place + 2 * width]
-                    nc.vector.tensor_tensor(result, y1[:, cols], squashed[:, cols], MULT)
-                    row = P * n
+                    nc.vector.tensor_tensor(result, y1[:, cols], tanhs[c, g][:, cols], MULT)
                     nc.sync.dma_start(
-                        out[row : row + 2 * P, STARTS[c] : STARTS[c] + width].rearrange("(i p) m -> p i m", p=P),
+                        out[P * n : P * (n + 2), STARTS[c] : STARTS[c] + width].rearrange("(i p) m -> p i m", p=P),
                         result.rearrange("p (i m) -> p i m", i=2),
                     )
 
@@ -303,43 +302,50 @@ def tile_list_hero_villain_reads_kernel(
             cols = slice(STARTS[c], STARTS[c] + WIDTHS[c])
             multiply(c, 0, z0_codes[:, cols], z0_scales[:, cols])
 
-        late_gates = held([P, PACK, PAIRS], F32, "late_gates", "z0_planes")
+        late_gates = held([P, PACK, PAIRS], F32, "late_gates", "z0_dealt")
         for t in range(PACK):
             make_gate(PACK + t, late_gates[:, t, :])
+        z0_codes, z0_scales = quantise(z0_staged[:], "z0")
         first_pass(0)
         first_pass(1)
 
-        def read_chunk(c, tag):
-            planes = held([P, PACK, WIDTHS[c]], F32, "planes%d" % c, tag)
+        def read_chunks(first, last, tag):
+            start, stop = STARTS[first], STARTS[last] + WIDTHS[last]
+            z = held([P, PACK, stop - start], F32, "z1_%d" % first, tag)
             for t in range(PACK):
-                read_hero(PACK + t, STARTS[c], STARTS[c] + WIDTHS[c], late_gates[:, t, :], planes[:, t, :])
-            return planes[:]
+                read_hero(PACK + t, start, stop, late_gates[:, t, :], z[:, t, :])
+            return [z[:, :, STARTS[c] - start : STARTS[c] - start + WIDTHS[c]] for c in range(first, last + 1)]
 
         staging_tags = ("w1_raw0", "w1_raw128", "w1_raw256", "w1_staged0", "w1_staged128")
 
-        def second_pass(c, planes):
+        def stage(c, z):
             staged = held([P, WIDTHS[c], PACK], BF16, "z1_staged%d" % c, staging_tags[c])
-            interleave(staged[:], planes)
-            codes, scales = quantise(staged[:], "z1_%d" % c)
+            interleave(staged[:], z)
+            return staged
+
+        def second_pass(c, staged):
+            codes, scales = quantise(staged[:], "z1_q%d" % c)
             multiply(c, 1, codes[:], scales[:])
 
-        results = held([P, PACK * PAIRS], F32, "results", "table_words")
-        squash_tags = ["wgs_dealt%d" % t for t in range(PACK)] + ["gate%d" % t for t in range(PACK)]
-        planes0 = read_chunk(0, "lane0")
-        planes1 = read_chunk(1, "lane1")
-        second_pass(0, planes0)
-        planes2 = read_chunk(2, "lane0")
-        second_pass(1, planes1)
+        results = held([P, N // P * PAIRS], F32, "results", "table_words")
+        [z_chunk0] = read_chunks(0, 0, "h_buffer0")
+        [z_chunk1] = read_chunks(1, 1, "h_buffer1")
+        second_pass(0, stage(0, z_chunk0))
+        z_chunk2, z_chunk3 = read_chunks(2, 3, "h_buffer0")
+        second_pass(1, stage(1, z_chunk1))
+        squash(0)
         finish(0)
         first_pass(2)
-        planes3 = read_chunk(3, squash_tags[1])
-        second_pass(2, planes2)
-        finish(1)
+        [z_chunk4] = read_chunks(4, 4, tanh_tags[1])
+        squash(1)
         first_pass(3)
+        second_pass(2, stage(2, z_chunk2))
+        staged3 = stage(3, z_chunk3)
+        staged4 = stage(4, z_chunk4)
+        finish(1)
         first_pass(4)
-        planes4 = read_chunk(4, squash_tags[2])
-        second_pass(3, planes3)
-        second_pass(4, planes4)
-        finish(2)
-        finish(3)
-        finish(4)
+        second_pass(3, staged3)
+        second_pass(4, staged4)
+        for c in range(2, CHUNKS):
+            squash(c)
+            finish(c)

@@ -276,6 +276,12 @@ def tile_list_hero_villain_reads_kernel(
         tanh_tags = ["wgs_dealt%d" % t for t in range(PACK)] + ["gate%d" % u for u in range(PACK)]
         tanhs = {}
 
+        def store(c, n, result):
+            nc.sync.dma_start(
+                out[P * n : P * (n + 2), STARTS[c] : STARTS[c] + WIDTHS[c]].rearrange("(i p) m -> p i m", p=P),
+                result.rearrange("p (i m) -> p i m", i=2),
+            )
+
         def squash(c):
             for g in range(N // P * WIDTHS[c] // BANK):
                 tile = held([P, BANK], F32, "tanh%d_%d" % (c, g), tanh_tags[N // P * STARTS[c] // BANK + g])
@@ -293,28 +299,32 @@ def tile_list_hero_villain_reads_kernel(
                     place = N // P * STARTS[c] + width * n
                     result = results[:, place : place + 2 * width]
                     nc.vector.tensor_tensor(result, y1[:, cols], tanhs[c, g][:, cols], MULT)
-                    nc.sync.dma_start(
-                        out[P * n : P * (n + 2), STARTS[c] : STARTS[c] + width].rearrange("(i p) m -> p i m", p=P),
-                        result.rearrange("p (i m) -> p i m", i=2),
-                    )
+                    store(c, n, result)
 
         def first_pass(c):
             cols = slice(STARTS[c], STARTS[c] + WIDTHS[c])
             multiply(c, 0, z0_codes[:, cols], z0_scales[:, cols])
 
-        late_gates = held([P, PACK, PAIRS], F32, "late_gates", "z0_dealt")
+        late = held([P, PACK * PAIRS], F32, "late_gates", "z0_dealt")
+        first_gates = [late[:, HALF * t : HALF * (t + 1)] for t in range(PACK)]
+        rest_gates = [late[:, HALF * (PACK + t) : HALF * (PACK + t + 1)] for t in range(PACK)]
+
+        def read_villain(t, start, stop, raw, gate):
+            nc.vector.tensor_copy(raw, pages[PACK + t][:].indirect(list_slice(villains, start, stop)))
+            nc.scalar.activation(gate, raw, SIGMOID, scale=rates[1][:, t : t + 1])
+
+        def read_late(start, stop, z):
+            for t in range(PACK):
+                gate = (first_gates if start < HALF else rest_gates)[t][:, start % HALF : (stop - 1) % HALF + 1]
+                nc.vector.tensor_tensor(
+                    z[:, t, :], pages[PACK + t][:].indirect(list_slice(heroes, start, stop)), gate, MULT
+                )
+
         for t in range(PACK):
-            make_gate(PACK + t, late_gates[:, t, :])
+            read_villain(t, 0, HALF, first_gates[t], first_gates[t])
         z0_codes, z0_scales = quantise(z0_staged[:], "z0")
         first_pass(0)
         first_pass(1)
-
-        def read_chunks(first, last, tag):
-            start, stop = STARTS[first], STARTS[last] + WIDTHS[last]
-            z = held([P, PACK, stop - start], F32, "z1_%d" % first, tag)
-            for t in range(PACK):
-                read_hero(PACK + t, start, stop, late_gates[:, t, :], z[:, t, :])
-            return [z[:, :, STARTS[c] - start : STARTS[c] - start + WIDTHS[c]] for c in range(first, last + 1)]
 
         staging_tags = ("w1_raw0", "w1_raw128", "w1_raw256", "w1_staged0", "w1_staged128")
 
@@ -328,24 +338,46 @@ def tile_list_hero_villain_reads_kernel(
             multiply(c, 1, codes[:], scales[:])
 
         results = held([P, N // P * PAIRS], F32, "results", "table_words")
-        [z_chunk0] = read_chunks(0, 0, "h_buffer0")
-        [z_chunk1] = read_chunks(1, 1, "h_buffer1")
-        second_pass(0, stage(0, z_chunk0))
-        z_chunk2, z_chunk3 = read_chunks(2, 3, "h_buffer0")
-        second_pass(1, stage(1, z_chunk1))
-        squash(0)
-        finish(0)
+        z_chunk0 = held([P, PACK, 256], F32, "z1_0", "h_buffer0")
+        z_chunk1 = held([P, PACK, 256], F32, "z1_1", "h_buffer1")
+        read_late(0, 256, z_chunk0[:])
+        read_late(256, 512, z_chunk1[:])
+        second_pass(0, stage(0, z_chunk0[:]))
+        staged1 = stage(1, z_chunk1[:])
+        raw0 = held([P, HALF], F32, "raw_villains0", "h_buffer0")
+        nc.vector.tensor_copy(raw0[:], pages[PACK][:].indirect(list_slice(villains, HALF, PAIRS)))
+        second_pass(1, staged1)
+        at = PACK * HALF + HALF // 2
+        tanh_b = held([P, BANK], F32, "tanh0_b", "wgs_dealt1")
+        y1_b = held([P, BANK], F32, "y1_b", "wgs_dealt0")
+        pieces = ((late[:, at : at + BANK], late[:, at + 2 * BANK : at + 3 * BANK]), (tanh_b[:], y1_b[:]))
+        for g, (tanh_y2, y1) in enumerate(pieces):
+            nc.scalar.activation(tanh_y2, sums[0][2 * g][:], TANH)
+            nc.scalar.copy(y1, sums[0][2 * g + 1][:])
+            nc.gpsimd.tensor_tensor(results[:, BANK * g : BANK * (g + 1)], y1, tanh_y2, MULT)
+            store(0, 2 * g, results[:, BANK * g : BANK * (g + 1)])
         first_pass(2)
-        [z_chunk4] = read_chunks(4, 4, tanh_tags[1])
+        nc.scalar.activation(rest_gates[0], raw0[:], SIGMOID, scale=rates[1][:, 0:1])
+        raw = held([P, PACK - 1, HALF], F32, "raw_villains", "h_buffer1")
+        for t in range(1, PACK):
+            read_villain(t, HALF, PAIRS, raw[:, t - 1, :], rest_gates[t])
         squash(1)
         first_pass(3)
-        second_pass(2, stage(2, z_chunk2))
-        staged3 = stage(3, z_chunk3)
-        staged4 = stage(4, z_chunk4)
+
+        z_chunks23 = held([P, PACK, 384], F32, "z1_2", "wgs_dealt1")
+        read_late(512, 896, z_chunks23[:])
+        staged2 = stage(2, z_chunks23[:, :, 0:256])
         finish(1)
         first_pass(4)
+        second_pass(2, staged2)
+        staged3 = stage(3, z_chunks23[:, :, 256:384])
+        z_chunk4 = held([P, PACK, 128], F32, "z1_4", staging_tags[2])
+        read_late(896, 1024, z_chunk4[:])
         second_pass(3, staged3)
+        staged4 = stage(4, z_chunk4[:])
+        squash(2)
         second_pass(4, staged4)
-        for c in range(2, CHUNKS):
+        finish(2)
+        for c in range(3, CHUNKS):
             squash(c)
             finish(c)

@@ -27,10 +27,10 @@ QUARTER = S // 4
 LEAD = T // 4
 H_BANKS = 4
 H_BUFFERS = 3
-WIDTHS = (256, 256, 256, 128, 128)
-STARTS = (0, 256, 512, 768, 896)
+WIDTHS = (256, 128, 256, 256, 128)
+STARTS = (0, 256, 384, 640, 896)
 CHUNKS = len(WIDTHS)
-BANKS = ((4, 5, 6, 7), (0, 1, 2, 3), (4, 5, 6, 7), (0, 2), (1, 3))
+BANKS = ((4, 5, 6, 7), (0, 1), (4, 5, 6, 7), (2, 3, 0, 1), (4, 6))
 
 
 def list_slice(offsets, start, stop):
@@ -244,12 +244,17 @@ def tile_list_hero_villain_reads_kernel(
         sums = {}
 
         def multiply(c, a, z_codes, z_scales):
+            for g in range(N // P * WIDTHS[c] // BANK):
+                multiply_y2(c, a, g, z_codes, z_scales)
+                multiply_y1(c, a, g, z_codes, z_scales)
+
+        def multiply_y2(c, a, g, z_codes, z_scales):
             width = WIDTHS[c]
             per_bank = BANK // width
             if a == 0:
-                sums[c] = [bank(index, "y_acc") for index in BANKS[c]]
-            for g in range(N // P // per_bank):
-                y2, y1 = sums[c][2 * g], sums[c][2 * g + 1]
+                sums[c, 2 * g] = bank(BANKS[c][2 * g], "y_acc")
+            y2 = sums[c, 2 * g]
+            if True:
                 for i in range(per_bank):
                     cols = slice(N * a + P * (per_bank * g + i), N * a + P * (per_bank * g + i + 1))
                     nc.tensor.matmul_mx(
@@ -261,6 +266,13 @@ def tile_list_hero_villain_reads_kernel(
                         start=(a == 0 and i == 0),
                         stop=(a == 1 and i == per_bank - 1),
                     )
+
+        def multiply_y1(c, a, g, z_codes, z_scales):
+            width = WIDTHS[c]
+            if a == 0:
+                sums[c, 2 * g + 1] = bank(BANKS[c][2 * g + 1], "y_acc")
+            y1 = sums[c, 2 * g + 1]
+            if True:
                 for i in range(BANK // P):
                     n, s = divmod(BANK // P * g + i, width // P)
                     nc.tensor.matmul_mx(
@@ -285,14 +297,14 @@ def tile_list_hero_villain_reads_kernel(
         def squash(c):
             for g in range(N // P * WIDTHS[c] // BANK):
                 tile = held([P, BANK], F32, "tanh%d_%d" % (c, g), tanh_tags[N // P * STARTS[c] // BANK + g])
-                nc.scalar.activation(tile[:], sums[c][2 * g][:], TANH)
+                nc.scalar.activation(tile[:], sums[c, 2 * g][:], TANH)
                 tanhs[c, g] = tile
 
         def finish(c):
             width = WIDTHS[c]
             per_bank = BANK // width
             for g in range(N // P // per_bank):
-                y1 = sums[c][2 * g + 1]
+                y1 = sums[c, 2 * g + 1]
                 for two in range(per_bank // 2):
                     cols = slice(2 * width * two, 2 * width * (two + 1))
                     n = per_bank * g + 2 * two
@@ -305,28 +317,34 @@ def tile_list_hero_villain_reads_kernel(
             cols = slice(STARTS[c], STARTS[c] + WIDTHS[c])
             multiply(c, 0, z0_codes[:, cols], z0_scales[:, cols])
 
+        early = STARTS[2]
+        rest = PAIRS - early
         late = held([P, PACK * PAIRS], F32, "late_gates", "z0_dealt")
-        first_gates = [late[:, HALF * t : HALF * (t + 1)] for t in range(PACK)]
-        rest_gates = [late[:, HALF * (PACK + t) : HALF * (PACK + t + 1)] for t in range(PACK)]
+        first_gates = [late[:, early * t : early * (t + 1)] for t in range(PACK)]
+        rest_gates = [late[:, PACK * early + rest * t : PACK * early + rest * (t + 1)] for t in range(PACK)]
 
-        def read_villain(t, start, stop, raw, gate):
+        def read_villain(t, start, stop, raw):
             nc.vector.tensor_copy(raw, pages[PACK + t][:].indirect(list_slice(villains, start, stop)))
+
+        def open_gate(t, gate, raw):
             nc.scalar.activation(gate, raw, SIGMOID, scale=rates[1][:, t : t + 1])
 
-        def read_late(start, stop, z):
+        def read_late(c, z):
+            start, stop = STARTS[c], STARTS[c] + WIDTHS[c]
             for t in range(PACK):
-                gate = (first_gates if start < HALF else rest_gates)[t][:, start % HALF : (stop - 1) % HALF + 1]
+                gate = first_gates[t][:, start:stop] if start < early else rest_gates[t][:, start - early : stop - early]
                 nc.vector.tensor_tensor(
                     z[:, t, :], pages[PACK + t][:].indirect(list_slice(heroes, start, stop)), gate, MULT
                 )
 
         for t in range(PACK):
-            read_villain(t, 0, HALF, first_gates[t], first_gates[t])
+            read_villain(t, 0, early, first_gates[t])
+            open_gate(t, first_gates[t], first_gates[t])
         z0_codes, z0_scales = quantise(z0_staged[:], "z0")
         first_pass(0)
         first_pass(1)
 
-        staging_tags = ("w1_raw0", "w1_raw128", "w1_raw256", "w1_staged0", "w1_staged128")
+        staging_tags = ("w1_raw0", "w1_staged0", "w1_raw128", "w1_raw256", "w1_staged128")
 
         def stage(c, z):
             staged = held([P, WIDTHS[c], PACK], BF16, "z1_staged%d" % c, staging_tags[c])
@@ -338,46 +356,65 @@ def tile_list_hero_villain_reads_kernel(
             multiply(c, 1, codes[:], scales[:])
 
         results = held([P, N // P * PAIRS], F32, "results", "table_words")
-        z_chunk0 = held([P, PACK, 256], F32, "z1_0", "h_buffer0")
-        z_chunk1 = held([P, PACK, 256], F32, "z1_1", "h_buffer1")
-        read_late(0, 256, z_chunk0[:])
-        read_late(256, 512, z_chunk1[:])
+
+        def finish_on_gpsimd(c, g, tanh_y2, y1):
+            width = WIDTHS[c]
+            place = N // P * STARTS[c] + BANK * g
+            nc.scalar.activation(tanh_y2, sums[c, 2 * g][:], TANH)
+            nc.scalar.copy(y1, sums[c, 2 * g + 1][:])
+            nc.gpsimd.tensor_tensor(results[:, place : place + BANK], y1, tanh_y2, MULT)
+            for two in range(BANK // width // 2):
+                at = place + 2 * width * two
+                store(c, BANK // width * g + 2 * two, results[:, at : at + 2 * width])
+
+        z_chunk0 = held([P, PACK, WIDTHS[0]], F32, "z1_0", "h_buffer0")
+        z_chunk1 = held([P, PACK, WIDTHS[1]], F32, "z1_1", "h_buffer1")
+        read_late(0, z_chunk0[:])
+        read_late(1, z_chunk1[:])
         second_pass(0, stage(0, z_chunk0[:]))
         staged1 = stage(1, z_chunk1[:])
-        raw0 = held([P, HALF], F32, "raw_villains0", "h_buffer0")
-        nc.vector.tensor_copy(raw0[:], pages[PACK][:].indirect(list_slice(villains, HALF, PAIRS)))
+        raw0 = held([P, rest], F32, "raw_villains0", "h_buffer0")
+        read_villain(0, early, PAIRS, raw0[:])
         second_pass(1, staged1)
-        at = PACK * HALF + HALF // 2
-        tanh_b = held([P, BANK], F32, "tanh0_b", "wgs_dealt1")
-        y1_b = held([P, BANK], F32, "y1_b", "wgs_dealt0")
-        pieces = ((late[:, at : at + BANK], late[:, at + 2 * BANK : at + 3 * BANK]), (tanh_b[:], y1_b[:]))
-        for g, (tanh_y2, y1) in enumerate(pieces):
-            nc.scalar.activation(tanh_y2, sums[0][2 * g][:], TANH)
-            nc.scalar.copy(y1, sums[0][2 * g + 1][:])
-            nc.gpsimd.tensor_tensor(results[:, BANK * g : BANK * (g + 1)], y1, tanh_y2, MULT)
-            store(0, 2 * g, results[:, BANK * g : BANK * (g + 1)])
+        at = PACK * early + rest - BANK // 2
+        finish_on_gpsimd(0, 0, late[:, at : at + BANK], late[:, at + 2 * rest : at + 2 * rest + BANK])
+        finish_on_gpsimd(
+            0, 1, held([P, BANK], F32, "tanh0_b", "wgs_dealt0")[:], held([P, BANK], F32, "y1_0b", "wgs_dealt2")[:]
+        )
+        finish_on_gpsimd(
+            1, 0, held([P, BANK], F32, "tanh1", "wgs_dealt1")[:], held([P, BANK], F32, "y1_1", "h_buffer2")[:]
+        )
         first_pass(2)
-        nc.scalar.activation(rest_gates[0], raw0[:], SIGMOID, scale=rates[1][:, 0:1])
-        raw = held([P, PACK - 1, HALF], F32, "raw_villains", "h_buffer1")
-        for t in range(1, PACK):
-            read_villain(t, HALF, PAIRS, raw[:, t - 1, :], rest_gates[t])
-        squash(1)
         first_pass(3)
+        raw = held([P, PACK - 1, rest], F32, "raw_villains", "h_buffer1")
+        for t in range(1, PACK):
+            read_villain(t, early, PAIRS, raw[:, t - 1, :])
+        for t in range(PACK):
+            open_gate(t, rest_gates[t], raw0[:] if t == 0 else raw[:, t - 1, :])
 
-        z_chunks23 = held([P, PACK, 384], F32, "z1_2", "wgs_dealt1")
-        read_late(512, 896, z_chunks23[:])
-        staged2 = stage(2, z_chunks23[:, :, 0:256])
-        finish(1)
-        first_pass(4)
+        z_chunk2 = held([P, PACK, WIDTHS[2]], F32, "z1_2", "wgs_dealt1")
+        z_chunk3 = held([P, PACK, WIDTHS[3]], F32, "z1_3", "h_buffer1")
+        read_late(2, z_chunk2[:])
+        read_late(3, z_chunk3[:])
+        staged2 = stage(2, z_chunk2[:])
+        staged3 = stage(3, z_chunk3[:])
         second_pass(2, staged2)
-        staged3 = stage(3, z_chunks23[:, :, 256:384])
-        z_chunk4 = held([P, PACK, 128], F32, "z1_4", staging_tags[2])
-        read_late(896, 1024, z_chunk4[:])
-        second_pass(3, staged3)
-        staged4 = stage(4, z_chunk4[:])
         squash(2)
-        second_pass(4, staged4)
+        z_chunk4 = held([P, PACK, WIDTHS[4]], F32, "z1_4", staging_tags[2])
+        read_late(4, z_chunk4[:])
+        codes3, scales3 = quantise(staged3[:], "z1_q3")
+        for g in range(2):
+            multiply_y2(3, 1, g, codes3[:], scales3[:])
+        staged4 = stage(4, z_chunk4[:])
+        last = slice(STARTS[4], PAIRS)
+        multiply_y2(4, 0, 0, z0_codes[:, last], z0_scales[:, last])
+        for g in range(2):
+            multiply_y1(3, 1, g, codes3[:], scales3[:])
         finish(2)
+        codes4, scales4 = quantise(staged4[:], "z1_q4")
+        multiply_y2(4, 1, 0, codes4[:], scales4[:])
+        multiply_y1(4, 0, 0, z0_codes[:, last], z0_scales[:, last])
+        multiply_y1(4, 1, 0, codes4[:], scales4[:])
         for c in range(3, CHUNKS):
             squash(c)
             finish(c)

@@ -28,7 +28,7 @@ LEAD = T // 4
 H_BANKS = 4
 H_BUFFERS = 3
 WIDTHS = (256, 128, 256, 256, 128)
-STARTS = (0, 256, 384, 640, 896)
+STARTS = (0, 256, 512, 768, 384)
 CHUNKS = len(WIDTHS)
 BANKS = ((4, 5, 6, 7), (0, 1), (4, 5, 6, 7), (2, 3, 0, 1), (4, 6))
 
@@ -89,10 +89,10 @@ def tile_list_hero_villain_reads_kernel(
         def interleave(staged, rows):
             nc.scalar.copy(staged.rearrange("p (c i) t -> p c t i", i=4), rows.rearrange("p t (c i) -> p c t i", i=4))
 
-        def quantise(staged, name):
+        def quantise(staged, name, tag=None, scales_tag=None):
             width = staged.shape[1]
-            codes = held([P, width], U32, name + "_codes")
-            scales = held([P, width], U8, name + "_scales")
+            codes = held([P, width], U32, name + "_codes", tag)
+            scales = held([P, width], U8, name + "_scales", scales_tag)
             nc.vector.quantize_mx(
                 out=codes[:].bitcast(FP8X4), scales=scales[:], in_=staged.rearrange("p m t -> p (m t)")
             )
@@ -238,7 +238,7 @@ def tile_list_hero_villain_reads_kernel(
             interleave(w3_staged[:, a], w3_raw[:, a])
         w3_codes, w3_scales = quantise(w3_staged[:].rearrange("p a n t -> p (a n) t"), "w3")
         z0_staged = held([P, PAIRS, PACK], BF16, "z0_staged")
-        for start in range(0, PAIRS, QUARTER):
+        for start in reversed(range(0, PAIRS, QUARTER)):
             interleave(z0_staged[:, start : start + QUARTER, :], z0_dealt[:, :, start : start + QUARTER])
 
         sums = {}
@@ -285,7 +285,7 @@ def tile_list_hero_villain_reads_kernel(
                         stop=(a == 1 and i == BANK // P - 1),
                     )
 
-        tanh_tags = ["wgs_dealt%d" % t for t in range(PACK)] + ["gate%d" % u for u in range(PACK)]
+        tanh_tags = ["wgs_dealt%d" % t for t in range(PACK)] + ["gate0", "h_buffer1", "gate2", "gate3"]
         tanhs = {}
 
         def store(c, n, result):
@@ -294,16 +294,16 @@ def tile_list_hero_villain_reads_kernel(
                 result.rearrange("p (i m) -> p i m", i=2),
             )
 
-        def squash(c):
-            for g in range(N // P * WIDTHS[c] // BANK):
+        def squash(c, groups):
+            for g in groups:
                 tile = held([P, BANK], F32, "tanh%d_%d" % (c, g), tanh_tags[N // P * STARTS[c] // BANK + g])
                 nc.scalar.activation(tile[:], sums[c, 2 * g][:], TANH)
                 tanhs[c, g] = tile
 
-        def finish(c):
+        def finish(c, groups):
             width = WIDTHS[c]
             per_bank = BANK // width
-            for g in range(N // P // per_bank):
+            for g in groups:
                 y1 = sums[c, 2 * g + 1]
                 for two in range(per_bank // 2):
                     cols = slice(2 * width * two, 2 * width * (two + 1))
@@ -314,10 +314,10 @@ def tile_list_hero_villain_reads_kernel(
                     store(c, n, result)
 
         def first_pass(c):
-            cols = slice(STARTS[c], STARTS[c] + WIDTHS[c])
-            multiply(c, 0, z0_codes[:, cols], z0_scales[:, cols])
+            codes, scales = z0_q[c]
+            multiply(c, 0, codes, scales)
 
-        early = STARTS[2]
+        early = WIDTHS[0] + WIDTHS[1]
         rest = PAIRS - early
         late = held([P, PACK * PAIRS], F32, "late_gates", "z0_dealt")
         first_gates = [late[:, early * t : early * (t + 1)] for t in range(PACK)]
@@ -337,10 +337,20 @@ def tile_list_hero_villain_reads_kernel(
                     z[:, t, :], pages[PACK + t][:].indirect(list_slice(heroes, start, stop)), gate, MULT
                 )
 
+        raw = held([P, PACK, early], F32, "raw_villains0", "gate1")
         for t in range(PACK):
-            read_villain(t, 0, early, first_gates[t])
-            open_gate(t, first_gates[t], first_gates[t])
-        z0_codes, z0_scales = quantise(z0_staged[:], "z0")
+            read_villain(t, 0, early, raw[:, t, :])
+            open_gate(t, first_gates[t], raw[:, t, :])
+        z0_codes, z0_scales = quantise(z0_staged[:, 0:HALF, :], "z0_a")
+        z0_q = {}
+        for c in range(2):
+            cols = slice(STARTS[c], STARTS[c] + WIDTHS[c])
+            z0_q[c] = (z0_codes[:, cols], z0_scales[:, cols])
+
+        def quantise_z0(c, tag, scales_tag):
+            codes, scales = quantise(z0_staged[:, STARTS[c] : STARTS[c] + WIDTHS[c], :], "z0_%d" % c, tag, scales_tag)
+            z0_q[c] = (codes[:], scales[:])
+
         first_pass(0)
         first_pass(1)
 
@@ -368,13 +378,12 @@ def tile_list_hero_villain_reads_kernel(
                 store(c, BANK // width * g + 2 * two, results[:, at : at + 2 * width])
 
         z_chunk0 = held([P, PACK, WIDTHS[0]], F32, "z1_0", "h_buffer0")
-        z_chunk1 = held([P, PACK, WIDTHS[1]], F32, "z1_1", "h_buffer1")
+        z_chunk1 = held([P, PACK, WIDTHS[1]], F32, "z1_1", "gate1")
         read_late(0, z_chunk0[:])
         read_late(1, z_chunk1[:])
         second_pass(0, stage(0, z_chunk0[:]))
         staged1 = stage(1, z_chunk1[:])
-        raw0 = held([P, rest], F32, "raw_villains0", "h_buffer0")
-        read_villain(0, early, PAIRS, raw0[:])
+        quantise_z0(2, "h_buffer0", None)
         second_pass(1, staged1)
         at = PACK * early + rest - BANK // 2
         finish_on_gpsimd(0, 0, late[:, at : at + BANK], late[:, at + 2 * rest : at + 2 * rest + BANK])
@@ -385,36 +394,43 @@ def tile_list_hero_villain_reads_kernel(
             1, 0, held([P, BANK], F32, "tanh1", "wgs_dealt1")[:], held([P, BANK], F32, "y1_1", "h_buffer2")[:]
         )
         first_pass(2)
-        first_pass(3)
-        raw = held([P, PACK - 1, rest], F32, "raw_villains", "h_buffer1")
-        for t in range(1, PACK):
-            read_villain(t, early, PAIRS, raw[:, t - 1, :])
+        raw = held([P, PACK, rest], F32, "raw_villains1", "gate1")
         for t in range(PACK):
-            open_gate(t, rest_gates[t], raw0[:] if t == 0 else raw[:, t - 1, :])
+            read_villain(t, early, PAIRS, raw[:, t, :])
+        for t in range(PACK):
+            open_gate(t, rest_gates[t], raw[:, t, :])
 
         z_chunk2 = held([P, PACK, WIDTHS[2]], F32, "z1_2", "wgs_dealt1")
-        z_chunk3 = held([P, PACK, WIDTHS[3]], F32, "z1_3", "h_buffer1")
+        z_chunk3 = held([P, PACK, WIDTHS[3]], F32, "z1_3", "gate1")
         read_late(2, z_chunk2[:])
+        quantise_z0(3, None, "rates1")
+        first_pass(3)
         read_late(3, z_chunk3[:])
         staged2 = stage(2, z_chunk2[:])
         staged3 = stage(3, z_chunk3[:])
         second_pass(2, staged2)
-        squash(2)
-        z_chunk4 = held([P, PACK, WIDTHS[4]], F32, "z1_4", staging_tags[2])
+        squash(2, [0])
+        z_chunk4 = held([P, PACK, WIDTHS[4]], F32, "z1_4", "wgs_dealt1")
         read_late(4, z_chunk4[:])
+        squash(2, [1])
         codes3, scales3 = quantise(staged3[:], "z1_q3")
         for g in range(2):
             multiply_y2(3, 1, g, codes3[:], scales3[:])
-        staged4 = stage(4, z_chunk4[:])
-        last = slice(STARTS[4], PAIRS)
+        staged4 = held([P, WIDTHS[4], PACK], BF16, "z1_staged4", "gate1")
+        nc.vector.tensor_copy(
+            staged4[:].rearrange("p (c i) t -> p c t i", i=4), z_chunk4[:].rearrange("p t (c i) -> p c t i", i=4)
+        )
+        last = slice(STARTS[4], HALF)
         multiply_y2(4, 0, 0, z0_codes[:, last], z0_scales[:, last])
-        for g in range(2):
-            multiply_y1(3, 1, g, codes3[:], scales3[:])
-        finish(2)
+        multiply_y1(3, 1, 0, codes3[:], scales3[:])
+        finish(2, [0])
         codes4, scales4 = quantise(staged4[:], "z1_q4")
         multiply_y2(4, 1, 0, codes4[:], scales4[:])
+        multiply_y1(3, 1, 1, codes3[:], scales3[:])
         multiply_y1(4, 0, 0, z0_codes[:, last], z0_scales[:, last])
         multiply_y1(4, 1, 0, codes4[:], scales4[:])
-        for c in range(3, CHUNKS):
-            squash(c)
-            finish(c)
+        finish(2, [1])
+        squash(3, [0, 1])
+        finish(3, [0, 1])
+        squash(4, [0])
+        finish(4, [0])

@@ -24,6 +24,7 @@ TILES = H // P
 BANK = 512
 HALF = S // 2
 QUARTER = S // 4
+FIRST = 384
 LEAD = T // 4
 H_BANKS = 4
 H_BUFFERS = 3
@@ -44,9 +45,12 @@ def tile_list_hero_villain_reads_kernel(
     with ExitStack() as ctx:
         lists = ctx.enter_context(tc.tile_pool(name="lists", bufs=1))
         keep = ctx.enter_context(tc.tile_pool(name="keep", bufs=1))
+        reuse = ctx.enter_context(tc.tile_pool(name="reuse", bufs=1))
         psum = ctx.enter_context(tc.psum_pool(name="psum", bufs=1))
 
         def held(shape, dtype, name, tag=None):
+            if tag is not None and tag.startswith("wgs_dealt"):
+                return reuse.tile(shape, dtype, name=name, tag=name, align_bytes=64, offset=4 * S * int(tag[-1]))
             return keep.tile(shape, dtype, name=name, tag=tag or name, align_bytes=64)
 
         def bank(index, name):
@@ -70,12 +74,12 @@ def tile_list_hero_villain_reads_kernel(
             nc.sync.dma_start(raw[:], w1[:, start:stop].rearrange("(p j) c -> p j c", j=PACK))
             return raw
 
-        def load_dealt_weights(t):
-            tile = held([P, S], F32, "wgs_dealt%d" % t)
-            rows = wgs.rearrange("(q t) j -> t q j", t=PACK)[t]
+        def load_dealt_weights():
+            tile = held([P, PACK * S], F32, "wgs_dealt", "wgs_dealt0")
+            rows = wgs.rearrange("(q t) j -> q (t j)", t=PACK)
             for q in (0, 2, 1, 3):
                 nc.sync.dma_start(tile[32 * q : 32 * (q + 1), :], rows)
-            return tile
+            return [tile[:, S * t : S * (t + 1)] for t in range(PACK)]
 
         def load_page(u):
             tile = held([P, T2], F32, "page%d" % u)
@@ -100,14 +104,15 @@ def tile_list_hero_villain_reads_kernel(
 
         w1_q = {}
 
-        def prepare_w1(raw, start, stop):
+        def prepare_w1(raws, start, stop):
             staged = held([P, stop - start, PACK], BF16, "w1_staged%d" % start)
             if start < PASS:
-                interleave(staged[:], raw[:])
+                for i, raw in enumerate(raws):
+                    interleave(staged[:, P * i : P * (i + 1), :], raw[:])
             else:
                 nc.scalar.copy(
                     staged[:].rearrange("p (t m) j -> p m t j", t=PACK),
-                    raw[:].rearrange("p j (m t) -> p m t j", t=PACK),
+                    raws[0][:].rearrange("p j (m t) -> p m t j", t=PACK),
                 )
             codes, scales = quantise(staged[:], "w1_%d" % start)
             for u in range(start // P, stop // P):
@@ -132,19 +137,20 @@ def tile_list_hero_villain_reads_kernel(
         nc.sync.dma_start(table_scales[0:P:8, :].bitcast(I32), tab_scales[0].bitcast(I32))
         nc.sync.dma_start(table_words[:, LEAD:T].bitcast(I32), words[:, LEAD:T])
         plain_weights = held([P, S], F32, "wgs_plain")
-        nc.sync.dma_start(plain_weights[:, 0:HALF], wgs[:, 0:HALF])
+        nc.sync.dma_start(plain_weights[:, 0:FIRST], wgs[:, 0:FIRST])
         picked = [pick_scales(0)]
         move_scales(0, picked[0])
-        prepare_w1(w1_tile0, 0, P)
+        prepare_w1([w1_tile0], 0, P)
         picked.append(pick_scales(1))
         pages = [load_page(0)]
         move_scales(1, picked[1])
         w1_tile1 = load_w1(P, 2 * P)
-        w1_tiles23 = load_w1(2 * P, PASS)
-        nc.sync.dma_start(plain_weights[:, HALF:S], wgs[:, HALF:S])
-        v_words = [held([P, HALF], U32, "v_words%d" % c) for c in range(2)]
-        for c in range(2):
-            nc.vector.tensor_copy(v_words[c][:], table_words[:].indirect(list_slice(picks, HALF * c, HALF * (c + 1))))
+        w1_tile2 = load_w1(2 * P, 3 * P)
+        nc.sync.dma_start(plain_weights[:, FIRST:S], wgs[:, FIRST:S])
+        w1_tile3 = load_w1(3 * P, PASS)
+        v_words = held([P, S], U32, "v_words")
+        for start, stop in ((0, FIRST), (FIRST, S)):
+            nc.vector.tensor_copy(v_words[:, start:stop], table_words[:].indirect(list_slice(picks, start, stop)))
 
         h_rows = {}
         h_products = []
@@ -152,7 +158,7 @@ def tile_list_hero_villain_reads_kernel(
         def make_h(u, tag):
             codes, scales = w1_q[u]
             h_rows[u] = held([P, S], F32, "h%d" % u, tag)
-            pieces = ((0, QUARTER), (QUARTER, HALF), (HALF, S)) if u == 0 else ((0, HALF), (HALF, S))
+            pieces = ((0, QUARTER), (QUARTER, FIRST), (FIRST, HALF), (HALF, S)) if u == 0 else ((0, HALF), (HALF, S))
             for start, stop in pieces:
                 c, at = divmod(start, HALF)
                 acc = bank(len(h_products) % H_BANKS, "h_acc")
@@ -161,7 +167,7 @@ def tile_list_hero_villain_reads_kernel(
                     out=acc[:, 0 : stop - start],
                     lhsT=codes.bitcast(FP8X4),
                     lhsT_scale=scales,
-                    rhs=v_words[c][:, at : at + stop - start].bitcast(FP8X4),
+                    rhs=v_words[:, start:stop].bitcast(FP8X4),
                     rhs_scale=v_scales[c][:, at : at + stop - start],
                     start=True,
                     stop=True,
@@ -177,19 +183,20 @@ def tile_list_hero_villain_reads_kernel(
             )
 
         make_h(0, "h_buffer0")
-        scatter(0, 0, HALF, plain_weights)
-        prepare_w1(w1_tile1, P, 2 * P)
-        scatter(0, HALF, S, plain_weights)
-        prepare_w1(w1_tiles23, 2 * P, PASS)
+        scatter(0, 0, FIRST, plain_weights)
+        prepare_w1([w1_tile1], P, 2 * P)
+        scatter(0, FIRST, S, plain_weights)
+        prepare_w1([w1_tile2, w1_tile3], 2 * P, PASS)
 
         pages.append(load_page(1))
-        prepare_w1(load_w1(PASS, H), PASS, H)
+        prepare_w1([load_w1(PASS, H)], PASS, H)
         for u in range(2, PACK):
             pages.append(load_page(u))
         w3_raw = held([P, 2, PACK, N], F32, "w3_raw", "table_words")
-        for a in range(2):
-            nc.sync.dma_start(w3_raw[:, a], w3[PASS * a : PASS * (a + 1), :].rearrange("(p j) n -> p j n", j=PACK))
-        dealt_weights = [load_dealt_weights(0)]
+        nc.sync.dma_start(
+            w3_raw[:].rearrange("p a j n -> p a (j n)"), w3.rearrange("(a p j) n -> p a (j n)", p=P, j=PACK)
+        )
+        dealt_weights = load_dealt_weights()
         pages.append(load_page(PACK))
         villains = load_list(offs4, "villains")
         rates = [held([P, PACK], F32, "rates%d" % a) for a in range(2)]
@@ -197,7 +204,6 @@ def tile_list_hero_villain_reads_kernel(
             nc.sync.dma_start(rates[0][:], rate[0:PASS].rearrange("(u p) -> p u", p=P))
         nc.sync.dma_start(rates[1][:], rate[PASS:H].rearrange("(p t) -> p t", t=PACK))
         for t in range(1, PACK):
-            dealt_weights.append(load_dealt_weights(t))
             pages.append(load_page(PACK + t))
         w2_codes = held([P, 2, 2 * N], U8, "w2_codes")
         nc.sync.dma_start(w2_codes[:].bitcast(I32), w2_words.rearrange("a p c -> p a c").bitcast(I32))
@@ -272,26 +278,26 @@ def tile_list_hero_villain_reads_kernel(
             if a == 0:
                 sums[c, 2 * g + 1] = bank(BANKS[c][2 * g + 1], "y_acc")
             y1 = sums[c, 2 * g + 1]
-            if True:
-                for i in range(BANK // P):
-                    n, s = divmod(BANK // P * g + i, width // P)
-                    nc.tensor.matmul_mx(
-                        out=y1[:, P * i : P * (i + 1)],
-                        lhsT=w2_codes[:, a, 2 * P * n : 2 * P * (n + 1)].bitcast(FP4X4),
-                        lhsT_scale=w2_scale_rows[:, a, P * n : P * (n + 1)],
-                        rhs=z_codes[:, P * s : P * (s + 1)].bitcast(FP8X4),
-                        rhs_scale=z_scales[:, P * s : P * (s + 1)],
-                        start=(a == 0 and i == 0),
-                        stop=(a == 1 and i == BANK // P - 1),
-                    )
+            per_bank = BANK // width
+            for i in range(per_bank):
+                n = per_bank * g + i
+                nc.tensor.matmul_mx(
+                    out=y1[:, width * i : width * (i + 1)],
+                    lhsT=w2_codes[:, a, 2 * P * n : 2 * P * (n + 1)].bitcast(FP4X4),
+                    lhsT_scale=w2_scale_rows[:, a, P * n : P * (n + 1)],
+                    rhs=z_codes.bitcast(FP8X4),
+                    rhs_scale=z_scales,
+                    start=(a == 0 and i == 0),
+                    stop=(a == 1 and i == per_bank - 1),
+                )
 
         tanh_tags = ["wgs_dealt%d" % t for t in range(PACK)] + ["gate0", "h_buffer1", "gate2", "gate3"]
         tanhs = {}
 
-        def store(c, n, result):
+        def store(c, n, result, count=2):
             nc.sync.dma_start(
-                out[P * n : P * (n + 2), STARTS[c] : STARTS[c] + WIDTHS[c]].rearrange("(i p) m -> p i m", p=P),
-                result.rearrange("p (i m) -> p i m", i=2),
+                out[P * n : P * (n + count), STARTS[c] : STARTS[c] + WIDTHS[c]].rearrange("(i p) m -> p i m", p=P),
+                result.rearrange("p (i m) -> p i m", i=count),
             )
 
         def squash(c, groups):
@@ -305,13 +311,13 @@ def tile_list_hero_villain_reads_kernel(
             per_bank = BANK // width
             for g in groups:
                 y1 = sums[c, 2 * g + 1]
-                for two in range(per_bank // 2):
-                    cols = slice(2 * width * two, 2 * width * (two + 1))
-                    n = per_bank * g + 2 * two
+                for half in range(2):
+                    cols = slice(BANK // 2 * half, BANK // 2 * (half + 1))
+                    n = per_bank * g + per_bank // 2 * half
                     place = N // P * STARTS[c] + width * n
-                    result = results[:, place : place + 2 * width]
+                    result = results[:, place : place + BANK // 2]
                     nc.vector.tensor_tensor(result, y1[:, cols], tanhs[c, g][:, cols], MULT)
-                    store(c, n, result)
+                    store(c, n, result, per_bank // 2)
 
         def first_pass(c):
             codes, scales = z0_q[c]
@@ -329,13 +335,15 @@ def tile_list_hero_villain_reads_kernel(
         def open_gate(t, gate, raw):
             nc.scalar.activation(gate, raw, SIGMOID, scale=rates[1][:, t : t + 1])
 
-        def read_late(c, z):
-            start, stop = STARTS[c], STARTS[c] + WIDTHS[c]
-            for t in range(PACK):
+        def read_pairs(start, stop, slots_read, z):
+            for i, t in enumerate(slots_read):
                 gate = first_gates[t][:, start:stop] if start < early else rest_gates[t][:, start - early : stop - early]
                 nc.vector.tensor_tensor(
-                    z[:, t, :], pages[PACK + t][:].indirect(list_slice(heroes, start, stop)), gate, MULT
+                    z[:, i, :], pages[PACK + t][:].indirect(list_slice(heroes, start, stop)), gate, MULT
                 )
+
+        def read_late(c, z, slots_read=range(PACK)):
+            read_pairs(STARTS[c], STARTS[c] + WIDTHS[c], slots_read, z)
 
         raw = held([P, PACK, early], F32, "raw_villains0", "gate1")
         for t in range(PACK):
@@ -361,6 +369,11 @@ def tile_list_hero_villain_reads_kernel(
             interleave(staged[:], z)
             return staged
 
+        def stage_low(c, z):
+            staged = held([P, WIDTHS[c], PACK], BF16, "z1_staged%d" % c, staging_tags[c])
+            interleave(staged[:, :, 0:2], z)
+            return staged
+
         def second_pass(c, staged):
             codes, scales = quantise(staged[:], "z1_q%d" % c)
             multiply(c, 1, codes[:], scales[:])
@@ -377,13 +390,18 @@ def tile_list_hero_villain_reads_kernel(
                 at = place + 2 * width * two
                 store(c, BANK // width * g + 2 * two, results[:, at : at + 2 * width])
 
-        z_chunk0 = held([P, PACK, WIDTHS[0]], F32, "z1_0", "h_buffer0")
-        z_chunk1 = held([P, PACK, WIDTHS[1]], F32, "z1_1", "gate1")
-        read_late(0, z_chunk0[:])
-        read_late(1, z_chunk1[:])
-        second_pass(0, stage(0, z_chunk0[:]))
-        staged1 = stage(1, z_chunk1[:])
+        z_low = held([P, 2, early], F32, "z1_low", "h_buffer0")
+        z_chunk0 = held([P, 2, WIDTHS[0]], F32, "z1_0", "h_buffer2")
+        z_chunk1 = held([P, 2, WIDTHS[1]], F32, "z1_1", "gate1")
+        read_pairs(0, early, (0, 1), z_low[:])
+        read_late(0, z_chunk0[:], (2, 3))
+        read_late(1, z_chunk1[:], (2, 3))
+        staged0 = stage_low(0, z_low[:, :, 0 : WIDTHS[0]])
+        staged1 = stage_low(1, z_low[:, :, WIDTHS[0] : early])
+        interleave(staged0[:, :, 2:4], z_chunk0[:])
+        interleave(staged1[:, :, 2:4], z_chunk1[:])
         quantise_z0(2, "h_buffer0", None)
+        second_pass(0, staged0)
         second_pass(1, staged1)
         at = PACK * early + rest - BANK // 2
         finish_on_gpsimd(0, 0, late[:, at : at + BANK], late[:, at + 2 * rest : at + 2 * rest + BANK])

@@ -74,12 +74,12 @@ def tile_list_hero_villain_reads_kernel(
             nc.sync.dma_start(raw[:], w1[:, start:stop].rearrange("(p j) c -> p j c", j=PACK))
             return raw
 
-        def load_dealt_weights():
-            tile = held([P, PACK * S], F32, "wgs_dealt", "wgs_dealt0")
-            rows = wgs.rearrange("(q t) j -> q (t j)", t=PACK)
+        def load_dealt_weights(first, count):
+            tile = held([P, count * S], F32, "wgs_rows%d" % first, "wgs_dealt%d" % first)
+            rows = wgs.rearrange("(q t) j -> q (t j)", t=PACK)[:, S * first : S * (first + count)]
             for q in (0, 2, 1, 3):
                 nc.sync.dma_start(tile[32 * q : 32 * (q + 1), :], rows)
-            return [tile[:, S * t : S * (t + 1)] for t in range(PACK)]
+            return [tile[:, S * t : S * (t + 1)] for t in range(count)]
 
         def load_page(u):
             tile = held([P, T2], F32, "page%d" % u)
@@ -196,15 +196,18 @@ def tile_list_hero_villain_reads_kernel(
         nc.sync.dma_start(
             w3_raw[:].rearrange("p a j n -> p a (j n)"), w3.rearrange("(a p j) n -> p a (j n)", p=P, j=PACK)
         )
-        dealt_weights = load_dealt_weights()
+        dealt_weights = load_dealt_weights(0, 1)
         pages.append(load_page(PACK))
         villains = load_list(offs4, "villains")
         rates = [held([P, PACK], F32, "rates%d" % a) for a in range(2)]
         with nc.allow_non_contiguous_dma(reason="one rate a partition"):
             nc.sync.dma_start(rates[0][:], rate[0:PASS].rearrange("(u p) -> p u", p=P))
         nc.sync.dma_start(rates[1][:], rate[PASS:H].rearrange("(p t) -> p t", t=PACK))
-        for t in range(1, PACK):
-            pages.append(load_page(PACK + t))
+        for u in range(PACK + 1, TILES):
+            pages.append(load_page(u))
+        heroes = load_list(offs3, "heroes")
+        dealt_weights.extend(load_dealt_weights(1, 1))
+        dealt_weights.extend(load_dealt_weights(2, 2))
         w2_codes = held([P, 2, 2 * N], U8, "w2_codes")
         nc.sync.dma_start(w2_codes[:].bitcast(I32), w2_words.rearrange("a p c -> p a c").bitcast(I32))
         for q in range(4):
@@ -212,7 +215,6 @@ def tile_list_hero_villain_reads_kernel(
                 w2_scale_rows[32 * q : 32 * q + 4, :, :].bitcast(I32),
                 w2_scales[:, 4 * q : 4 * q + 4, :].rearrange("a r c -> r a c").bitcast(I32),
             )
-        heroes = load_list(offs3, "heroes")
 
         for u in range(1, PACK + 1):
             make_h(u, "h_buffer%d" % (u % H_BUFFERS))

@@ -392,18 +392,13 @@ def tile_list_hero_villain_reads_kernel(
                 at = place + 2 * width * two
                 store(c, BANK // width * g + 2 * two, results[:, at : at + 2 * width])
 
-        z_low = held([P, 2, early], F32, "z1_low", "h_buffer0")
-        z_chunk0 = held([P, 2, WIDTHS[0]], F32, "z1_0", "h_buffer2")
-        z_chunk1 = held([P, 2, WIDTHS[1]], F32, "z1_1", "gate1")
-        read_pairs(0, early, (0, 1), z_low[:])
-        read_late(0, z_chunk0[:], (2, 3))
-        read_late(1, z_chunk1[:], (2, 3))
-        staged0 = stage_low(0, z_low[:, :, 0 : WIDTHS[0]])
-        staged1 = stage_low(1, z_low[:, :, WIDTHS[0] : early])
-        interleave(staged0[:, :, 2:4], z_chunk0[:])
-        interleave(staged1[:, :, 2:4], z_chunk1[:])
+        z_chunk0 = held([P, PACK, WIDTHS[0]], F32, "z1_0", "h_buffer0")
+        z_chunk1 = held([P, PACK, WIDTHS[1]], F32, "z1_1", "gate1")
+        read_late(0, z_chunk0[:])
+        read_late(1, z_chunk1[:])
+        second_pass(0, stage(0, z_chunk0[:]))
+        staged1 = stage(1, z_chunk1[:])
         quantise_z0(2, "h_buffer0", None)
-        second_pass(0, staged0)
         second_pass(1, staged1)
         at = PACK * early + rest - BANK // 2
         finish_on_gpsimd(0, 0, late[:, at : at + BANK], late[:, at + 2 * rest : at + 2 * rest + BANK])

@@ -26,11 +26,11 @@ HALF = S // 2
 QUARTER = S // 4
 FIRST = 384
 LEAD = T // 4
+AHEAD = T2 // 4
 H_BANKS = 4
 H_BUFFERS = 3
 WIDTHS = (256, 128, 256, 256, 128)
 STARTS = (0, 256, 512, 768, 384)
-CHUNKS = len(WIDTHS)
 BANKS = ((4, 5, 6, 7), (0, 1), (4, 5, 6, 7), (2, 3, 0, 1), (4, 6))
 
 
@@ -49,9 +49,10 @@ def tile_list_hero_villain_reads_kernel(
         psum = ctx.enter_context(tc.psum_pool(name="psum", bufs=1))
 
         def held(shape, dtype, name, tag=None):
-            if tag is not None and tag.startswith("wgs_dealt"):
-                return reuse.tile(shape, dtype, name=name, tag=name, align_bytes=64, offset=4 * S * int(tag[-1]))
             return keep.tile(shape, dtype, name=name, tag=tag or name, align_bytes=64)
+
+        def placed(shape, name, place):
+            return reuse.tile(shape, F32, name=name, tag=name, align_bytes=64, offset=4 * S * place)
 
         def bank(index, name):
             return psum.tile([P, BANK], F32, name=name, tag="bank%d" % index)
@@ -75,7 +76,7 @@ def tile_list_hero_villain_reads_kernel(
             return raw
 
         def load_dealt_weights(first, count):
-            tile = held([P, count * S], F32, "wgs_rows%d" % first, "wgs_dealt%d" % first)
+            tile = placed([P, count * S], "wgs_rows%d" % first, first)
             rows = wgs.rearrange("(q t) j -> q (t j)", t=PACK)[:, S * first : S * (first + count)]
             for q in (0, 2, 1, 3):
                 nc.sync.dma_start(tile[32 * q : 32 * (q + 1), :], rows)
@@ -138,11 +139,13 @@ def tile_list_hero_villain_reads_kernel(
         nc.sync.dma_start(table_words[:, LEAD:T].bitcast(I32), words[:, LEAD:T])
         plain_weights = held([P, S], F32, "wgs_plain")
         nc.sync.dma_start(plain_weights[:, 0:FIRST], wgs[:, 0:FIRST])
+        pages = [held([P, T2], F32, "page0")]
+        nc.sync.dma_start(pages[0][:, 0:AHEAD], page0[0:P, 0:AHEAD])
         picked = [pick_scales(0)]
         move_scales(0, picked[0])
         prepare_w1([w1_tile0], 0, P)
         picked.append(pick_scales(1))
-        pages = [load_page(0)]
+        nc.sync.dma_start(pages[0][:, AHEAD:T2], page0[0:P, AHEAD:T2])
         move_scales(1, picked[1])
         w1_tile1 = load_w1(P, 2 * P)
         w1_tile2 = load_w1(2 * P, 3 * P)
@@ -220,17 +223,20 @@ def tile_list_hero_villain_reads_kernel(
             make_h(u, "h_buffer%d" % (u % H_BUFFERS))
             scatter(u, 0, S, plain_weights if u < PACK else dealt_weights[0])
 
-        def make_gate(u, gate):
+        def read_villain(u, start, stop, raw):
+            nc.vector.tensor_copy(raw, pages[u][:].indirect(list_slice(villains, start, stop)))
+
+        def open_gate(u, gate, raw):
             a, t = divmod(u, PACK)
-            nc.vector.tensor_copy(gate, pages[u][:].indirect(villains[:]))
-            nc.scalar.activation(gate, gate, SIGMOID, scale=rates[a][:, t : t + 1])
+            nc.scalar.activation(gate, raw, SIGMOID, scale=rates[a][:, t : t + 1])
 
         def read_hero(u, start, stop, gate, z):
-            nc.vector.tensor_tensor(z, pages[u][:].indirect(list_slice(heroes, start, stop)), gate[:, start:stop], MULT)
+            nc.vector.tensor_tensor(z, pages[u][:].indirect(list_slice(heroes, start, stop)), gate, MULT)
 
         gates = [held([P, PAIRS], F32, "gate%d" % u) for u in range(PACK)]
         for u in range(PACK):
-            make_gate(u, gates[u][:])
+            read_villain(u, 0, PAIRS, gates[u][:])
+            open_gate(u, gates[u][:], gates[u][:])
         z0_plain = held([P, PACK, PAIRS], F32, "z0_plain")
         z0_dealt = held([P, PACK, PAIRS], F32, "z0_dealt")
         for u in range(PACK):
@@ -249,111 +255,97 @@ def tile_list_hero_villain_reads_kernel(
         for start in reversed(range(0, PAIRS, QUARTER)):
             interleave(z0_staged[:, start : start + QUARTER, :], z0_dealt[:, :, start : start + QUARTER])
 
-        sums = {}
+        y2_sums = {}
+        y1_sums = {}
 
-        def multiply(c, a, z_codes, z_scales):
-            for g in range(N // P * WIDTHS[c] // BANK):
-                multiply_y2(c, a, g, z_codes, z_scales)
-                multiply_y1(c, a, g, z_codes, z_scales)
-
-        def multiply_y2(c, a, g, z_codes, z_scales):
+        def multiply_group(acc, c, a, g, stationary, z_codes, z_scales):
             width = WIDTHS[c]
-            per_bank = BANK // width
-            if a == 0:
-                sums[c, 2 * g] = bank(BANKS[c][2 * g], "y_acc")
-            y2 = sums[c, 2 * g]
-            if True:
-                for i in range(per_bank):
-                    cols = slice(N * a + P * (per_bank * g + i), N * a + P * (per_bank * g + i + 1))
-                    nc.tensor.matmul_mx(
-                        out=y2[:, width * i : width * (i + 1)],
-                        lhsT=w3_codes[:, cols].bitcast(FP8X4),
-                        lhsT_scale=w3_scales[:, cols],
-                        rhs=z_codes.bitcast(FP8X4),
-                        rhs_scale=z_scales,
-                        start=(a == 0 and i == 0),
-                        stop=(a == 1 and i == per_bank - 1),
-                    )
-
-        def multiply_y1(c, a, g, z_codes, z_scales):
-            width = WIDTHS[c]
-            if a == 0:
-                sums[c, 2 * g + 1] = bank(BANKS[c][2 * g + 1], "y_acc")
-            y1 = sums[c, 2 * g + 1]
             per_bank = BANK // width
             for i in range(per_bank):
-                n = per_bank * g + i
+                codes, scales = stationary(a, per_bank * g + i)
                 nc.tensor.matmul_mx(
-                    out=y1[:, width * i : width * (i + 1)],
-                    lhsT=w2_codes[:, a, 2 * P * n : 2 * P * (n + 1)].bitcast(FP4X4),
-                    lhsT_scale=w2_scale_rows[:, a, P * n : P * (n + 1)],
+                    out=acc[:, width * i : width * (i + 1)],
+                    lhsT=codes,
+                    lhsT_scale=scales,
                     rhs=z_codes.bitcast(FP8X4),
                     rhs_scale=z_scales,
                     start=(a == 0 and i == 0),
                     stop=(a == 1 and i == per_bank - 1),
                 )
 
-        tanh_tags = ["wgs_dealt%d" % t for t in range(PACK)] + ["gate0", "h_buffer1", "gate2", "gate3"]
-        tanhs = {}
+        def w3_operand(a, n):
+            cols = slice(N * a + P * n, N * a + P * (n + 1))
+            return w3_codes[:, cols].bitcast(FP8X4), w3_scales[:, cols]
 
-        def store(c, n, result, count=2):
+        def w2_operand(a, n):
+            codes = w2_codes[:, a, 2 * P * n : 2 * P * (n + 1)].bitcast(FP4X4)
+            return codes, w2_scale_rows[:, a, P * n : P * (n + 1)]
+
+        def multiply_y2(c, a, g, z_codes, z_scales):
+            if a == 0:
+                y2_sums[c, g] = bank(BANKS[c][2 * g], "y_acc")
+            multiply_group(y2_sums[c, g], c, a, g, w3_operand, z_codes, z_scales)
+
+        def multiply_y1(c, a, g, z_codes, z_scales):
+            if a == 0:
+                y1_sums[c, g] = bank(BANKS[c][2 * g + 1], "y_acc")
+            multiply_group(y1_sums[c, g], c, a, g, w2_operand, z_codes, z_scales)
+
+        def multiply(c, a, z_codes, z_scales):
+            for g in range(N // P * WIDTHS[c] // BANK):
+                multiply_y2(c, a, g, z_codes, z_scales)
+                multiply_y1(c, a, g, z_codes, z_scales)
+
+        def store(c, n, count, result):
             nc.sync.dma_start(
                 out[P * n : P * (n + count), STARTS[c] : STARTS[c] + WIDTHS[c]].rearrange("(i p) m -> p i m", p=P),
                 result.rearrange("p (i m) -> p i m", i=count),
             )
 
-        def squash(c, groups):
-            for g in groups:
-                tile = held([P, BANK], F32, "tanh%d_%d" % (c, g), tanh_tags[N // P * STARTS[c] // BANK + g])
-                nc.scalar.activation(tile[:], sums[c, 2 * g][:], TANH)
-                tanhs[c, g] = tile
+        tanhs = {}
 
-        def finish(c, groups):
+        def squash(c, g, tile):
+            nc.scalar.activation(tile[:], y2_sums[c, g][:], TANH)
+            tanhs[c, g] = tile
+
+        def finish(c, g):
             width = WIDTHS[c]
             per_bank = BANK // width
-            for g in groups:
-                y1 = sums[c, 2 * g + 1]
-                for half in range(2):
-                    cols = slice(BANK // 2 * half, BANK // 2 * (half + 1))
-                    n = per_bank * g + per_bank // 2 * half
-                    place = N // P * STARTS[c] + width * n
-                    result = results[:, place : place + BANK // 2]
-                    nc.vector.tensor_tensor(result, y1[:, cols], tanhs[c, g][:, cols], MULT)
-                    store(c, n, result, per_bank // 2)
+            for half in range(2):
+                cols = slice(BANK // 2 * half, BANK // 2 * (half + 1))
+                n = per_bank * g + per_bank // 2 * half
+                place = N // P * STARTS[c] + width * n
+                result = results[:, place : place + BANK // 2]
+                nc.vector.tensor_tensor(result, y1_sums[c, g][:, cols], tanhs[c, g][:, cols], MULT)
+                store(c, n, per_bank // 2, result)
 
-        def first_pass(c):
-            codes, scales = z0_q[c]
-            multiply(c, 0, codes, scales)
+        def finish_on_gpsimd(c, g, tanh_y2, y1):
+            width = WIDTHS[c]
+            place = N // P * STARTS[c] + BANK * g
+            nc.scalar.activation(tanh_y2, y2_sums[c, g][:], TANH)
+            nc.scalar.copy(y1, y1_sums[c, g][:])
+            nc.gpsimd.tensor_tensor(results[:, place : place + BANK], y1, tanh_y2, MULT)
+            store(c, BANK // width * g, BANK // width, results[:, place : place + BANK])
 
         early = WIDTHS[0] + WIDTHS[1]
         rest = PAIRS - early
-        late = held([P, PACK * PAIRS], F32, "late_gates", "z0_dealt")
-        first_gates = [late[:, early * t : early * (t + 1)] for t in range(PACK)]
-        rest_gates = [late[:, PACK * early + rest * t : PACK * early + rest * (t + 1)] for t in range(PACK)]
+        late_gates = held([P, PACK * PAIRS], F32, "late_gates", "z0_dealt")
+        first_gates = [late_gates[:, early * t : early * (t + 1)] for t in range(PACK)]
+        rest_gates = [late_gates[:, PACK * early + rest * t : PACK * early + rest * (t + 1)] for t in range(PACK)]
 
-        def read_villain(t, start, stop, raw):
-            nc.vector.tensor_copy(raw, pages[PACK + t][:].indirect(list_slice(villains, start, stop)))
-
-        def open_gate(t, gate, raw):
-            nc.scalar.activation(gate, raw, SIGMOID, scale=rates[1][:, t : t + 1])
-
-        def read_pairs(start, stop, slots_read, z):
-            for i, t in enumerate(slots_read):
+        def read_chunk(c, z):
+            start, stop = STARTS[c], STARTS[c] + WIDTHS[c]
+            for t in range(PACK):
                 gate = first_gates[t][:, start:stop] if start < early else rest_gates[t][:, start - early : stop - early]
-                nc.vector.tensor_tensor(
-                    z[:, i, :], pages[PACK + t][:].indirect(list_slice(heroes, start, stop)), gate, MULT
-                )
+                read_hero(PACK + t, start, stop, gate, z[:, t, :])
 
-        def read_late(c, z, slots_read=range(PACK)):
-            read_pairs(STARTS[c], STARTS[c] + WIDTHS[c], slots_read, z)
-
-        raw = held([P, PACK, early], F32, "raw_villains0", "gate1")
+        first_villains = held([P, PACK, early], F32, "raw_villains0", "gate1")
         for t in range(PACK):
-            read_villain(t, 0, early, raw[:, t, :])
-            open_gate(t, first_gates[t], raw[:, t, :])
+            read_villain(PACK + t, 0, early, first_villains[:, t, :])
+            open_gate(PACK + t, first_gates[t], first_villains[:, t, :])
         z0_codes, z0_scales = quantise(z0_staged[:, 0:HALF, :], "z0_a")
         z0_q = {}
-        for c in range(2):
+        for c in (0, 1, 4):
             cols = slice(STARTS[c], STARTS[c] + WIDTHS[c])
             z0_q[c] = (z0_codes[:, cols], z0_scales[:, cols])
 
@@ -361,91 +353,74 @@ def tile_list_hero_villain_reads_kernel(
             codes, scales = quantise(z0_staged[:, STARTS[c] : STARTS[c] + WIDTHS[c], :], "z0_%d" % c, tag, scales_tag)
             z0_q[c] = (codes[:], scales[:])
 
-        first_pass(0)
-        first_pass(1)
-
-        staging_tags = ("w1_raw0", "w1_staged0", "w1_raw128", "w1_raw256", "w1_staged128")
-
-        def stage(c, z):
-            staged = held([P, WIDTHS[c], PACK], BF16, "z1_staged%d" % c, staging_tags[c])
+        def stage(c, z, tag):
+            staged = held([P, WIDTHS[c], PACK], BF16, "z1_staged%d" % c, tag)
             interleave(staged[:], z)
             return staged
 
-        def stage_low(c, z):
-            staged = held([P, WIDTHS[c], PACK], BF16, "z1_staged%d" % c, staging_tags[c])
-            interleave(staged[:, :, 0:2], z)
-            return staged
-
-        def second_pass(c, staged):
+        def quantise_z1(c, staged):
             codes, scales = quantise(staged[:], "z1_q%d" % c)
-            multiply(c, 1, codes[:], scales[:])
+            return codes[:], scales[:]
 
+        multiply(0, 0, *z0_q[0])
+        multiply(1, 0, *z0_q[1])
         results = held([P, N // P * PAIRS], F32, "results", "table_words")
-
-        def finish_on_gpsimd(c, g, tanh_y2, y1):
-            width = WIDTHS[c]
-            place = N // P * STARTS[c] + BANK * g
-            nc.scalar.activation(tanh_y2, sums[c, 2 * g][:], TANH)
-            nc.scalar.copy(y1, sums[c, 2 * g + 1][:])
-            nc.gpsimd.tensor_tensor(results[:, place : place + BANK], y1, tanh_y2, MULT)
-            for two in range(BANK // width // 2):
-                at = place + 2 * width * two
-                store(c, BANK // width * g + 2 * two, results[:, at : at + 2 * width])
 
         z_chunk0 = held([P, PACK, WIDTHS[0]], F32, "z1_0", "h_buffer0")
         z_chunk1 = held([P, PACK, WIDTHS[1]], F32, "z1_1", "gate1")
-        read_late(0, z_chunk0[:])
-        read_late(1, z_chunk1[:])
-        second_pass(0, stage(0, z_chunk0[:]))
-        staged1 = stage(1, z_chunk1[:])
+        read_chunk(0, z_chunk0[:])
+        read_chunk(1, z_chunk1[:])
+        multiply(0, 1, *quantise_z1(0, stage(0, z_chunk0[:], "w1_raw0")))
+        staged1 = stage(1, z_chunk1[:], "w1_staged0")
         quantise_z0(2, "h_buffer0", None)
-        second_pass(1, staged1)
-        at = PACK * early + rest - BANK // 2
-        finish_on_gpsimd(0, 0, late[:, at : at + BANK], late[:, at + 2 * rest : at + 2 * rest + BANK])
-        finish_on_gpsimd(
-            0, 1, held([P, BANK], F32, "tanh0_b", "wgs_dealt0")[:], held([P, BANK], F32, "y1_0b", "wgs_dealt2")[:]
-        )
-        finish_on_gpsimd(
-            1, 0, held([P, BANK], F32, "tanh1", "wgs_dealt1")[:], held([P, BANK], F32, "y1_1", "h_buffer2")[:]
-        )
-        first_pass(2)
-        raw = held([P, PACK, rest], F32, "raw_villains1", "gate1")
-        for t in range(PACK):
-            read_villain(t, early, PAIRS, raw[:, t, :])
-        for t in range(PACK):
-            open_gate(t, rest_gates[t], raw[:, t, :])
+        multiply(1, 1, *quantise_z1(1, staged1))
 
-        z_chunk2 = held([P, PACK, WIDTHS[2]], F32, "z1_2", "wgs_dealt1")
+        across = PACK * early + rest - BANK // 2
+        finish_on_gpsimd(
+            0, 0, late_gates[:, across : across + BANK], late_gates[:, across + 2 * rest : across + 2 * rest + BANK]
+        )
+        finish_on_gpsimd(0, 1, placed([P, BANK], "tanh0_b", 0)[:], placed([P, BANK], "y1_0b", 2)[:])
+        finish_on_gpsimd(1, 0, placed([P, BANK], "tanh1", 1)[:], held([P, BANK], F32, "y1_1", "h_buffer2")[:])
+        multiply(2, 0, *z0_q[2])
+        rest_villains = held([P, PACK, rest], F32, "raw_villains1", "gate1")
+        for t in range(PACK):
+            read_villain(PACK + t, early, PAIRS, rest_villains[:, t, :])
+        for t in range(PACK):
+            open_gate(PACK + t, rest_gates[t], rest_villains[:, t, :])
+
+        z_chunk2 = placed([P, PACK, WIDTHS[2]], "z1_2", 1)
         z_chunk3 = held([P, PACK, WIDTHS[3]], F32, "z1_3", "gate1")
-        read_late(2, z_chunk2[:])
+        read_chunk(2, z_chunk2[:])
         quantise_z0(3, None, "rates1")
-        first_pass(3)
-        read_late(3, z_chunk3[:])
-        staged2 = stage(2, z_chunk2[:])
-        staged3 = stage(3, z_chunk3[:])
-        second_pass(2, staged2)
-        squash(2, [0])
-        z_chunk4 = held([P, PACK, WIDTHS[4]], F32, "z1_4", "wgs_dealt1")
-        read_late(4, z_chunk4[:])
-        squash(2, [1])
-        codes3, scales3 = quantise(staged3[:], "z1_q3")
+        multiply(3, 0, *z0_q[3])
+        read_chunk(3, z_chunk3[:])
+        staged2 = stage(2, z_chunk2[:], "w1_raw128")
+        staged3 = stage(3, z_chunk3[:], "w1_raw256")
+        multiply(2, 1, *quantise_z1(2, staged2))
+        squash(2, 0, held([P, BANK], F32, "tanh2_0", "gate0"))
+        z_chunk4 = placed([P, PACK, WIDTHS[4]], "z1_4", 1)
+        read_chunk(4, z_chunk4[:])
+        squash(2, 1, held([P, BANK], F32, "tanh2_1", "h_buffer1"))
+
+        z1_q3 = quantise_z1(3, staged3)
         for g in range(2):
-            multiply_y2(3, 1, g, codes3[:], scales3[:])
+            multiply_y2(3, 1, g, *z1_q3)
         staged4 = held([P, WIDTHS[4], PACK], BF16, "z1_staged4", "gate1")
         nc.vector.tensor_copy(
             staged4[:].rearrange("p (c i) t -> p c t i", i=4), z_chunk4[:].rearrange("p t (c i) -> p c t i", i=4)
         )
-        last = slice(STARTS[4], HALF)
-        multiply_y2(4, 0, 0, z0_codes[:, last], z0_scales[:, last])
-        multiply_y1(3, 1, 0, codes3[:], scales3[:])
-        finish(2, [0])
-        codes4, scales4 = quantise(staged4[:], "z1_q4")
-        multiply_y2(4, 1, 0, codes4[:], scales4[:])
-        multiply_y1(3, 1, 1, codes3[:], scales3[:])
-        multiply_y1(4, 0, 0, z0_codes[:, last], z0_scales[:, last])
-        multiply_y1(4, 1, 0, codes4[:], scales4[:])
-        finish(2, [1])
-        squash(3, [0, 1])
-        finish(3, [0, 1])
-        squash(4, [0])
-        finish(4, [0])
+        multiply_y2(4, 0, 0, *z0_q[4])
+        multiply_y1(3, 1, 0, *z1_q3)
+        finish(2, 0)
+        z1_q4 = quantise_z1(4, staged4)
+        multiply_y2(4, 1, 0, *z1_q4)
+        multiply_y1(3, 1, 1, *z1_q3)
+        multiply_y1(4, 0, 0, *z0_q[4])
+        multiply_y1(4, 1, 0, *z1_q4)
+        finish(2, 1)
+        squash(3, 0, held([P, BANK], F32, "tanh3_0", "gate2"))
+        squash(3, 1, held([P, BANK], F32, "tanh3_1", "gate3"))
+        finish(3, 0)
+        finish(3, 1)
+        squash(4, 0, placed([P, BANK], "tanh4_0", 3))
+        finish(4, 0)

@@ -71,8 +71,8 @@ def tile_list_hero_villain_reads_kernel(
             return tile
 
         def load_w1(start, stop):
-            raw = held([P, PACK, stop - start], F32, "w1_raw%d" % start)
-            nc.sync.dma_start(raw[:], w1[:, start:stop].rearrange("(p j) c -> p j c", j=PACK))
+            raw = held([P, PACK, stop - start], F32, "w1_raw%d" % start)[:]
+            nc.sync.dma_start(raw, w1[:, start:stop].rearrange("(p j) c -> p j c", j=PACK))
             return raw
 
         def load_dealt_weights(first, count):
@@ -105,15 +105,14 @@ def tile_list_hero_villain_reads_kernel(
 
         w1_q = {}
 
-        def prepare_w1(raws, start, stop):
+        def prepare_w1(raw, start, stop):
             staged = held([P, stop - start, PACK], BF16, "w1_staged%d" % start)
             if start < PASS:
-                for i, raw in enumerate(raws):
-                    interleave(staged[:, P * i : P * (i + 1), :], raw[:])
+                interleave(staged[:], raw)
             else:
                 nc.scalar.copy(
                     staged[:].rearrange("p (t m) j -> p m t j", t=PACK),
-                    raws[0][:].rearrange("p j (m t) -> p m t j", t=PACK),
+                    raw.rearrange("p j (m t) -> p m t j", t=PACK),
                 )
             codes, scales = quantise(staged[:], "w1_%d" % start)
             for u in range(start // P, stop // P):
@@ -143,56 +142,58 @@ def tile_list_hero_villain_reads_kernel(
         nc.sync.dma_start(pages[0][:, 0:AHEAD], page0[0:P, 0:AHEAD])
         picked = [pick_scales(0)]
         move_scales(0, picked[0])
-        prepare_w1([w1_tile0], 0, P)
+        prepare_w1(w1_tile0, 0, P)
         picked.append(pick_scales(1))
         nc.sync.dma_start(pages[0][:, AHEAD:T2], page0[0:P, AHEAD:T2])
-        move_scales(1, picked[1])
         w1_tile1 = load_w1(P, 2 * P)
-        w1_tile2 = load_w1(2 * P, 3 * P)
+        move_scales(1, picked[1])
         nc.sync.dma_start(plain_weights[:, FIRST:S], wgs[:, FIRST:S])
-        w1_tile3 = load_w1(3 * P, PASS)
+        w1_tiles23 = load_w1(2 * P, PASS)
         v_words = held([P, S], U32, "v_words")
         for start, stop in ((0, FIRST), (FIRST, S)):
             nc.vector.tensor_copy(v_words[:, start:stop], table_words[:].indirect(list_slice(picks, start, stop)))
 
-        h_rows = {}
-        h_products = []
+
+        def multiply_h(u, start, stop, index):
+            codes, scales = w1_q[u]
+            c, at = divmod(start, HALF)
+            acc = bank(index, "h_acc")
+            nc.tensor.matmul_mx(
+                out=acc[:, 0 : stop - start],
+                lhsT=codes.bitcast(FP8X4),
+                lhsT_scale=scales,
+                rhs=v_words[:, start:stop].bitcast(FP8X4),
+                rhs_scale=v_scales[c][:, at : at + stop - start],
+                start=True,
+                stop=True,
+            )
+            return acc
 
         def make_h(u, tag):
-            codes, scales = w1_q[u]
-            h_rows[u] = held([P, S], F32, "h%d" % u, tag)
-            pieces = ((0, QUARTER), (QUARTER, FIRST), (FIRST, HALF), (HALF, S)) if u == 0 else ((0, HALF), (HALF, S))
-            for start, stop in pieces:
-                c, at = divmod(start, HALF)
-                acc = bank(len(h_products) % H_BANKS, "h_acc")
-                h_products.append(acc)
-                nc.tensor.matmul_mx(
-                    out=acc[:, 0 : stop - start],
-                    lhsT=codes.bitcast(FP8X4),
-                    lhsT_scale=scales,
-                    rhs=v_words[:, start:stop].bitcast(FP8X4),
-                    rhs_scale=v_scales[c][:, at : at + stop - start],
-                    start=True,
-                    stop=True,
-                )
-                nc.scalar.copy(h_rows[u][:, start:stop], acc[:, 0 : stop - start])
+            rows = held([P, S], F32, "h%d" % u, tag)
+            for c in range(2):
+                acc = multiply_h(u, HALF * c, HALF * (c + 1), (2 * u + 1 + c) % H_BANKS)
+                nc.scalar.copy(rows[:, HALF * c : HALF * (c + 1)], acc[:])
+            return rows[:]
 
-        def scatter(u, start, stop, weights):
+        def scatter(u, start, stop, h, weights):
             nc.vector.tensor_tensor(
                 pages[u][:].indirect(list_slice(slots, start, stop)),
-                h_rows[u][:, start:stop],
+                h,
                 weights[:, start:stop],
                 MULT,
             )
 
-        make_h(0, "h_buffer0")
-        scatter(0, 0, FIRST, plain_weights)
-        prepare_w1([w1_tile1], P, 2 * P)
-        scatter(0, FIRST, S, plain_weights)
-        prepare_w1([w1_tile2, w1_tile3], 2 * P, PASS)
+        first_h = held([P, S], F32, "h0", "h_buffer0")
+        for index, (start, stop) in enumerate(((0, QUARTER), (QUARTER, FIRST), (FIRST, HALF), (HALF, S))):
+            nc.scalar.copy(first_h[:, start:stop], multiply_h(0, start, stop, index)[:, 0 : stop - start])
+        scatter(0, 0, FIRST, first_h[:, 0:FIRST], plain_weights)
+        prepare_w1(w1_tile1, P, 2 * P)
+        scatter(0, FIRST, S, first_h[:, FIRST:S], plain_weights)
+        prepare_w1(w1_tiles23, 2 * P, PASS)
 
         pages.append(load_page(1))
-        prepare_w1([load_w1(PASS, H)], PASS, H)
+        prepare_w1(load_w1(PASS, H), PASS, H)
         for u in range(2, PACK):
             pages.append(load_page(u))
         w3_raw = held([P, 2, PACK, N], F32, "w3_raw", "table_words")
@@ -220,8 +221,8 @@ def tile_list_hero_villain_reads_kernel(
             )
 
         for u in range(1, PACK + 1):
-            make_h(u, "h_buffer%d" % (u % H_BUFFERS))
-            scatter(u, 0, S, plain_weights if u < PACK else dealt_weights[0])
+            h = make_h(u, "h_buffer%d" % (u % H_BUFFERS))
+            scatter(u, 0, S, h, plain_weights if u < PACK else dealt_weights[0])
 
         def read_villain(u, start, stop, raw):
             nc.vector.tensor_copy(raw, pages[u][:].indirect(list_slice(villains, start, stop)))
@@ -245,8 +246,8 @@ def tile_list_hero_villain_reads_kernel(
                 nc.sync.dma_start(z0_dealt[32 * u : 32 * (u + 1), t, :], z0_plain[t:P:PACK, u, :])
 
         for u in range(PACK + 1, TILES):
-            make_h(u, "gate%d" % (u - PACK - 1))
-            scatter(u, 0, S, dealt_weights[u - PACK])
+            h = make_h(u, "gate%d" % (u - PACK - 1))
+            scatter(u, 0, S, h, dealt_weights[u - PACK])
         w3_staged = held([P, 2, N, PACK], BF16, "w3_staged", "w1_raw%d" % PASS)
         for a in range(2):
             interleave(w3_staged[:, a], w3_raw[:, a])
@@ -325,7 +326,9 @@ def tile_list_hero_villain_reads_kernel(
             nc.scalar.activation(tanh_y2, y2_sums[c, g][:], TANH)
             nc.scalar.copy(y1, y1_sums[c, g][:])
             nc.gpsimd.tensor_tensor(results[:, place : place + BANK], y1, tanh_y2, MULT)
-            store(c, BANK // width * g, BANK // width, results[:, place : place + BANK])
+            for two in range(BANK // width // 2):
+                start = place + 2 * width * two
+                store(c, BANK // width * g + 2 * two, 2, results[:, start : start + 2 * width])
 
         early = WIDTHS[0] + WIDTHS[1]
         rest = PAIRS - early

@@ -207,6 +207,8 @@ def tile_list_hero_villain_reads_kernel(
         with nc.allow_non_contiguous_dma(reason="one rate a partition"):
             nc.sync.dma_start(rates[0][:], rate[0:PASS].rearrange("(u p) -> p u", p=P))
         nc.sync.dma_start(rates[1][:], rate[PASS:H].rearrange("(p t) -> p t", t=PACK))
+        first_rates = held([P, PACK], F32, "first_rates")
+        nc.sync.dma_start(first_rates[:], rate[PASS:H].rearrange("(p t) -> p t", t=PACK))
         for u in range(PACK + 1, TILES):
             pages.append(load_page(u))
         heroes = load_list(offs3, "heroes")
@@ -227,9 +229,8 @@ def tile_list_hero_villain_reads_kernel(
         def read_villain(u, start, stop, raw):
             nc.vector.tensor_copy(raw, pages[u][:].indirect(list_slice(villains, start, stop)))
 
-        def open_gate(u, gate, raw):
-            a, t = divmod(u, PACK)
-            nc.scalar.activation(gate, raw, SIGMOID, scale=rates[a][:, t : t + 1])
+        def open_gate(gate, raw, rate_column):
+            nc.scalar.activation(gate, raw, SIGMOID, scale=rate_column)
 
         def read_hero(u, start, stop, gate, z):
             nc.vector.tensor_tensor(z, pages[u][:].indirect(list_slice(heroes, start, stop)), gate, MULT)
@@ -237,7 +238,7 @@ def tile_list_hero_villain_reads_kernel(
         gates = [held([P, PAIRS], F32, "gate%d" % u) for u in range(PACK)]
         for u in range(PACK):
             read_villain(u, 0, PAIRS, gates[u][:])
-            open_gate(u, gates[u][:], gates[u][:])
+            open_gate(gates[u][:], gates[u][:], rates[0][:, u : u + 1])
         z0_plain = held([P, PACK, PAIRS], F32, "z0_plain")
         z0_dealt = held([P, PACK, PAIRS], F32, "z0_dealt")
         for u in range(PACK):
@@ -251,7 +252,7 @@ def tile_list_hero_villain_reads_kernel(
         w3_staged = held([P, 2, N, PACK], BF16, "w3_staged", "w1_raw%d" % PASS)
         for a in range(2):
             interleave(w3_staged[:, a], w3_raw[:, a])
-        w3_codes, w3_scales = quantise(w3_staged[:].rearrange("p a n t -> p (a n) t"), "w3")
+        w3_q = [quantise(w3_staged[:, 0], "w3_0")]
         z0_staged = held([P, PAIRS, PACK], BF16, "z0_staged")
         for start in reversed(range(0, PAIRS, QUARTER)):
             interleave(z0_staged[:, start : start + QUARTER, :], z0_dealt[:, :, start : start + QUARTER])
@@ -275,8 +276,9 @@ def tile_list_hero_villain_reads_kernel(
                 )
 
         def w3_operand(a, n):
-            cols = slice(N * a + P * n, N * a + P * (n + 1))
-            return w3_codes[:, cols].bitcast(FP8X4), w3_scales[:, cols]
+            codes, scales = w3_q[a]
+            cols = slice(P * n, P * (n + 1))
+            return codes[:, cols].bitcast(FP8X4), scales[:, cols]
 
         def w2_operand(a, n):
             codes = w2_codes[:, a, 2 * P * n : 2 * P * (n + 1)].bitcast(FP4X4)
@@ -326,9 +328,7 @@ def tile_list_hero_villain_reads_kernel(
             nc.scalar.activation(tanh_y2, y2_sums[c, g][:], TANH)
             nc.scalar.copy(y1, y1_sums[c, g][:])
             nc.gpsimd.tensor_tensor(results[:, place : place + BANK], y1, tanh_y2, MULT)
-            for two in range(BANK // width // 2):
-                start = place + 2 * width * two
-                store(c, BANK // width * g + 2 * two, 2, results[:, start : start + 2 * width])
+            store(c, BANK // width * g, BANK // width, results[:, place : place + BANK])
 
         early = WIDTHS[0] + WIDTHS[1]
         rest = PAIRS - early
@@ -345,7 +345,7 @@ def tile_list_hero_villain_reads_kernel(
         first_villains = held([P, PACK, early], F32, "raw_villains0", "gate1")
         for t in range(PACK):
             read_villain(PACK + t, 0, early, first_villains[:, t, :])
-            open_gate(PACK + t, first_gates[t], first_villains[:, t, :])
+            open_gate(first_gates[t], first_villains[:, t, :], first_rates[:, t : t + 1])
         z0_codes, z0_scales = quantise(z0_staged[:, 0:HALF, :], "z0_a")
         z0_q = {}
         for c in (0, 1, 4):
@@ -373,6 +373,7 @@ def tile_list_hero_villain_reads_kernel(
         z_chunk1 = held([P, PACK, WIDTHS[1]], F32, "z1_1", "gate1")
         read_chunk(0, z_chunk0[:])
         read_chunk(1, z_chunk1[:])
+        w3_q.append(quantise(w3_staged[:, 1], "w3_1", None, "first_rates"))
         multiply(0, 1, *quantise_z1(0, stage(0, z_chunk0[:], "w1_raw0")))
         staged1 = stage(1, z_chunk1[:], "w1_staged0")
         quantise_z0(2, "h_buffer0", None)
@@ -389,7 +390,7 @@ def tile_list_hero_villain_reads_kernel(
         for t in range(PACK):
             read_villain(PACK + t, early, PAIRS, rest_villains[:, t, :])
         for t in range(PACK):
-            open_gate(PACK + t, rest_gates[t], rest_villains[:, t, :])
+            open_gate(rest_gates[t], rest_villains[:, t, :], rates[1][:, t : t + 1])
 
         z_chunk2 = placed([P, PACK, WIDTHS[2]], "z1_2", 1)
         z_chunk3 = held([P, PACK, WIDTHS[3]], F32, "z1_3", "gate1")

@@ -14,6 +14,7 @@ U8 = mybir.dt.uint8
 FP8X4 = mybir.dt.float8_e4m3fn_x4
 FP4X4 = mybir.dt.float4_e2m1fn_x4
 MULT = mybir.AluOpType.mult
+ADD = mybir.AluOpType.add
 SIGMOID = mybir.ActivationFunctionType.Sigmoid
 TANH = mybir.ActivationFunctionType.Tanh
 
@@ -409,19 +410,24 @@ def tile_list_hero_villain_reads_kernel(
         z1_q3 = quantise_z1(3, staged3)
         for g in range(2):
             multiply_y2(3, 1, g, *z1_q3)
-        staged4 = held([P, WIDTHS[4], PACK], BF16, "z1_staged4", "gate1")
-        nc.vector.tensor_copy(
-            staged4[:].rearrange("p (c i) t -> p c t i", i=4), z_chunk4[:].rearrange("p t (c i) -> p c t i", i=4)
+        staged4 = held([P, WIDTHS[4], PACK], BF16, "z1_staged4", "w1_raw256")
+        nc.gpsimd.tensor_scalar(
+            staged4[:],
+            z_chunk4[:].rearrange("p t m -> p m t"),
+            1.0,
+            0.0,
+            MULT,
+            ADD,
         )
         multiply_y2(4, 0, 0, *z0_q[4])
         multiply_y1(3, 1, 0, *z1_q3)
         finish(2, 0)
+        finish(2, 1)
         z1_q4 = quantise_z1(4, staged4)
         multiply_y2(4, 1, 0, *z1_q4)
         multiply_y1(3, 1, 1, *z1_q3)
         multiply_y1(4, 0, 0, *z0_q[4])
         multiply_y1(4, 1, 0, *z1_q4)
-        finish(2, 1)
         squash(3, 0, held([P, BANK], F32, "tanh3_0", "gate2"))
         squash(3, 1, held([P, BANK], F32, "tanh3_1", "gate3"))
         finish(3, 0)

@@ -14,7 +14,6 @@ U8 = mybir.dt.uint8
 FP8X4 = mybir.dt.float8_e4m3fn_x4
 FP4X4 = mybir.dt.float4_e2m1fn_x4
 MULT = mybir.AluOpType.mult
-ADD = mybir.AluOpType.add
 SIGMOID = mybir.ActivationFunctionType.Sigmoid
 TANH = mybir.ActivationFunctionType.Tanh
 
@@ -30,9 +29,10 @@ LEAD = T // 4
 AHEAD = T2 // 4
 H_BANKS = 4
 H_BUFFERS = 3
-WIDTHS = (256, 128, 256, 256, 128)
-STARTS = (0, 256, 512, 768, 384)
-BANKS = ((4, 5, 6, 7), (0, 1), (4, 5, 6, 7), (2, 3, 0, 1), (4, 6))
+WIDTHS = (256, 256, 256, 128, 128)
+STARTS = (0, 256, 512, 768, 896)
+BANKS = ((4, 5, 6, 7), (0, 1, 2, 3), (4, 5, 6, 7), (0, 1), (2, 3))
+GATES, Z_PLAIN, Z_DEALT, WEIGHTS, H_ROWS = 0, 16, 32, 48, 64
 
 
 def list_slice(offsets, start, stop):
@@ -46,14 +46,14 @@ def tile_list_hero_villain_reads_kernel(
     with ExitStack() as ctx:
         lists = ctx.enter_context(tc.tile_pool(name="lists", bufs=1))
         keep = ctx.enter_context(tc.tile_pool(name="keep", bufs=1))
-        reuse = ctx.enter_context(tc.tile_pool(name="reuse", bufs=1))
+        shared = ctx.enter_context(tc.tile_pool(name="shared", bufs=1))
         psum = ctx.enter_context(tc.psum_pool(name="psum", bufs=1))
 
         def held(shape, dtype, name, tag=None):
             return keep.tile(shape, dtype, name=name, tag=tag or name, align_bytes=64)
 
-        def placed(shape, name, place):
-            return reuse.tile(shape, F32, name=name, tag=name, align_bytes=64, offset=4 * S * place)
+        def placed(shape, dtype, name, place):
+            return shared.tile(shape, dtype, name=name, tag=name, align_bytes=64, offset=1024 * place)
 
         def bank(index, name):
             return psum.tile([P, BANK], F32, name=name, tag="bank%d" % index)
@@ -77,7 +77,7 @@ def tile_list_hero_villain_reads_kernel(
             return raw
 
         def load_dealt_weights(first, count):
-            tile = placed([P, count * S], "wgs_rows%d" % first, first)
+            tile = placed([P, count * S], F32, "wgs_rows%d" % first, WEIGHTS + 4 * first)
             rows = wgs.rearrange("(q t) j -> q (t j)", t=PACK)[:, S * first : S * (first + count)]
             for q in (0, 2, 1, 3):
                 nc.sync.dma_start(tile[32 * q : 32 * (q + 1), :], rows)
@@ -95,10 +95,13 @@ def tile_list_hero_villain_reads_kernel(
         def interleave(staged, rows):
             nc.scalar.copy(staged.rearrange("p (c i) t -> p c t i", i=4), rows.rearrange("p t (c i) -> p c t i", i=4))
 
-        def quantise(staged, name, tag=None, scales_tag=None):
+        def quantise(staged, name, place=None):
             width = staged.shape[1]
-            codes = held([P, width], U32, name + "_codes", tag)
-            scales = held([P, width], U8, name + "_scales", scales_tag)
+            if place is None:
+                codes = held([P, width], U32, name + "_codes")
+            else:
+                codes = placed([P, width], U32, name + "_codes", place)
+            scales = held([P, width], U8, name + "_scales")
             nc.vector.quantize_mx(
                 out=codes[:].bitcast(FP8X4), scales=scales[:], in_=staged.rearrange("p m t -> p (m t)")
             )
@@ -170,8 +173,8 @@ def tile_list_hero_villain_reads_kernel(
             )
             return acc
 
-        def make_h(u, tag):
-            rows = held([P, S], F32, "h%d" % u, tag)
+        def make_h(u, place):
+            rows = placed([P, S], F32, "h%d" % u, place)
             for c in range(2):
                 acc = multiply_h(u, HALF * c, HALF * (c + 1), (2 * u + 1 + c) % H_BANKS)
                 nc.scalar.copy(rows[:, HALF * c : HALF * (c + 1)], acc[:])
@@ -185,7 +188,7 @@ def tile_list_hero_villain_reads_kernel(
                 MULT,
             )
 
-        first_h = held([P, S], F32, "h0", "h_buffer0")
+        first_h = placed([P, S], F32, "h0", H_ROWS)
         for index, (start, stop) in enumerate(((0, QUARTER), (QUARTER, FIRST), (FIRST, HALF), (HALF, S))):
             nc.scalar.copy(first_h[:, start:stop], multiply_h(0, start, stop, index)[:, 0 : stop - start])
         scatter(0, 0, FIRST, first_h[:, 0:FIRST], plain_weights)
@@ -208,8 +211,6 @@ def tile_list_hero_villain_reads_kernel(
         with nc.allow_non_contiguous_dma(reason="one rate a partition"):
             nc.sync.dma_start(rates[0][:], rate[0:PASS].rearrange("(u p) -> p u", p=P))
         nc.sync.dma_start(rates[1][:], rate[PASS:H].rearrange("(p t) -> p t", t=PACK))
-        first_rates = held([P, PACK], F32, "first_rates")
-        nc.sync.dma_start(first_rates[:], rate[PASS:H].rearrange("(p t) -> p t", t=PACK))
         for u in range(PACK + 1, TILES):
             pages.append(load_page(u))
         heroes = load_list(offs3, "heroes")
@@ -224,7 +225,7 @@ def tile_list_hero_villain_reads_kernel(
             )
 
         for u in range(1, PACK + 1):
-            h = make_h(u, "h_buffer%d" % (u % H_BUFFERS))
+            h = make_h(u, H_ROWS + 4 * (u % H_BUFFERS))
             scatter(u, 0, S, h, plain_weights if u < PACK else dealt_weights[0])
 
         def read_villain(u, start, stop, raw):
@@ -236,19 +237,19 @@ def tile_list_hero_villain_reads_kernel(
         def read_hero(u, start, stop, gate, z):
             nc.vector.tensor_tensor(z, pages[u][:].indirect(list_slice(heroes, start, stop)), gate, MULT)
 
-        gates = [held([P, PAIRS], F32, "gate%d" % u) for u in range(PACK)]
+        gates = [placed([P, PAIRS], F32, "gate%d" % u, GATES + 4 * u) for u in range(PACK)]
         for u in range(PACK):
             read_villain(u, 0, PAIRS, gates[u][:])
             open_gate(gates[u][:], gates[u][:], rates[0][:, u : u + 1])
-        z0_plain = held([P, PACK, PAIRS], F32, "z0_plain")
-        z0_dealt = held([P, PACK, PAIRS], F32, "z0_dealt")
+        z0_plain = placed([P, PACK, PAIRS], F32, "z0_plain", Z_PLAIN)
+        z0_dealt = placed([P, PACK, PAIRS], F32, "z0_dealt", Z_DEALT)
         for u in range(PACK):
             read_hero(u, 0, PAIRS, gates[u][:], z0_plain[:, u, :])
             for t in range(PACK):
                 nc.sync.dma_start(z0_dealt[32 * u : 32 * (u + 1), t, :], z0_plain[t:P:PACK, u, :])
 
         for u in range(PACK + 1, TILES):
-            h = make_h(u, "gate%d" % (u - PACK - 1))
+            h = make_h(u, GATES + 4 * (u - PACK - 1))
             scatter(u, 0, S, h, dealt_weights[u - PACK])
         w3_staged = held([P, 2, N, PACK], BF16, "w3_staged", "w1_raw%d" % PASS)
         for a in range(2):
@@ -306,131 +307,124 @@ def tile_list_hero_villain_reads_kernel(
                 result.rearrange("p (i m) -> p i m", i=count),
             )
 
-        tanhs = {}
+        def squash(c, g, place):
+            tanh_y2 = placed([P, BANK], F32, "tanh%d_%d" % (c, g), place)
+            nc.scalar.activation(tanh_y2[:], y2_sums[c, g][:], TANH)
+            return tanh_y2
 
-        def squash(c, g, tile):
-            nc.scalar.activation(tile[:], y2_sums[c, g][:], TANH)
-            tanhs[c, g] = tile
-
-        def finish(c, g):
-            width = WIDTHS[c]
-            per_bank = BANK // width
+        def finish(c, g, tanh_y2, place):
+            per_bank = BANK // WIDTHS[c]
+            result = placed([P, BANK], F32, "result%d_%d" % (c, g), place)
             for half in range(2):
                 cols = slice(BANK // 2 * half, BANK // 2 * (half + 1))
-                n = per_bank * g + per_bank // 2 * half
-                place = N // P * STARTS[c] + width * n
-                result = results[:, place : place + BANK // 2]
-                nc.vector.tensor_tensor(result, y1_sums[c, g][:, cols], tanhs[c, g][:, cols], MULT)
-                store(c, n, per_bank // 2, result)
+                nc.vector.tensor_tensor(result[:, cols], y1_sums[c, g][:, cols], tanh_y2[:, cols], MULT)
+                store(c, per_bank * g + per_bank // 2 * half, per_bank // 2, result[:, cols])
 
-        def finish_on_gpsimd(c, g, tanh_y2, y1):
-            width = WIDTHS[c]
-            place = N // P * STARTS[c] + BANK * g
-            nc.scalar.activation(tanh_y2, y2_sums[c, g][:], TANH)
-            nc.scalar.copy(y1, y1_sums[c, g][:])
-            nc.gpsimd.tensor_tensor(results[:, place : place + BANK], y1, tanh_y2, MULT)
-            store(c, BANK // width * g, BANK // width, results[:, place : place + BANK])
+        def finish_on_gpsimd(c, g, operands, place, pieces):
+            per_bank = BANK // WIDTHS[c]
+            tanh_y2 = squash(c, g, operands)
+            y1 = placed([P, BANK], F32, "y1_%d_%d" % (c, g), operands + 2)
+            nc.scalar.copy(y1[:], y1_sums[c, g][:])
+            result = placed([P, BANK], F32, "result%d_%d" % (c, g), place)
+            nc.gpsimd.tensor_tensor(result[:], y1[:], tanh_y2[:], MULT)
+            for i in range(pieces):
+                cols = slice(BANK // pieces * i, BANK // pieces * (i + 1))
+                store(c, per_bank * g + per_bank // pieces * i, per_bank // pieces, result[:, cols])
 
-        early = WIDTHS[0] + WIDTHS[1]
-        rest = PAIRS - early
-        late_gates = held([P, PACK * PAIRS], F32, "late_gates", "z0_dealt")
-        first_gates = [late_gates[:, early * t : early * (t + 1)] for t in range(PACK)]
-        rest_gates = [late_gates[:, PACK * early + rest * t : PACK * early + rest * (t + 1)] for t in range(PACK)]
-
-        def read_chunk(c, z):
-            start, stop = STARTS[c], STARTS[c] + WIDTHS[c]
+        def read_villains(start, stop, name, place):
+            raw = placed([P, PACK, stop - start], F32, name, place)
             for t in range(PACK):
-                gate = first_gates[t][:, start:stop] if start < early else rest_gates[t][:, start - early : stop - early]
-                read_hero(PACK + t, start, stop, gate, z[:, t, :])
+                read_villain(PACK + t, start, stop, raw[:, t, :])
+            return raw
 
-        first_villains = held([P, PACK, early], F32, "raw_villains0", "gate1")
-        for t in range(PACK):
-            read_villain(PACK + t, 0, early, first_villains[:, t, :])
-            open_gate(first_gates[t], first_villains[:, t, :], first_rates[:, t : t + 1])
-        z0_codes, z0_scales = quantise(z0_staged[:, 0:HALF, :], "z0_a")
-        z0_q = {}
-        for c in (0, 1, 4):
-            cols = slice(STARTS[c], STARTS[c] + WIDTHS[c])
-            z0_q[c] = (z0_codes[:, cols], z0_scales[:, cols])
+        def open_gates(raw, gates):
+            for t in range(PACK):
+                open_gate(gates[t], raw[:, t, :], rates[1][:, t : t + 1])
 
-        def quantise_z0(c, tag, scales_tag):
-            codes, scales = quantise(z0_staged[:, STARTS[c] : STARTS[c] + WIDTHS[c], :], "z0_%d" % c, tag, scales_tag)
-            z0_q[c] = (codes[:], scales[:])
+        def read_chunk(c, gates, origin, place):
+            start, stop = STARTS[c], STARTS[c] + WIDTHS[c]
+            z = placed([P, PACK, WIDTHS[c]], F32, "z1_%d" % c, place)
+            for t in range(PACK):
+                read_hero(PACK + t, start, stop, gates[t][:, start - origin : stop - origin], z[:, t, :])
+            return z
 
         def stage(c, z, tag):
             staged = held([P, WIDTHS[c], PACK], BF16, "z1_staged%d" % c, tag)
-            interleave(staged[:], z)
+            interleave(staged[:], z[:])
             return staged
 
         def quantise_z1(c, staged):
             codes, scales = quantise(staged[:], "z1_q%d" % c)
             return codes[:], scales[:]
 
-        multiply(0, 0, *z0_q[0])
-        multiply(1, 0, *z0_q[1])
-        results = held([P, N // P * PAIRS], F32, "results", "table_words")
+        def z0_operand(q, c, origin):
+            cols = slice(STARTS[c] - origin, STARTS[c] - origin + WIDTHS[c])
+            return q[0][:, cols], q[1][:, cols]
 
-        z_chunk0 = held([P, PACK, WIDTHS[0]], F32, "z1_0", "h_buffer0")
-        z_chunk1 = held([P, PACK, WIDTHS[1]], F32, "z1_1", "gate1")
-        read_chunk(0, z_chunk0[:])
-        read_chunk(1, z_chunk1[:])
-        w3_q.append(quantise(w3_staged[:, 1], "w3_1", None, "first_rates"))
-        multiply(0, 1, *quantise_z1(0, stage(0, z_chunk0[:], "w1_raw0")))
-        staged1 = stage(1, z_chunk1[:], "w1_staged0")
-        quantise_z0(2, "h_buffer0", None)
-        multiply(1, 1, *quantise_z1(1, staged1))
+        def multiply_half(acc, a, half, z_codes, z_scales):
+            width = WIDTHS[4]
+            for i in range(2):
+                codes, scales = w3_operand(a, 2 * half + i)
+                nc.tensor.matmul_mx(
+                    out=acc[:, width * i : width * (i + 1)],
+                    lhsT=codes,
+                    lhsT_scale=scales,
+                    rhs=z_codes.bitcast(FP8X4),
+                    rhs_scale=z_scales,
+                    start=(a == 0 and i == 0),
+                    stop=(a == 1 and i == 1),
+                )
+            return acc
 
-        across = PACK * early + rest - BANK // 2
-        finish_on_gpsimd(
-            0, 0, late_gates[:, across : across + BANK], late_gates[:, across + 2 * rest : across + 2 * rest + BANK]
-        )
-        finish_on_gpsimd(0, 1, placed([P, BANK], "tanh0_b", 0)[:], placed([P, BANK], "y1_0b", 2)[:])
-        finish_on_gpsimd(1, 0, placed([P, BANK], "tanh1", 1)[:], held([P, BANK], F32, "y1_1", "h_buffer2")[:])
-        multiply(2, 0, *z0_q[2])
-        rest_villains = held([P, PACK, rest], F32, "raw_villains1", "gate1")
-        for t in range(PACK):
-            read_villain(PACK + t, early, PAIRS, rest_villains[:, t, :])
-        for t in range(PACK):
-            open_gate(rest_gates[t], rest_villains[:, t, :], rates[1][:, t : t + 1])
-
-        z_chunk2 = placed([P, PACK, WIDTHS[2]], "z1_2", 1)
-        z_chunk3 = held([P, PACK, WIDTHS[3]], F32, "z1_3", "gate1")
-        read_chunk(2, z_chunk2[:])
-        quantise_z0(3, None, "rates1")
-        multiply(3, 0, *z0_q[3])
-        read_chunk(3, z_chunk3[:])
-        staged2 = stage(2, z_chunk2[:], "w1_raw128")
-        staged3 = stage(3, z_chunk3[:], "w1_raw256")
-        multiply(2, 1, *quantise_z1(2, staged2))
-        squash(2, 0, held([P, BANK], F32, "tanh2_0", "gate0"))
-        z_chunk4 = placed([P, PACK, WIDTHS[4]], "z1_4", 1)
-        read_chunk(4, z_chunk4[:])
-        squash(2, 1, held([P, BANK], F32, "tanh2_1", "h_buffer1"))
-
-        z1_q3 = quantise_z1(3, staged3)
+        raw01 = read_villains(0, HALF, "raw01", GATES)
+        gates01 = [placed([P, HALF], F32, "gates01_%d" % t, Z_DEALT + 2 * t)[:] for t in range(PACK)]
+        open_gates(raw01, gates01)
+        z0_early = quantise(z0_staged[:, 0:HALF, :], "z0_early")
+        multiply(0, 0, *z0_operand(z0_early, 0, 0))
+        multiply(1, 0, *z0_operand(z0_early, 1, 0))
+        z_0 = read_chunk(0, gates01, 0, Z_PLAIN + 2)
+        w3_q.append(quantise(w3_staged[:, 1], "w3_1", GATES))
+        z0_late = quantise(z0_staged[:, HALF:PAIRS, :], "z0_late", GATES + 2)
+        multiply(0, 1, *quantise_z1(0, stage(0, z_0, "w1_raw0")))
+        z_1 = read_chunk(1, gates01, 0, Z_PLAIN)
+        raw2 = read_villains(STARTS[2], STARTS[3], "raw2", Z_PLAIN + 4)
+        finish_on_gpsimd(0, 0, WEIGHTS, Z_DEALT + 6, 2)
+        finish_on_gpsimd(0, 1, WEIGHTS + 4, Z_DEALT + 14, 2)
+        multiply(2, 0, *z0_operand(z0_late, 2, HALF))
+        multiply(1, 1, *quantise_z1(1, stage(1, z_1, "w1_raw128")))
+        gate2 = placed([P, PACK, WIDTHS[2]], F32, "gates2", Z_PLAIN + 8)
+        gates2 = [gate2[:, t, :] for t in range(PACK)]
+        open_gates(raw2, gates2)
+        z_2 = read_chunk(2, gates2, STARTS[2], Z_DEALT + 8)
+        raw34 = read_villains(STARTS[3], PAIRS, "raw34", Z_PLAIN + 4)
+        finish_on_gpsimd(1, 0, WEIGHTS + 8, Z_PLAIN + 8, 1)
+        finish_on_gpsimd(1, 1, WEIGHTS + 12, GATES + 12, 1)
+        multiply(3, 0, *z0_operand(z0_late, 3, HALF))
+        multiply_y1(4, 0, 0, *z0_operand(z0_late, 4, HALF))
+        last_y2 = [multiply_half(bank(BANKS[4][0], "y_acc"), 0, 0, *z0_operand(z0_late, 4, HALF))]
+        q_2 = quantise_z1(2, stage(2, z_2, "w1_raw256"))
         for g in range(2):
-            multiply_y2(3, 1, g, *z1_q3)
-        staged4 = held([P, WIDTHS[4], PACK], BF16, "z1_staged4", "w1_raw256")
-        nc.gpsimd.tensor_scalar(
-            staged4[:],
-            z_chunk4[:].rearrange("p t m -> p m t"),
-            1.0,
-            0.0,
-            MULT,
-            ADD,
-        )
-        multiply_y2(4, 0, 0, *z0_q[4])
-        multiply_y1(3, 1, 0, *z1_q3)
-        finish(2, 0)
-        finish(2, 1)
-        z1_q4 = quantise_z1(4, staged4)
-        multiply_y2(4, 1, 0, *z1_q4)
-        multiply_y1(3, 1, 1, *z1_q3)
-        multiply_y1(4, 0, 0, *z0_q[4])
-        multiply_y1(4, 1, 0, *z1_q4)
-        squash(3, 0, held([P, BANK], F32, "tanh3_0", "gate2"))
-        squash(3, 1, held([P, BANK], F32, "tanh3_1", "gate3"))
-        finish(3, 0)
-        finish(3, 1)
-        squash(4, 0, placed([P, BANK], "tanh4_0", 3))
-        finish(4, 0)
+            multiply_y2(2, 1, g, *q_2)
+        for g in range(2):
+            multiply_y1(2, 1, g, *q_2)
+        gate34 = placed([P, PACK, PAIRS - STARTS[3]], F32, "gates34", Z_PLAIN + 12)
+        gates34 = [gate34[:, t, :] for t in range(PACK)]
+        open_gates(raw34, gates34)
+        z_3 = read_chunk(3, gates34, STARTS[3], Z_DEALT + 12)
+        z_4 = read_chunk(4, gates34, STARTS[3], Z_PLAIN + 4)
+        tanh2 = [squash(2, g, H_ROWS + 2 * g) for g in range(2)]
+        last_y2.append(multiply_half(bank(BANKS[2][0], "y_acc"), 0, 1, *z0_operand(z0_late, 4, HALF)))
+        staged3 = stage(3, z_3, "w1_staged0")
+        staged4 = stage(4, z_4, "w1_staged128")
+        multiply(3, 1, *quantise_z1(3, staged3))
+        finish(2, 0, tanh2[0], Z_DEALT + 12)
+        q_4 = quantise_z1(4, staged4)
+        for half in range(2):
+            multiply_half(last_y2[half], 1, half, *q_4)
+        multiply_y1(4, 1, 0, *q_4)
+        finish(2, 1, tanh2[1], Z_PLAIN + 4)
+        finish(3, 0, squash(3, 0, H_ROWS + 4), H_ROWS + 8)
+        tanh4 = placed([P, BANK], F32, "tanh4", H_ROWS + 6)
+        for half in range(2):
+            nc.scalar.activation(tanh4[:, BANK // 2 * half : BANK // 2 * (half + 1)], last_y2[half][:, 0 : BANK // 2], TANH)
+        finish(4, 0, tanh4, H_ROWS + 10)

@@ -29,9 +29,9 @@ LEAD = T // 4
 AHEAD = T2 // 4
 H_BANKS = 4
 H_BUFFERS = 3
-WIDTHS = (256, 256, 256, 128, 128)
-STARTS = (0, 256, 512, 768, 896)
-BANKS = ((4, 5, 6, 7), (0, 1, 2, 3), (4, 5, 6, 7), (0, 1), (2, 3))
+WIDTHS = (256, 128, 256, 128, 128, 128)
+STARTS = (0, 256, 512, 384, 768, 896)
+BANKS = ((4, 5, 6, 7), (0, 1), (4, 5, 6, 7), (2, 3), (0, 1), (4, 6))
 GATES, Z_PLAIN, Z_DEALT, WEIGHTS, H_ROWS = 0, 16, 32, 48, 64
 
 
@@ -312,13 +312,16 @@ def tile_list_hero_villain_reads_kernel(
             nc.scalar.activation(tanh_y2[:], y2_sums[c, g][:], TANH)
             return tanh_y2
 
-        def finish(c, g, tanh_y2, place):
+        def finish_half(c, g, half, tanh_y2, result):
             per_bank = BANK // WIDTHS[c]
+            cols = slice(BANK // 2 * half, BANK // 2 * (half + 1))
+            nc.vector.tensor_tensor(result, y1_sums[c, g][:, cols], tanh_y2[:, cols], MULT)
+            store(c, per_bank * g + per_bank // 2 * half, per_bank // 2, result)
+
+        def finish(c, g, tanh_y2, place):
             result = placed([P, BANK], F32, "result%d_%d" % (c, g), place)
             for half in range(2):
-                cols = slice(BANK // 2 * half, BANK // 2 * (half + 1))
-                nc.vector.tensor_tensor(result[:, cols], y1_sums[c, g][:, cols], tanh_y2[:, cols], MULT)
-                store(c, per_bank * g + per_bank // 2 * half, per_bank // 2, result[:, cols])
+                finish_half(c, g, half, tanh_y2, result[:, BANK // 2 * half : BANK // 2 * (half + 1)])
 
         def finish_on_gpsimd(c, g, operands, place, pieces):
             per_bank = BANK // WIDTHS[c]
@@ -362,7 +365,7 @@ def tile_list_hero_villain_reads_kernel(
             return q[0][:, cols], q[1][:, cols]
 
         def multiply_half(acc, a, half, z_codes, z_scales):
-            width = WIDTHS[4]
+            width = WIDTHS[5]
             for i in range(2):
                 codes, scales = w3_operand(a, 2 * half + i)
                 nc.tensor.matmul_mx(
@@ -376,55 +379,61 @@ def tile_list_hero_villain_reads_kernel(
                 )
             return acc
 
-        raw01 = read_villains(0, HALF, "raw01", GATES)
-        gates01 = [placed([P, HALF], F32, "gates01_%d" % t, Z_DEALT + 2 * t)[:] for t in range(PACK)]
-        open_gates(raw01, gates01)
+        early = WIDTHS[0] + WIDTHS[1]
+        raw_early = read_villains(0, early, "raw_early", GATES)
+        gate_early = placed([P, PACK, early], F32, "gates_early", Z_DEALT)
+        gates_early = [gate_early[:, t, :] for t in range(PACK)]
+        open_gates(raw_early, gates_early)
         z0_early = quantise(z0_staged[:, 0:HALF, :], "z0_early")
-        multiply(0, 0, *z0_operand(z0_early, 0, 0))
-        multiply(1, 0, *z0_operand(z0_early, 1, 0))
-        z_0 = read_chunk(0, gates01, 0, Z_PLAIN + 2)
+        for c in (0, 1, 3):
+            multiply(c, 0, *z0_operand(z0_early, c, 0))
+        z_0 = read_chunk(0, gates_early, 0, Z_PLAIN)
+        z_1 = read_chunk(1, gates_early, 0, GATES + 4)
         w3_q.append(quantise(w3_staged[:, 1], "w3_1", GATES))
-        z0_late = quantise(z0_staged[:, HALF:PAIRS, :], "z0_late", GATES + 2)
         multiply(0, 1, *quantise_z1(0, stage(0, z_0, "w1_raw0")))
-        z_1 = read_chunk(1, gates01, 0, Z_PLAIN)
-        raw2 = read_villains(STARTS[2], STARTS[3], "raw2", Z_PLAIN + 4)
-        finish_on_gpsimd(0, 0, WEIGHTS, Z_DEALT + 6, 2)
-        finish_on_gpsimd(0, 1, WEIGHTS + 4, Z_DEALT + 14, 2)
-        multiply(2, 0, *z0_operand(z0_late, 2, HALF))
-        multiply(1, 1, *quantise_z1(1, stage(1, z_1, "w1_raw128")))
-        gate2 = placed([P, PACK, WIDTHS[2]], F32, "gates2", Z_PLAIN + 8)
-        gates2 = [gate2[:, t, :] for t in range(PACK)]
-        open_gates(raw2, gates2)
-        z_2 = read_chunk(2, gates2, STARTS[2], Z_DEALT + 8)
-        raw34 = read_villains(STARTS[3], PAIRS, "raw34", Z_PLAIN + 4)
-        finish_on_gpsimd(1, 0, WEIGHTS + 8, Z_PLAIN + 8, 1)
-        finish_on_gpsimd(1, 1, WEIGHTS + 12, GATES + 12, 1)
-        multiply(3, 0, *z0_operand(z0_late, 3, HALF))
-        multiply_y1(4, 0, 0, *z0_operand(z0_late, 4, HALF))
-        last_y2 = [multiply_half(bank(BANKS[4][0], "y_acc"), 0, 0, *z0_operand(z0_late, 4, HALF))]
-        q_2 = quantise_z1(2, stage(2, z_2, "w1_raw256"))
+        staged1 = stage(1, z_1, "w1_staged0")
+        z0_2 = quantise(z0_staged[:, STARTS[2] : STARTS[4], :], "z0_2", Z_PLAIN)
+        multiply(1, 1, *quantise_z1(1, staged1))
+        finish_on_gpsimd(0, 0, Z_DEALT + 8, Z_PLAIN + 4, 2)
+        finish_on_gpsimd(0, 1, WEIGHTS, Z_PLAIN + 6, 1)
+        finish_on_gpsimd(1, 0, WEIGHTS + 4, Z_PLAIN + 8, 1)
+        multiply(2, 0, *z0_operand(z0_2, 2, STARTS[2]))
+        raw_late = read_villains(early, PAIRS, "raw_late", GATES + 4)
+        gate_late = placed([P, PACK, PAIRS - early], F32, "gates_late", Z_DEALT + 6)
+        gates_late = [gate_late[:, t, :] for t in range(PACK)]
+        open_gates(raw_late, gates_late)
+
+        z_2 = read_chunk(2, gates_late, early, WEIGHTS + 8)
+        z0_45 = quantise(z0_staged[:, STARTS[4] : PAIRS, :], "z0_45", GATES + 4)
+        multiply(4, 0, *z0_operand(z0_45, 4, STARTS[4]))
+        z_3 = read_chunk(3, gates_late, early, GATES + 6)
+        q_2 = quantise_z1(2, stage(2, z_2, "w1_raw128"))
         for g in range(2):
             multiply_y2(2, 1, g, *q_2)
         for g in range(2):
             multiply_y1(2, 1, g, *q_2)
-        gate34 = placed([P, PACK, PAIRS - STARTS[3]], F32, "gates34", Z_PLAIN + 12)
-        gates34 = [gate34[:, t, :] for t in range(PACK)]
-        open_gates(raw34, gates34)
-        z_3 = read_chunk(3, gates34, STARTS[3], Z_DEALT + 12)
-        z_4 = read_chunk(4, gates34, STARTS[3], Z_PLAIN + 4)
+        z_4 = read_chunk(4, gates_late, early, WEIGHTS + 8)
+        multiply(3, 1, *quantise_z1(3, stage(3, z_3, "w1_staged128")))
+        z_5 = read_chunk(5, gates_late, early, GATES + 6)
         tanh2 = [squash(2, g, H_ROWS + 2 * g) for g in range(2)]
-        last_y2.append(multiply_half(bank(BANKS[2][0], "y_acc"), 0, 1, *z0_operand(z0_late, 4, HALF)))
-        staged3 = stage(3, z_3, "w1_staged0")
-        staged4 = stage(4, z_4, "w1_staged128")
-        multiply(3, 1, *quantise_z1(3, staged3))
-        finish(2, 0, tanh2[0], Z_DEALT + 12)
-        q_4 = quantise_z1(4, staged4)
+        z0_5 = z0_operand(z0_45, 5, STARTS[4])
+        last_y2 = [multiply_half(bank(BANKS[5][0], "y_acc"), 0, 0, *z0_5)]
+        multiply_y1(5, 0, 0, *z0_5)
+        staged4 = stage(4, z_4, "w1_raw256")
+        tanh3 = squash(3, 0, H_ROWS + 4)
+        multiply(4, 1, *quantise_z1(4, staged4))
+        last_y2.append(multiply_half(bank(BANKS[3][0], "y_acc"), 0, 1, *z0_5))
+        staged5 = stage(5, z_5, "w1_staged256")
+        finish(2, 0, tanh2[0], WEIGHTS + 7)
+        finish_half(2, 1, 0, tanh2[1], placed([P, BANK // 2], F32, "result2_1a", WEIGHTS + 9)[:])
+        q_5 = quantise_z1(5, staged5)
         for half in range(2):
-            multiply_half(last_y2[half], 1, half, *q_4)
-        multiply_y1(4, 1, 0, *q_4)
-        finish(2, 1, tanh2[1], Z_PLAIN + 4)
-        finish(3, 0, squash(3, 0, H_ROWS + 4), H_ROWS + 8)
-        tanh4 = placed([P, BANK], F32, "tanh4", H_ROWS + 6)
+            multiply_half(last_y2[half], 1, half, *q_5)
+        multiply_y1(5, 1, 0, *q_5)
+        finish_half(2, 1, 1, tanh2[1], placed([P, BANK // 2], F32, "result2_1b", GATES + 6)[:])
+        finish(3, 0, tanh3, GATES + 7)
+        finish(4, 0, squash(4, 0, H_ROWS + 6), H_ROWS + 10)
+        tanh5 = placed([P, BANK], F32, "tanh5", H_ROWS + 8)
         for half in range(2):
-            nc.scalar.activation(tanh4[:, BANK // 2 * half : BANK // 2 * (half + 1)], last_y2[half][:, 0 : BANK // 2], TANH)
-        finish(4, 0, tanh4, H_ROWS + 10)
+            nc.scalar.activation(tanh5[:, BANK // 2 * half : BANK // 2 * (half + 1)], last_y2[half][:, 0 : BANK // 2], TANH)
+        finish(5, 0, tanh5, WEIGHTS + 12)

@@ -27,12 +27,16 @@ QUARTER = S // 4
 FIRST = 384
 LEAD = T // 4
 AHEAD = T2 // 4
+ROW0, ROW_STEP = 11, 7
 H_BANKS = 4
 H_BUFFERS = 3
 WIDTHS = (256, 128, 256, 128, 128, 128)
 STARTS = (0, 256, 512, 384, 768, 896)
+LAST = len(WIDTHS) - 1
 BANKS = ((4, 5, 6, 7), (0, 1), (4, 5, 6, 7), (2, 3), (0, 1), (4, 6))
+ROW_KIB = 4
 GATES, Z_PLAIN, Z_DEALT, WEIGHTS, H_ROWS = 0, 16, 32, 48, 64
+BANK_KIB = 2
 
 
 def list_slice(offsets, start, stop):
@@ -77,7 +81,7 @@ def tile_list_hero_villain_reads_kernel(
             return raw
 
         def load_dealt_weights(first, count):
-            tile = placed([P, count * S], F32, "wgs_rows%d" % first, WEIGHTS + 4 * first)
+            tile = placed([P, count * S], F32, "wgs_rows%d" % first, WEIGHTS + ROW_KIB * first)
             rows = wgs.rearrange("(q t) j -> q (t j)", t=PACK)[:, S * first : S * (first + count)]
             for q in (0, 2, 1, 3):
                 nc.sync.dma_start(tile[32 * q : 32 * (q + 1), :], rows)
@@ -130,7 +134,9 @@ def tile_list_hero_villain_reads_kernel(
 
         def move_scales(c, picked):
             for r in range(4):
-                nc.sync.dma_start(v_scales[c][r:P:32, :].bitcast(I32), picked[8 * r : P : 32, :].bitcast(I32))
+                first = ROW0 + ROW_STEP * r
+                rows = picked[first : first + 12 * ROW_STEP + 1 : 4 * ROW_STEP, :]
+                nc.sync.dma_start(v_scales[c][r:P:32, :].bitcast(I32), rows.bitcast(I32))
 
         w1_tile0 = load_w1(0, P)
         picks = load_list(offs, "picks")
@@ -138,7 +144,8 @@ def tile_list_hero_villain_reads_kernel(
         table_words = held([P, T], U32, "table_words")
         words = tab_words[0].rearrange("p n t -> p (n t)").bitcast(I32)
         nc.sync.dma_start(table_words[:, 0:LEAD].bitcast(I32), words[:, 0:LEAD])
-        nc.sync.dma_start(table_scales[0:P:8, :].bitcast(I32), tab_scales[0].bitcast(I32))
+        rows_end = ROW0 + 15 * ROW_STEP + 1
+        nc.sync.dma_start(table_scales[ROW0:rows_end:ROW_STEP, :].bitcast(I32), tab_scales[0].bitcast(I32))
         nc.sync.dma_start(table_words[:, LEAD:T].bitcast(I32), words[:, LEAD:T])
         plain_weights = held([P, S], F32, "wgs_plain")
         nc.sync.dma_start(plain_weights[:, 0:FIRST], wgs[:, 0:FIRST])
@@ -156,7 +163,6 @@ def tile_list_hero_villain_reads_kernel(
         v_words = held([P, S], U32, "v_words")
         for start, stop in ((0, FIRST), (FIRST, S)):
             nc.vector.tensor_copy(v_words[:, start:stop], table_words[:].indirect(list_slice(picks, start, stop)))
-
 
         def multiply_h(u, start, stop, index):
             codes, scales = w1_q[u]
@@ -225,7 +231,7 @@ def tile_list_hero_villain_reads_kernel(
             )
 
         for u in range(1, PACK + 1):
-            h = make_h(u, H_ROWS + 4 * (u % H_BUFFERS))
+            h = make_h(u, H_ROWS + ROW_KIB * (u % H_BUFFERS))
             scatter(u, 0, S, h, plain_weights if u < PACK else dealt_weights[0])
 
         def read_villain(u, start, stop, raw):
@@ -237,7 +243,7 @@ def tile_list_hero_villain_reads_kernel(
         def read_hero(u, start, stop, gate, z):
             nc.vector.tensor_tensor(z, pages[u][:].indirect(list_slice(heroes, start, stop)), gate, MULT)
 
-        gates = [placed([P, PAIRS], F32, "gate%d" % u, GATES + 4 * u) for u in range(PACK)]
+        gates = [placed([P, PAIRS], F32, "gate%d" % u, GATES + ROW_KIB * u) for u in range(PACK)]
         for u in range(PACK):
             read_villain(u, 0, PAIRS, gates[u][:])
             open_gate(gates[u][:], gates[u][:], rates[0][:, u : u + 1])
@@ -249,7 +255,7 @@ def tile_list_hero_villain_reads_kernel(
                 nc.sync.dma_start(z0_dealt[32 * u : 32 * (u + 1), t, :], z0_plain[t:P:PACK, u, :])
 
         for u in range(PACK + 1, TILES):
-            h = make_h(u, GATES + 4 * (u - PACK - 1))
+            h = make_h(u, GATES + ROW_KIB * (u - PACK - 1))
             scatter(u, 0, S, h, dealt_weights[u - PACK])
         w3_staged = held([P, 2, N, PACK], BF16, "w3_staged", "w1_raw%d" % PASS)
         for a in range(2):
@@ -326,7 +332,7 @@ def tile_list_hero_villain_reads_kernel(
         def finish_on_gpsimd(c, g, operands, place, pieces):
             per_bank = BANK // WIDTHS[c]
             tanh_y2 = squash(c, g, operands)
-            y1 = placed([P, BANK], F32, "y1_%d_%d" % (c, g), operands + 2)
+            y1 = placed([P, BANK], F32, "y1_%d_%d" % (c, g), operands + BANK_KIB)
             nc.scalar.copy(y1[:], y1_sums[c, g][:])
             result = placed([P, BANK], F32, "result%d_%d" % (c, g), place)
             nc.gpsimd.tensor_tensor(result[:], y1[:], tanh_y2[:], MULT)
@@ -340,15 +346,17 @@ def tile_list_hero_villain_reads_kernel(
                 read_villain(PACK + t, start, stop, raw[:, t, :])
             return raw
 
-        def open_gates(raw, gates):
+        def open_gates(raw, name, place):
+            opened = placed([P, PACK, raw.shape[2]], F32, name, place)
             for t in range(PACK):
-                open_gate(gates[t], raw[:, t, :], rates[1][:, t : t + 1])
+                open_gate(opened[:, t, :], raw[:, t, :], rates[1][:, t : t + 1])
+            return opened
 
-        def read_chunk(c, gates, origin, place):
+        def read_chunk(c, opened, origin, place):
             start, stop = STARTS[c], STARTS[c] + WIDTHS[c]
             z = placed([P, PACK, WIDTHS[c]], F32, "z1_%d" % c, place)
             for t in range(PACK):
-                read_hero(PACK + t, start, stop, gates[t][:, start - origin : stop - origin], z[:, t, :])
+                read_hero(PACK + t, start, stop, opened[:, t, start - origin : stop - origin], z[:, t, :])
             return z
 
         def stage(c, z, tag):
@@ -360,12 +368,13 @@ def tile_list_hero_villain_reads_kernel(
             codes, scales = quantise(staged[:], "z1_q%d" % c)
             return codes[:], scales[:]
 
-        def z0_operand(q, c, origin):
+        def z0_operand(quantised, c, origin):
+            codes, scales = quantised
             cols = slice(STARTS[c] - origin, STARTS[c] - origin + WIDTHS[c])
-            return q[0][:, cols], q[1][:, cols]
+            return codes[:, cols], scales[:, cols]
 
         def multiply_half(acc, a, half, z_codes, z_scales):
-            width = WIDTHS[5]
+            width = WIDTHS[LAST]
             for i in range(2):
                 codes, scales = w3_operand(a, 2 * half + i)
                 nc.tensor.matmul_mx(
@@ -381,59 +390,65 @@ def tile_list_hero_villain_reads_kernel(
 
         early = WIDTHS[0] + WIDTHS[1]
         raw_early = read_villains(0, early, "raw_early", GATES)
-        gate_early = placed([P, PACK, early], F32, "gates_early", Z_DEALT)
-        gates_early = [gate_early[:, t, :] for t in range(PACK)]
-        open_gates(raw_early, gates_early)
+        gates_early = open_gates(raw_early, "gates_early", Z_DEALT)
         z0_early = quantise(z0_staged[:, 0:HALF, :], "z0_early")
         for c in (0, 1, 3):
             multiply(c, 0, *z0_operand(z0_early, c, 0))
         z_0 = read_chunk(0, gates_early, 0, Z_PLAIN)
-        z_1 = read_chunk(1, gates_early, 0, GATES + 4)
+        z_1_place = GATES + 4
+        z_1 = read_chunk(1, gates_early, 0, z_1_place)
         w3_q.append(quantise(w3_staged[:, 1], "w3_1", GATES))
         multiply(0, 1, *quantise_z1(0, stage(0, z_0, "w1_raw0")))
         staged1 = stage(1, z_1, "w1_staged0")
-        z0_2 = quantise(z0_staged[:, STARTS[2] : STARTS[4], :], "z0_2", Z_PLAIN)
+        z0_2 = quantise(z0_staged[:, STARTS[2] : STARTS[2] + WIDTHS[2], :], "z0_2", Z_PLAIN)
         multiply(1, 1, *quantise_z1(1, staged1))
-        finish_on_gpsimd(0, 0, Z_DEALT + 8, Z_PLAIN + 4, 2)
-        finish_on_gpsimd(0, 1, WEIGHTS, Z_PLAIN + 6, 1)
-        finish_on_gpsimd(1, 0, WEIGHTS + 4, Z_PLAIN + 8, 1)
-        multiply(2, 0, *z0_operand(z0_2, 2, STARTS[2]))
-        raw_late = read_villains(early, PAIRS, "raw_late", GATES + 4)
-        gate_late = placed([P, PACK, PAIRS - early], F32, "gates_late", Z_DEALT + 6)
-        gates_late = [gate_late[:, t, :] for t in range(PACK)]
-        open_gates(raw_late, gates_late)
 
-        z_2 = read_chunk(2, gates_late, early, WEIGHTS + 8)
-        z0_45 = quantise(z0_staged[:, STARTS[4] : PAIRS, :], "z0_45", GATES + 4)
+        gates_late_place = Z_DEALT + 6
+        results_place = Z_PLAIN + ROW_KIB
+        finish_on_gpsimd(0, 0, gates_late_place + BANK_KIB, results_place, 2)
+        finish_on_gpsimd(0, 1, WEIGHTS, results_place + BANK_KIB, 1)
+        finish_on_gpsimd(1, 0, WEIGHTS + 2 * BANK_KIB, results_place + 2 * BANK_KIB, 1)
+        multiply(2, 0, *z0_operand(z0_2, 2, STARTS[2]))
+        raw_late = read_villains(early, PAIRS, "raw_late", z_1_place)
+        gates_late = open_gates(raw_late, "gates_late", gates_late_place)
+
+        even_place = WEIGHTS + 2 * ROW_KIB
+        odd_place = z_1_place + 2
+        z_2 = read_chunk(2, gates_late, early, even_place)
+        z0_45 = quantise(z0_staged[:, STARTS[4] : PAIRS, :], "z0_45", z_1_place)
         multiply(4, 0, *z0_operand(z0_45, 4, STARTS[4]))
-        z_3 = read_chunk(3, gates_late, early, GATES + 6)
-        q_2 = quantise_z1(2, stage(2, z_2, "w1_raw128"))
+        z_3 = read_chunk(3, gates_late, early, odd_place)
+        z1_2 = quantise_z1(2, stage(2, z_2, "w1_raw128"))
         for g in range(2):
-            multiply_y2(2, 1, g, *q_2)
+            multiply_y2(2, 1, g, *z1_2)
         for g in range(2):
-            multiply_y1(2, 1, g, *q_2)
-        z_4 = read_chunk(4, gates_late, early, WEIGHTS + 8)
+            multiply_y1(2, 1, g, *z1_2)
+        z_4 = read_chunk(4, gates_late, early, even_place)
         multiply(3, 1, *quantise_z1(3, stage(3, z_3, "w1_staged128")))
-        z_5 = read_chunk(5, gates_late, early, GATES + 6)
-        tanh2 = [squash(2, g, H_ROWS + 2 * g) for g in range(2)]
-        z0_5 = z0_operand(z0_45, 5, STARTS[4])
-        last_y2 = [multiply_half(bank(BANKS[5][0], "y_acc"), 0, 0, *z0_5)]
-        multiply_y1(5, 0, 0, *z0_5)
+        z_5 = read_chunk(LAST, gates_late, early, odd_place)
+
+        tanh_places = [H_ROWS + BANK_KIB * i for i in range(5)]
+        tanh_2 = [squash(2, g, tanh_places[g]) for g in range(2)]
+        z0_5 = z0_operand(z0_45, LAST, STARTS[4])
+        last_y2 = [multiply_half(bank(BANKS[LAST][0], "y_acc"), 0, 0, *z0_5)]
+        multiply_y1(LAST, 0, 0, *z0_5)
         staged4 = stage(4, z_4, "w1_raw256")
-        tanh3 = squash(3, 0, H_ROWS + 4)
+        tanh_3 = squash(3, 0, tanh_places[2])
         multiply(4, 1, *quantise_z1(4, staged4))
         last_y2.append(multiply_half(bank(BANKS[3][0], "y_acc"), 0, 1, *z0_5))
-        staged5 = stage(5, z_5, "w1_staged256")
-        finish(2, 0, tanh2[0], WEIGHTS + 7)
-        finish_half(2, 1, 0, tanh2[1], placed([P, BANK // 2], F32, "result2_1a", WEIGHTS + 9)[:])
-        q_5 = quantise_z1(5, staged5)
+        staged5 = stage(LAST, z_5, "w1_staged256")
+
+        finish(2, 0, tanh_2[0], even_place - 1)
+        finish_half(2, 1, 0, tanh_2[1], placed([P, BANK // 2], F32, "result2_1a", even_place + 1)[:])
+        z1_5 = quantise_z1(LAST, staged5)
         for half in range(2):
-            multiply_half(last_y2[half], 1, half, *q_5)
-        multiply_y1(5, 1, 0, *q_5)
-        finish_half(2, 1, 1, tanh2[1], placed([P, BANK // 2], F32, "result2_1b", GATES + 6)[:])
-        finish(3, 0, tanh3, GATES + 7)
-        finish(4, 0, squash(4, 0, H_ROWS + 6), H_ROWS + 10)
-        tanh5 = placed([P, BANK], F32, "tanh5", H_ROWS + 8)
+            multiply_half(last_y2[half], 1, half, *z1_5)
+        multiply_y1(LAST, 1, 0, *z1_5)
+        finish_half(2, 1, 1, tanh_2[1], placed([P, BANK // 2], F32, "result2_1b", odd_place)[:])
+        finish(3, 0, tanh_3, odd_place + 1)
+        finish(4, 0, squash(4, 0, tanh_places[3]), tanh_places[4] + BANK_KIB)
+        tanh_5 = placed([P, BANK], F32, "tanh5", tanh_places[4])
         for half in range(2):
-            nc.scalar.activation(tanh5[:, BANK // 2 * half : BANK // 2 * (half + 1)], last_y2[half][:, 0 : BANK // 2], TANH)
-        finish(5, 0, tanh5, WEIGHTS + 12)
+            cols = slice(BANK // 2 * half, BANK // 2 * (half + 1))
+            nc.scalar.activation(tanh_5[:, cols], last_y2[half][:, 0 : BANK // 2], TANH)
+        finish(LAST, 0, tanh_5, even_place + ROW_KIB)

@@ -54,10 +54,10 @@ def tile_list_hero_villain_reads_kernel(
         psum = ctx.enter_context(tc.psum_pool(name="psum", bufs=1))
 
         def held(shape, dtype, name, tag=None):
-            return keep.tile(shape, dtype, name=name, tag=tag or name, align_bytes=64)
+            return keep.tile(shape, dtype, name=name, tag=tag or name, align_bytes=256)
 
         def placed(shape, dtype, name, place):
-            return shared.tile(shape, dtype, name=name, tag=name, align_bytes=64, offset=1024 * place)
+            return shared.tile(shape, dtype, name=name, tag=name, align_bytes=256, offset=1024 * place)
 
         def bank(index, name):
             return psum.tile([P, BANK], F32, name=name, tag="bank%d" % index)

@@ -35,7 +35,7 @@ STARTS = (0, 256, 512, 384, 768, 896)
 LAST = len(WIDTHS) - 1
 BANKS = ((4, 5, 6, 7), (0, 1), (4, 5, 6, 7), (2, 3), (0, 1), (4, 6))
 ROW_KIB = 4
-GATES, Z_PLAIN, Z_DEALT, WEIGHTS, H_ROWS = 0, 16, 32, 48, 64
+Z_PLAIN, Z_DEALT, WEIGHTS, GATES, H_ROWS = 0, 16, 32, 48, 64
 BANK_KIB = 2
 
 
@@ -219,9 +219,9 @@ def tile_list_hero_villain_reads_kernel(
         nc.sync.dma_start(rates[1][:], rate[PASS:H].rearrange("(p t) -> p t", t=PACK))
         for u in range(PACK + 1, TILES):
             pages.append(load_page(u))
-        heroes = load_list(offs3, "heroes")
         dealt_weights.extend(load_dealt_weights(1, 1))
         dealt_weights.extend(load_dealt_weights(2, 2))
+        heroes = load_list(offs3, "heroes")
         w2_codes = held([P, 2, 2 * N], U8, "w2_codes")
         nc.sync.dma_start(w2_codes[:].bitcast(I32), w2_words.rearrange("a p c -> p a c").bitcast(I32))
         for q in range(4):
@@ -254,9 +254,14 @@ def tile_list_hero_villain_reads_kernel(
             for t in range(PACK):
                 nc.sync.dma_start(z0_dealt[32 * u : 32 * (u + 1), t, :], z0_plain[t:P:PACK, u, :])
 
+        early = WIDTHS[0] + WIDTHS[1]
+        early_place = GATES + 3 * ROW_KIB
+        raw_early = placed([P, PACK, early], F32, "raw_early", early_place)
         for u in range(PACK + 1, TILES):
             h = make_h(u, GATES + ROW_KIB * (u - PACK - 1))
             scatter(u, 0, S, h, dealt_weights[u - PACK])
+            read_villain(u - 1, 0, early, raw_early[:, u - 1 - PACK, :])
+        read_villain(TILES - 1, 0, early, raw_early[:, PACK - 1, :])
         w3_staged = held([P, 2, N, PACK], BF16, "w3_staged", "w1_raw%d" % PASS)
         for a in range(2):
             interleave(w3_staged[:, a], w3_raw[:, a])
@@ -388,16 +393,14 @@ def tile_list_hero_villain_reads_kernel(
                 )
             return acc
 
-        early = WIDTHS[0] + WIDTHS[1]
-        raw_early = read_villains(0, early, "raw_early", GATES)
         gates_early = open_gates(raw_early, "gates_early", Z_DEALT)
         z0_early = quantise(z0_staged[:, 0:HALF, :], "z0_early")
         for c in (0, 1, 3):
             multiply(c, 0, *z0_operand(z0_early, c, 0))
         z_0 = read_chunk(0, gates_early, 0, Z_PLAIN)
-        z_1_place = GATES + 4
+        z_1_place = early_place + 4
         z_1 = read_chunk(1, gates_early, 0, z_1_place)
-        w3_q.append(quantise(w3_staged[:, 1], "w3_1", GATES))
+        w3_q.append(quantise(w3_staged[:, 1], "w3_1", early_place))
         multiply(0, 1, *quantise_z1(0, stage(0, z_0, "w1_raw0")))
         staged1 = stage(1, z_1, "w1_staged0")
         z0_2 = quantise(z0_staged[:, STARTS[2] : STARTS[2] + WIDTHS[2], :], "z0_2", Z_PLAIN)
@@ -427,7 +430,7 @@ def tile_list_hero_villain_reads_kernel(
         multiply(3, 1, *quantise_z1(3, stage(3, z_3, "w1_staged128")))
         z_5 = read_chunk(LAST, gates_late, early, odd_place)
 
-        tanh_places = [H_ROWS + BANK_KIB * i for i in range(5)]
+        tanh_places = [GATES + BANK_KIB * i for i in range(5)]
         tanh_2 = [squash(2, g, tanh_places[g]) for g in range(2)]
         z0_5 = z0_operand(z0_45, LAST, STARTS[4])
         last_y2 = [multiply_half(bank(BANKS[LAST][0], "y_acc"), 0, 0, *z0_5)]

@@ -36,6 +36,10 @@ LAST = len(WIDTHS) - 1
 BANKS = ((4, 5, 6, 7), (0, 1), (4, 5, 6, 7), (2, 3), (0, 1), (4, 6))
 ROW_KIB = 4
 Z_PLAIN, Z_DEALT, WEIGHTS, GATES, H_ROWS = 0, 16, 32, 48, 64
+SCATTER_CUTS = (0, 256, 512, 768, 1024)
+LAST_SCATTER_CUTS = (0, 384, 768, 1024)
+VILLAIN_CUTS = (0, 512, 1024)
+HERO_CUTS = (0, 384, 768, 1024)
 BANK_KIB = 2
 
 
@@ -194,7 +198,7 @@ def tile_list_hero_villain_reads_kernel(
                 MULT,
             )
 
-        first_h = placed([P, S], F32, "h0", H_ROWS)
+        first_h = placed([P, S], F32, "h0", H_ROWS + 6)
         for index, (start, stop) in enumerate(((0, QUARTER), (QUARTER, FIRST), (FIRST, HALF), (HALF, S))):
             nc.scalar.copy(first_h[:, start:stop], multiply_h(0, start, stop, index)[:, 0 : stop - start])
         scatter(0, 0, FIRST, first_h[:, 0:FIRST], plain_weights)
@@ -202,26 +206,25 @@ def tile_list_hero_villain_reads_kernel(
         scatter(0, FIRST, S, first_h[:, FIRST:S], plain_weights)
         prepare_w1(w1_tiles23, 2 * P, PASS)
 
-        pages.append(load_page(1))
+        pages.extend([None] * (TILES - 1))
+        pages[1] = load_page(1)
         prepare_w1(load_w1(PASS, H), PASS, H)
-        for u in range(2, PACK):
-            pages.append(load_page(u))
-        w3_raw = held([P, 2, PACK, N], F32, "w3_raw", "table_words")
-        nc.sync.dma_start(
-            w3_raw[:].rearrange("p a j n -> p a (j n)"), w3.rearrange("(a p j) n -> p a (j n)", p=P, j=PACK)
-        )
-        dealt_weights = load_dealt_weights(0, 1)
-        pages.append(load_page(PACK))
-        villains = load_list(offs4, "villains")
         rates = [held([P, PACK], F32, "rates%d" % a) for a in range(2)]
         with nc.allow_non_contiguous_dma(reason="one rate a partition"):
             nc.sync.dma_start(rates[0][:], rate[0:PASS].rearrange("(u p) -> p u", p=P))
         nc.sync.dma_start(rates[1][:], rate[PASS:H].rearrange("(p t) -> p t", t=PACK))
-        for u in range(PACK + 1, TILES):
-            pages.append(load_page(u))
-        dealt_weights.extend(load_dealt_weights(1, 1))
-        dealt_weights.extend(load_dealt_weights(2, 2))
+        pages[3] = load_page(3)
+        pages[2] = load_page(2)
+        villains = load_list(offs4, "villains")
         heroes = load_list(offs3, "heroes")
+        dealt_weights = []
+        for t in range(PACK):
+            pages[PACK + t] = load_page(PACK + t)
+            dealt_weights.extend(load_dealt_weights(t, 1))
+        w3_raw = held([P, 2, PACK, N], F32, "w3_raw", "table_words")
+        nc.sync.dma_start(
+            w3_raw[:].rearrange("p a j n -> p a (j n)"), w3.rearrange("(a p j) n -> p a (j n)", p=P, j=PACK)
+        )
         w2_codes = held([P, 2, 2 * N], U8, "w2_codes")
         nc.sync.dma_start(w2_codes[:].bitcast(I32), w2_words.rearrange("a p c -> p a c").bitcast(I32))
         for q in range(4):
@@ -229,10 +232,6 @@ def tile_list_hero_villain_reads_kernel(
                 w2_scale_rows[32 * q : 32 * q + 4, :, :].bitcast(I32),
                 w2_scales[:, 4 * q : 4 * q + 4, :].rearrange("a r c -> r a c").bitcast(I32),
             )
-
-        for u in range(1, PACK + 1):
-            h = make_h(u, H_ROWS + ROW_KIB * (u % H_BUFFERS))
-            scatter(u, 0, S, h, plain_weights if u < PACK else dealt_weights[0])
 
         def read_villain(u, start, stop, raw):
             nc.vector.tensor_copy(raw, pages[u][:].indirect(list_slice(villains, start, stop)))
@@ -244,27 +243,55 @@ def tile_list_hero_villain_reads_kernel(
             nc.vector.tensor_tensor(z, pages[u][:].indirect(list_slice(heroes, start, stop)), gate, MULT)
 
         gates = [placed([P, PAIRS], F32, "gate%d" % u, GATES + ROW_KIB * u) for u in range(PACK)]
-        for u in range(PACK):
-            read_villain(u, 0, PAIRS, gates[u][:])
-            open_gate(gates[u][:], gates[u][:], rates[0][:, u : u + 1])
         z0_plain = placed([P, PACK, PAIRS], F32, "z0_plain", Z_PLAIN)
         z0_dealt = placed([P, PACK, PAIRS], F32, "z0_dealt", Z_DEALT)
-        for u in range(PACK):
-            read_hero(u, 0, PAIRS, gates[u][:], z0_plain[:, u, :])
-            for t in range(PACK):
-                nc.sync.dma_start(z0_dealt[32 * u : 32 * (u + 1), t, :], z0_plain[t:P:PACK, u, :])
-
         early = WIDTHS[0] + WIDTHS[1]
-        early_place = GATES + 3 * ROW_KIB
+        early_place = H_ROWS
         raw_early = placed([P, PACK, early], F32, "raw_early", early_place)
-        for u in range(PACK + 1, TILES):
-            h = make_h(u, GATES + ROW_KIB * (u - PACK - 1))
-            scatter(u, 0, S, h, dealt_weights[u - PACK])
-            read_villain(u - 1, 0, early, raw_early[:, u - 1 - PACK, :])
-        read_villain(TILES - 1, 0, early, raw_early[:, PACK - 1, :])
+
+        def villain_piece(u, start, stop, gate):
+            read_villain(u, start, stop, gate)
+            open_gate(gate, gate, rates[0][:, u : u + 1])
+
+        def hero_piece(u, start, stop, z):
+            read_hero(u, start, stop, gates[u][:, start:stop], z)
+            if stop == PAIRS:
+                for t in range(PACK):
+                    nc.sync.dma_start(z0_dealt[32 * u : 32 * (u + 1), t, :], z0_plain[t:P:PACK, u, :])
+
+        def pieces(read, u, cuts, row):
+            return [(read, u, start, stop, row[:, start:stop]) for start, stop in zip(cuts, cuts[1:])]
+
+        reads = []
+        for kind, u in ((0, 0), (0, 1), (1, 0), (0, 2), (1, 1), (0, 3), (1, 2), (1, 3)):
+            if kind:
+                reads.extend(pieces(hero_piece, u, HERO_CUTS, z0_plain[:, u, :]))
+            else:
+                reads.extend(pieces(villain_piece, u, VILLAIN_CUTS, gates[u][:]))
+        for u in range(PACK, TILES):
+            reads.extend(pieces(read_villain, u, (0, early), raw_early[:, u - PACK, :]))
+
+        scatter(1, 0, S, make_h(1, H_ROWS + 10), plain_weights)
+        puts = []
+        for u in range(2, TILES):
+            sums = [multiply_h(u, HALF * c, HALF * (c + 1), (2 * u + 1 + c) % H_BANKS) for c in range(2)]
+            cuts = SCATTER_CUTS if u + 1 < TILES else LAST_SCATTER_CUTS
+            for start, stop in zip(cuts, cuts[1:]):
+                h = reads[len(puts) + 1][4][:, 0 : stop - start]
+                for c in range(start // HALF, (stop - 1) // HALF + 1):
+                    first, last = max(start, HALF * c), min(stop, HALF * (c + 1))
+                    nc.scalar.copy(h[:, first - start : last - start], sums[c][:, first - HALF * c : last - HALF * c])
+                puts.append((u, start, stop, h, plain_weights if u < PACK else dealt_weights[u - PACK]))
+        for put, (read, u, start, stop, row) in zip(puts, reads):
+            scatter(*put)
+            read(u, start, stop, row)
+        read, u, start, stop, row = reads[-1]
+        read(u, start, stop, row)
         w3_staged = held([P, 2, N, PACK], BF16, "w3_staged", "w1_raw%d" % PASS)
         for a in range(2):
-            interleave(w3_staged[:, a], w3_raw[:, a])
+            for start in range(0, N, QUARTER):
+                cols = slice(start, start + QUARTER)
+                interleave(w3_staged[:, a, cols, :], w3_raw[:, a, :, cols])
         w3_q = [quantise(w3_staged[:, 0], "w3_0")]
         z0_staged = held([P, PAIRS, PACK], BF16, "z0_staged")
         for start in reversed(range(0, PAIRS, QUARTER)):

@@ -40,6 +40,7 @@ SCATTER_CUTS = (0, 256, 512, 768, 1024)
 LAST_SCATTER_CUTS = (0, 384, 768, 1024)
 VILLAIN_CUTS = (0, 512, 1024)
 HERO_CUTS = (0, 384, 768, 1024)
+TAIL = T2 // 8
 BANK_KIB = 2
 
 
@@ -91,14 +92,23 @@ def tile_list_hero_villain_reads_kernel(
                 nc.sync.dma_start(tile[32 * q : 32 * (q + 1), :], rows)
             return [tile[:, S * t : S * (t + 1)] for t in range(count)]
 
+        def page_rows(u):
+            if u < PACK:
+                return page0[P * u : P * (u + 1), :]
+            return page0[PASS:, :].rearrange("(p t) c -> t p c", t=PACK)[u - PACK]
+
         def load_page(u):
             tile = held([P, T2], F32, "page%d" % u)
-            if u < PACK:
-                rows = page0[P * u : P * (u + 1), :]
-            else:
-                rows = page0[PASS:, :].rearrange("(p t) c -> t p c", t=PACK)[u - PACK]
-            nc.sync.dma_start(tile[:], rows)
+            nc.sync.dma_start(tile[:], page_rows(u))
             return tile
+
+        def load_pair(u):
+            pages[u + 1] = held([P, T2], F32, "page%d" % (u + 1))
+            nc.sync.dma_start(pages[u + 1][:, 0 : T2 - TAIL], page_rows(u + 1)[:, 0 : T2 - TAIL])
+            pages[u] = load_page(u)
+
+        def load_tail(u):
+            nc.sync.dma_start(pages[u + 1][:, T2 - TAIL : T2], page_rows(u + 1)[:, T2 - TAIL : T2])
 
         def interleave(staged, rows):
             nc.scalar.copy(staged.rearrange("p (c i) t -> p c t i", i=4), rows.rearrange("p t (c i) -> p c t i", i=4))
@@ -213,14 +223,15 @@ def tile_list_hero_villain_reads_kernel(
         with nc.allow_non_contiguous_dma(reason="one rate a partition"):
             nc.sync.dma_start(rates[0][:], rate[0:PASS].rearrange("(u p) -> p u", p=P))
         nc.sync.dma_start(rates[1][:], rate[PASS:H].rearrange("(p t) -> p t", t=PACK))
-        pages[3] = load_page(3)
-        pages[2] = load_page(2)
+        load_pair(2)
         villains = load_list(offs4, "villains")
+        load_tail(2)
         heroes = load_list(offs3, "heroes")
         dealt_weights = []
-        for t in range(PACK):
-            pages[PACK + t] = load_page(PACK + t)
-            dealt_weights.extend(load_dealt_weights(t, 1))
+        for t in range(0, PACK, 2):
+            dealt_weights.extend(load_dealt_weights(t, 2))
+            load_pair(PACK + t)
+            load_tail(PACK + t)
         w3_raw = held([P, 2, PACK, N], F32, "w3_raw", "table_words")
         nc.sync.dma_start(
             w3_raw[:].rearrange("p a j n -> p a (j n)"), w3.rearrange("(a p j) n -> p a (j n)", p=P, j=PACK)
@@ -243,7 +254,7 @@ def tile_list_hero_villain_reads_kernel(
             nc.vector.tensor_tensor(z, pages[u][:].indirect(list_slice(heroes, start, stop)), gate, MULT)
 
         gates = [placed([P, PAIRS], F32, "gate%d" % u, GATES + ROW_KIB * u) for u in range(PACK)]
-        z0_plain = placed([P, PACK, PAIRS], F32, "z0_plain", Z_PLAIN)
+        z0_plain = [placed([P, PAIRS], F32, "z0_plain%d" % u, Z_PLAIN + ROW_KIB * u) for u in range(PACK)]
         z0_dealt = placed([P, PACK, PAIRS], F32, "z0_dealt", Z_DEALT)
         early = WIDTHS[0] + WIDTHS[1]
         early_place = H_ROWS
@@ -257,36 +268,50 @@ def tile_list_hero_villain_reads_kernel(
             read_hero(u, start, stop, gates[u][:, start:stop], z)
             if stop == PAIRS:
                 for t in range(PACK):
-                    nc.sync.dma_start(z0_dealt[32 * u : 32 * (u + 1), t, :], z0_plain[t:P:PACK, u, :])
+                    nc.sync.dma_start(z0_dealt[32 * u : 32 * (u + 1), t, :], z0_plain[u][t:P:PACK, :])
 
         def pieces(read, u, cuts, row):
             return [(read, u, start, stop, row[:, start:stop]) for start, stop in zip(cuts, cuts[1:])]
 
         reads = []
-        for kind, u in ((0, 0), (0, 1), (1, 0), (0, 2), (1, 1), (0, 3), (1, 2), (1, 3)):
+        for kind, u in ((0, 0), (0, 1), (1, 0), (1, 1), (0, 2), (0, 3), (1, 2), (1, 3)):
             if kind:
-                reads.extend(pieces(hero_piece, u, HERO_CUTS, z0_plain[:, u, :]))
+                reads.extend(pieces(hero_piece, u, HERO_CUTS, z0_plain[u][:]))
             else:
                 reads.extend(pieces(villain_piece, u, VILLAIN_CUTS, gates[u][:]))
-        for u in range(PACK, TILES):
+        for u in (4, 5, 7, 6):
             reads.extend(pieces(read_villain, u, (0, early), raw_early[:, u - PACK, :]))
 
         scatter(1, 0, S, make_h(1, H_ROWS + 10), plain_weights)
-        puts = []
-        for u in range(2, TILES):
+        plan = []
+        for u in range(2, TILES, 2):
+            first = [(u, a, b) for a, b in zip(SCATTER_CUTS, SCATTER_CUTS[1:])]
+            cuts = SCATTER_CUTS if u + 2 < TILES else LAST_SCATTER_CUTS
+            second = [(u + 1, a, b) for a, b in zip(cuts, cuts[1:])]
+            for i, piece in enumerate(first):
+                plan.append(piece)
+                plan.extend(second[i : i + 1])
+        parked = {}
+
+        def park_h(u):
             sums = [multiply_h(u, HALF * c, HALF * (c + 1), (2 * u + 1 + c) % H_BANKS) for c in range(2)]
-            cuts = SCATTER_CUTS if u + 1 < TILES else LAST_SCATTER_CUTS
-            for start, stop in zip(cuts, cuts[1:]):
-                h = reads[len(puts) + 1][4][:, 0 : stop - start]
-                for c in range(start // HALF, (stop - 1) // HALF + 1):
-                    first, last = max(start, HALF * c), min(stop, HALF * (c + 1))
-                    nc.scalar.copy(h[:, first - start : last - start], sums[c][:, first - HALF * c : last - HALF * c])
-                puts.append((u, start, stop, h, plain_weights if u < PACK else dealt_weights[u - PACK]))
-        for put, (read, u, start, stop, row) in zip(puts, reads):
-            scatter(*put)
+            for step, (tile, start, stop) in enumerate(plan):
+                if tile == u:
+                    h = reads[step + 1][4][:, 0 : stop - start]
+                    for c in range(start // HALF, (stop - 1) // HALF + 1):
+                        first, last = max(start, HALF * c), min(stop, HALF * (c + 1))
+                        nc.scalar.copy(
+                            h[:, first - start : last - start], sums[c][:, first - HALF * c : last - HALF * c]
+                        )
+                    parked[step] = h
+
+        for u in range(2, TILES):
+            park_h(u)
+        for step, (read, u, start, stop, row) in enumerate(reads):
+            if step < len(plan):
+                tile, first, last = plan[step]
+                scatter(tile, first, last, parked[step], plain_weights if tile < PACK else dealt_weights[tile - PACK])
             read(u, start, stop, row)
-        read, u, start, stop, row = reads[-1]
-        read(u, start, stop, row)
         w3_staged = held([P, 2, N, PACK], BF16, "w3_staged", "w1_raw%d" % PASS)
         for a in range(2):
             for start in range(0, N, QUARTER):
@@ -436,7 +461,7 @@ def tile_list_hero_villain_reads_kernel(
         gates_late_place = Z_DEALT + 6
         results_place = Z_PLAIN + ROW_KIB
         finish_on_gpsimd(0, 0, gates_late_place + BANK_KIB, results_place, 2)
-        finish_on_gpsimd(0, 1, WEIGHTS, results_place + BANK_KIB, 1)
+        finish_on_gpsimd(0, 1, WEIGHTS, results_place + BANK_KIB, 2)
         finish_on_gpsimd(1, 0, WEIGHTS + 2 * BANK_KIB, results_place + 2 * BANK_KIB, 1)
         multiply(2, 0, *z0_operand(z0_2, 2, STARTS[2]))
         raw_late = read_villains(early, PAIRS, "raw_late", z_1_place)

@@ -38,8 +38,8 @@ ROW_KIB = 4
 Z_PLAIN, Z_DEALT, WEIGHTS, GATES, H_ROWS = 0, 16, 32, 48, 64
 SCATTER_CUTS = (0, 256, 512, 768, 1024)
 LAST_SCATTER_CUTS = (0, 384, 768, 1024)
-VILLAIN_CUTS = (0, 512, 1024)
-HERO_CUTS = (0, 384, 768, 1024)
+VILLAIN_CUTS = (0, 256, 512, 768, 1024)
+HERO_LAG = 4
 TAIL = T2 // 8
 BANK_KIB = 2
 
@@ -258,29 +258,27 @@ def tile_list_hero_villain_reads_kernel(
         z0_dealt = placed([P, PACK, PAIRS], F32, "z0_dealt", Z_DEALT)
         early = WIDTHS[0] + WIDTHS[1]
         early_place = H_ROWS
-        raw_early = placed([P, PACK, early], F32, "raw_early", early_place)
+        raw_rows = placed([P, 8, early], F32, "raw_early", early_place)
 
         def villain_piece(u, start, stop, gate):
             read_villain(u, start, stop, gate)
             open_gate(gate, gate, rates[0][:, u : u + 1])
 
-        def hero_piece(u, start, stop, z):
-            read_hero(u, start, stop, gates[u][:, start:stop], z)
-            if stop == PAIRS:
-                for t in range(PACK):
-                    nc.sync.dma_start(z0_dealt[32 * u : 32 * (u + 1), t, :], z0_plain[u][t:P:PACK, :])
-
-        def pieces(read, u, cuts, row):
-            return [(read, u, start, stop, row[:, start:stop]) for start, stop in zip(cuts, cuts[1:])]
+        def hero_whole(u):
+            read_hero(u, 0, PAIRS, gates[u][:], z0_plain[u][:])
+            for t in range(PACK):
+                nc.sync.dma_start(z0_dealt[32 * u : 32 * (u + 1), t, :], z0_plain[u][t:P:PACK, :])
 
         reads = []
-        for kind, u in ((0, 0), (0, 1), (1, 0), (1, 1), (0, 2), (0, 3), (1, 2), (1, 3)):
-            if kind:
-                reads.extend(pieces(hero_piece, u, HERO_CUTS, z0_plain[u][:]))
-            else:
-                reads.extend(pieces(villain_piece, u, VILLAIN_CUTS, gates[u][:]))
-        for u in (4, 5, 7, 6):
-            reads.extend(pieces(read_villain, u, (0, early), raw_early[:, u - PACK, :]))
+        for u in range(PACK):
+            for start, stop in zip(VILLAIN_CUTS, VILLAIN_CUTS[1:]):
+                reads.append((villain_piece, u, start, stop, gates[u][:, start:stop], gates[u][:, start:stop]))
+        for u in (4, 5):
+            for i in range(3):
+                row = raw_rows[:, 3 * (u - PACK) + i, :]
+                reads.append((read_villain, u, P * i, P * (i + 1), row[:, 0:P], row))
+        for u in (7, 6):
+            reads.append((read_villain, u, 0, early, raw_rows[:, u, :], raw_rows[:, u, :]))
 
         scatter(1, 0, S, make_h(1, H_ROWS + 10), plain_weights)
         plan = []
@@ -297,7 +295,7 @@ def tile_list_hero_villain_reads_kernel(
             sums = [multiply_h(u, HALF * c, HALF * (c + 1), (2 * u + 1 + c) % H_BANKS) for c in range(2)]
             for step, (tile, start, stop) in enumerate(plan):
                 if tile == u:
-                    h = reads[step + 1][4][:, 0 : stop - start]
+                    h = reads[step + 1][5][:, 0 : stop - start]
                     for c in range(start // HALF, (stop - 1) // HALF + 1):
                         first, last = max(start, HALF * c), min(stop, HALF * (c + 1))
                         nc.scalar.copy(
@@ -307,11 +305,14 @@ def tile_list_hero_villain_reads_kernel(
 
         for u in range(2, TILES):
             park_h(u)
-        for step, (read, u, start, stop, row) in enumerate(reads):
+        for step, (read, u, start, stop, row, room) in enumerate(reads):
             if step < len(plan):
                 tile, first, last = plan[step]
                 scatter(tile, first, last, parked[step], plain_weights if tile < PACK else dealt_weights[tile - PACK])
             read(u, start, stop, row)
+            done, rest = divmod(step + 1 - HERO_LAG, PACK)
+            if rest == 0 and 1 <= done <= PACK:
+                hero_whole(done - 1)
         w3_staged = held([P, 2, N, PACK], BF16, "w3_staged", "w1_raw%d" % PASS)
         for a in range(2):
             for start in range(0, N, QUARTER):
@@ -445,7 +446,15 @@ def tile_list_hero_villain_reads_kernel(
                 )
             return acc
 
-        gates_early = open_gates(raw_early, "gates_early", Z_DEALT)
+        gates_early = placed([P, PACK, early], F32, "gates_early", Z_DEALT)
+        for t in range(2):
+            open_gate(
+                gates_early[:, t, :].rearrange("p (i m) -> p i m", i=3),
+                raw_rows[:, 3 * t : 3 * t + 3, 0:P],
+                rates[1][:, t : t + 1],
+            )
+        for t in range(2, PACK):
+            open_gate(gates_early[:, t, :], raw_rows[:, PACK + t, :], rates[1][:, t : t + 1])
         z0_early = quantise(z0_staged[:, 0:HALF, :], "z0_early")
         for c in (0, 1, 3):
             multiply(c, 0, *z0_operand(z0_early, c, 0))

@@ -36,10 +36,8 @@ LAST = len(WIDTHS) - 1
 BANKS = ((4, 5, 6, 7), (0, 1), (4, 5, 6, 7), (2, 3), (0, 1), (4, 6))
 ROW_KIB = 4
 Z_PLAIN, Z_DEALT, WEIGHTS, GATES, H_ROWS = 0, 16, 32, 48, 64
-SCATTER_CUTS = (0, 256, 512, 768, 1024)
-LAST_SCATTER_CUTS = (0, 384, 768, 1024)
-VILLAIN_CUTS = (0, 256, 512, 768, 1024)
-HERO_LAG = 4
+QUARTERS = (0, 256, 512, 768, 1024)
+THIRDS = (0, 384, 768, 1024)
 TAIL = T2 // 8
 BANK_KIB = 2
 
@@ -258,7 +256,8 @@ def tile_list_hero_villain_reads_kernel(
         z0_dealt = placed([P, PACK, PAIRS], F32, "z0_dealt", Z_DEALT)
         early = WIDTHS[0] + WIDTHS[1]
         early_place = H_ROWS
-        raw_rows = placed([P, 8, early], F32, "raw_early", early_place)
+        raw_rows = placed([P, PACK, HALF], F32, "raw_early", early_place)
+        raw_early = raw_rows[:, :, 0:early]
 
         def villain_piece(u, start, stop, gate):
             read_villain(u, start, stop, gate)
@@ -269,51 +268,41 @@ def tile_list_hero_villain_reads_kernel(
             for t in range(PACK):
                 nc.sync.dma_start(z0_dealt[32 * u : 32 * (u + 1), t, :], z0_plain[u][t:P:PACK, :])
 
-        reads = []
-        for u in range(PACK):
-            for start, stop in zip(VILLAIN_CUTS, VILLAIN_CUTS[1:]):
-                reads.append((villain_piece, u, start, stop, gates[u][:, start:stop], gates[u][:, start:stop]))
-        for u in (4, 5):
-            for i in range(3):
-                row = raw_rows[:, 3 * (u - PACK) + i, :]
-                reads.append((read_villain, u, P * i, P * (i + 1), row[:, 0:P], row))
-        for u in (7, 6):
-            reads.append((read_villain, u, 0, early, raw_rows[:, u, :], raw_rows[:, u, :]))
+        def villain_pieces(u, cuts):
+            return [(villain_piece, u, a, b, gates[u][:, a:b], gates[u][:, a:b]) for a, b in zip(cuts, cuts[1:])]
+
+        def park_h(u, cuts, rooms):
+            sums = [multiply_h(u, HALF * c, HALF * (c + 1), (2 * u + 1 + c) % H_BANKS) for c in range(2)]
+            weights = plain_weights if u < PACK else dealt_weights[u - PACK]
+            puts = []
+            for start, stop, room in zip(cuts, cuts[1:], rooms):
+                c, at = divmod(start, HALF)
+                nc.scalar.copy(room[:, 0 : stop - start], sums[c][:, at : at + stop - start])
+                puts.append((u, start, stop, room[:, 0 : stop - start], weights))
+            return puts
+
+        def weave(u, cuts, reads, last_room):
+            count = 2 * (len(cuts) - 1)
+            skip = count - len(reads)
+            rooms = [read[5] for read in reads[1 - skip :]] + last_room
+            pair = [park_h(u + i, cuts, rooms[i::2]) for i in range(2)]
+            for step in range(count):
+                scatter(*pair[step % 2][step // 2])
+                if step >= skip:
+                    read, tile, start, stop, row, room = reads[step - skip]
+                    read(tile, start, stop, row)
 
         scatter(1, 0, S, make_h(1, H_ROWS + 10), plain_weights)
-        plan = []
-        for u in range(2, TILES, 2):
-            first = [(u, a, b) for a, b in zip(SCATTER_CUTS, SCATTER_CUTS[1:])]
-            cuts = SCATTER_CUTS if u + 2 < TILES else LAST_SCATTER_CUTS
-            second = [(u + 1, a, b) for a, b in zip(cuts, cuts[1:])]
-            for i, piece in enumerate(first):
-                plan.append(piece)
-                plan.extend(second[i : i + 1])
-        parked = {}
-
-        def park_h(u):
-            sums = [multiply_h(u, HALF * c, HALF * (c + 1), (2 * u + 1 + c) % H_BANKS) for c in range(2)]
-            for step, (tile, start, stop) in enumerate(plan):
-                if tile == u:
-                    h = reads[step + 1][5][:, 0 : stop - start]
-                    for c in range(start // HALF, (stop - 1) // HALF + 1):
-                        first, last = max(start, HALF * c), min(stop, HALF * (c + 1))
-                        nc.scalar.copy(
-                            h[:, first - start : last - start], sums[c][:, first - HALF * c : last - HALF * c]
-                        )
-                    parked[step] = h
-
-        for u in range(2, TILES):
-            park_h(u)
-        for step, (read, u, start, stop, row, room) in enumerate(reads):
-            if step < len(plan):
-                tile, first, last = plan[step]
-                scatter(tile, first, last, parked[step], plain_weights if tile < PACK else dealt_weights[tile - PACK])
-            read(u, start, stop, row)
-            done, rest = divmod(step + 1 - HERO_LAG, PACK)
-            if rest == 0 and 1 <= done <= PACK:
-                hero_whole(done - 1)
-        w3_staged = held([P, 2, N, PACK], BF16, "w3_staged", "w1_raw%d" % PASS)
+        weave(2, QUARTERS, villain_pieces(0, QUARTERS) + villain_pieces(1, QUARTERS), [z0_plain[0][:]])
+        for u in (0, 1):
+            hero_whole(u)
+        weave(4, QUARTERS, villain_pieces(2, QUARTERS) + villain_pieces(3, THIRDS), [z0_plain[2][:]])
+        for u in (2, 3):
+            hero_whole(u)
+        early_reads = [(read_villain, PACK + t, 0, early, raw_early[:, t, :], raw_rows[:, t, :]) for t in range(PACK)]
+        weave(6, (0, HALF, S), early_reads[:-1], [raw_rows[:, PACK - 1, :]])
+        read_villain(TILES - 1, 0, early, raw_early[:, PACK - 1, :])
+        w3_staged = placed([P, 2, N, PACK], BF16, "w3_staged", GATES + ROW_KIB)
         for a in range(2):
             for start in range(0, N, QUARTER):
                 cols = slice(start, start + QUARTER)
@@ -446,15 +435,7 @@ def tile_list_hero_villain_reads_kernel(
                 )
             return acc
 
-        gates_early = placed([P, PACK, early], F32, "gates_early", Z_DEALT)
-        for t in range(2):
-            open_gate(
-                gates_early[:, t, :].rearrange("p (i m) -> p i m", i=3),
-                raw_rows[:, 3 * t : 3 * t + 3, 0:P],
-                rates[1][:, t : t + 1],
-            )
-        for t in range(2, PACK):
-            open_gate(gates_early[:, t, :], raw_rows[:, PACK + t, :], rates[1][:, t : t + 1])
+        gates_early = open_gates(raw_early, "gates_early", Z_DEALT)
         z0_early = quantise(z0_staged[:, 0:HALF, :], "z0_early")
         for c in (0, 1, 3):
             multiply(c, 0, *z0_operand(z0_early, c, 0))

@@ -224,12 +224,14 @@ def tile_list_hero_villain_reads_kernel(
         load_pair(2)
         villains = load_list(offs4, "villains")
         load_tail(2)
-        heroes = load_list(offs3, "heroes")
         dealt_weights = []
         for t in range(0, PACK, 2):
             dealt_weights.extend(load_dealt_weights(t, 2))
-            load_pair(PACK + t)
-            load_tail(PACK + t)
+        load_pair(PACK)
+        heroes = load_list(offs3, "heroes")
+        load_tail(PACK)
+        for u in (6, 7):
+            pages[u] = load_page(u)
         w3_raw = held([P, 2, PACK, N], F32, "w3_raw", "table_words")
         nc.sync.dma_start(
             w3_raw[:].rearrange("p a j n -> p a (j n)"), w3.rearrange("(a p j) n -> p a (j n)", p=P, j=PACK)
@@ -256,52 +258,59 @@ def tile_list_hero_villain_reads_kernel(
         z0_dealt = placed([P, PACK, PAIRS], F32, "z0_dealt", Z_DEALT)
         early = WIDTHS[0] + WIDTHS[1]
         early_place = H_ROWS
-        raw_rows = placed([P, PACK, HALF], F32, "raw_early", early_place)
-        raw_early = raw_rows[:, :, 0:early]
+        raw_rows = placed([P, 6, early], F32, "raw_early", early_place)
 
         def villain_piece(u, start, stop, gate):
             read_villain(u, start, stop, gate)
             open_gate(gate, gate, rates[0][:, u : u + 1])
 
-        def hero_whole(u):
-            read_hero(u, 0, PAIRS, gates[u][:], z0_plain[u][:])
+        def hero_row(u, start, stop, z):
+            read_hero(u, start, stop, gates[u][:], z)
             for t in range(PACK):
                 nc.sync.dma_start(z0_dealt[32 * u : 32 * (u + 1), t, :], z0_plain[u][t:P:PACK, :])
 
         def villain_pieces(u, cuts):
             return [(villain_piece, u, a, b, gates[u][:, a:b], gates[u][:, a:b]) for a, b in zip(cuts, cuts[1:])]
 
-        def park_h(u, cuts, rooms):
-            sums = [multiply_h(u, HALF * c, HALF * (c + 1), (2 * u + 1 + c) % H_BANKS) for c in range(2)]
-            weights = plain_weights if u < PACK else dealt_weights[u - PACK]
-            puts = []
-            for start, stop, room in zip(cuts, cuts[1:], rooms):
-                c, at = divmod(start, HALF)
-                nc.scalar.copy(room[:, 0 : stop - start], sums[c][:, at : at + stop - start])
-                puts.append((u, start, stop, room[:, 0 : stop - start], weights))
-            return puts
+        def hero(u):
+            return [(hero_row, u, 0, PAIRS, z0_plain[u][:], z0_plain[u][:])]
 
-        def weave(u, cuts, reads, last_room):
-            count = 2 * (len(cuts) - 1)
-            skip = count - len(reads)
-            rooms = [read[5] for read in reads[1 - skip :]] + last_room
-            pair = [park_h(u + i, cuts, rooms[i::2]) for i in range(2)]
-            for step in range(count):
-                scatter(*pair[step % 2][step // 2])
-                if step >= skip:
-                    read, tile, start, stop, row, room = reads[step - skip]
-                    read(tile, start, stop, row)
+        def early_pieces(u, first_row, count):
+            width = early // count
+            rows = [raw_rows[:, first_row + i, :] for i in range(count)]
+            return [(read_villain, u, width * i, width * (i + 1), rows[i][:, 0:width], rows[i]) for i in range(count)]
+
+        second, third = villain_pieces(2, THIRDS), villain_pieces(3, THIRDS)
+        reads = villain_pieces(0, QUARTERS) + villain_pieces(1, QUARTERS)
+        reads = reads + hero(0) + second[:1] + hero(1) + second[1:] + third
+        reads = reads + hero(2) + hero(3) + early_pieces(4, 0, 2) + early_pieces(5, 2, 2)
+        reads = reads + early_pieces(7, 5, 1) + early_pieces(6, 4, 1)
+        plan = []
+        for u in range(2, TILES, 2):
+            cuts = QUARTERS if u + 2 < TILES else THIRDS
+            others = [(u + 1, a, b) for a, b in zip(cuts, cuts[1:])]
+            for i, (a, b) in enumerate(zip(QUARTERS, QUARTERS[1:])):
+                plan.append((u, a, b))
+                plan.extend(others[i : i + 1])
 
         scatter(1, 0, S, make_h(1, H_ROWS + 10), plain_weights)
-        weave(2, QUARTERS, villain_pieces(0, QUARTERS) + villain_pieces(1, QUARTERS), [z0_plain[0][:]])
-        for u in (0, 1):
-            hero_whole(u)
-        weave(4, QUARTERS, villain_pieces(2, QUARTERS) + villain_pieces(3, THIRDS), [z0_plain[2][:]])
-        for u in (2, 3):
-            hero_whole(u)
-        early_reads = [(read_villain, PACK + t, 0, early, raw_early[:, t, :], raw_rows[:, t, :]) for t in range(PACK)]
-        weave(6, (0, HALF, S), early_reads[:-1], [raw_rows[:, PACK - 1, :]])
-        read_villain(TILES - 1, 0, early, raw_early[:, PACK - 1, :])
+        parked = {}
+        for u in range(2, TILES):
+            sums = [multiply_h(u, HALF * c, HALF * (c + 1), (2 * u + 1 + c) % H_BANKS) for c in range(2)]
+            for step, (tile, start, stop) in enumerate(plan):
+                if tile == u:
+                    h = reads[step + 1][5][:, 0 : stop - start]
+                    for c in range(start // HALF, (stop - 1) // HALF + 1):
+                        first, last = max(start, HALF * c), min(stop, HALF * (c + 1))
+                        nc.scalar.copy(
+                            h[:, first - start : last - start], sums[c][:, first - HALF * c : last - HALF * c]
+                        )
+                    parked[step] = h
+        for step, (read, u, start, stop, row, room) in enumerate(reads):
+            if step < len(plan):
+                tile, first, last = plan[step]
+                scatter(tile, first, last, parked[step], plain_weights if tile < PACK else dealt_weights[tile - PACK])
+            read(u, start, stop, row)
         w3_staged = placed([P, 2, N, PACK], BF16, "w3_staged", GATES + ROW_KIB)
         for a in range(2):
             for start in range(0, N, QUARTER):
@@ -435,7 +444,15 @@ def tile_list_hero_villain_reads_kernel(
                 )
             return acc
 
-        gates_early = open_gates(raw_early, "gates_early", Z_DEALT)
+        gates_early = placed([P, PACK, early], F32, "gates_early", Z_DEALT)
+        for t in range(2):
+            open_gate(
+                gates_early[:, t, :].rearrange("p (i m) -> p i m", i=2),
+                raw_rows[:, 2 * t : 2 * t + 2, 0 : early // 2],
+                rates[1][:, t : t + 1],
+            )
+        for t in range(2, PACK):
+            open_gate(gates_early[:, t, :], raw_rows[:, 2 + t, :], rates[1][:, t : t + 1])
         z0_early = quantise(z0_staged[:, 0:HALF, :], "z0_early")
         for c in (0, 1, 3):
             multiply(c, 0, *z0_operand(z0_early, c, 0))
@@ -452,7 +469,7 @@ def tile_list_hero_villain_reads_kernel(
         results_place = Z_PLAIN + ROW_KIB
         finish_on_gpsimd(0, 0, gates_late_place + BANK_KIB, results_place, 2)
         finish_on_gpsimd(0, 1, WEIGHTS, results_place + BANK_KIB, 2)
-        finish_on_gpsimd(1, 0, WEIGHTS + 2 * BANK_KIB, results_place + 2 * BANK_KIB, 1)
+        finish_on_gpsimd(1, 0, WEIGHTS + 2 * BANK_KIB, results_place + 2 * BANK_KIB, 2)
         multiply(2, 0, *z0_operand(z0_2, 2, STARTS[2]))
         raw_late = read_villains(early, PAIRS, "raw_late", z_1_place)
         gates_late = open_gates(raw_late, "gates_late", gates_late_place)

from contextlib import ExitStack

import concourse.mybir as mybir

K, T, S, H, T2, PAIRS, N = 512, 4096, 1024, 1024, 2048, 1024, 512
FLOPS = 2 * K * H * S + 2 * 2 * H * N * PAIRS

F32 = mybir.dt.float32
BF16 = mybir.dt.bfloat16
I32 = mybir.dt.int32
U32 = mybir.dt.uint32
U16 = mybir.dt.uint16
U8 = mybir.dt.uint8
FP8X4 = mybir.dt.float8_e4m3fn_x4
FP4X4 = mybir.dt.float4_e2m1fn_x4
MULT = mybir.AluOpType.mult
SIGMOID = mybir.ActivationFunctionType.Sigmoid
TANH = mybir.ActivationFunctionType.Tanh

P = 128
PACK = 4
PASS = P * PACK
TILES = H // P
BANK = 512
HALF = S // 2
QUARTER = S // 4
FIRST = 384
LEAD = T // 4
AHEAD = T2 // 4
ROW0, ROW_STEP = 11, 7
H_BANKS = 4
H_BUFFERS = 3
WIDTHS = (256, 128, 256, 128, 128, 128)
STARTS = (0, 256, 512, 384, 768, 896)
LAST = len(WIDTHS) - 1
BANKS = ((4, 5, 6, 7), (0, 1), (4, 5, 6, 7), (2, 3), (0, 1), (4, 6))
ROW_KIB = 4
Z_PLAIN, Z_DEALT, WEIGHTS, GATES, H_ROWS = 0, 16, 32, 48, 64
QUARTERS = (0, 256, 512, 768, 1024)
THIRDS = (0, 384, 768, 1024)
TAIL = T2 // 8
BANK_KIB = 2


def list_slice(offsets, start, stop):
    return offsets[:, start // 16 : stop // 16]


def tile_list_hero_villain_reads_kernel(
    tc, tab_words, tab_scales, offs, offs2, offs3, offs4, w1, wgs, page0, rate, w2_words, w2_scales, w3, out
):
    nc = tc.nc
    with ExitStack() as ctx:
        lists = ctx.enter_context(tc.tile_pool(name="lists", bufs=1))
        keep = ctx.enter_context(tc.tile_pool(name="keep", bufs=1))
        shared = ctx.enter_context(tc.tile_pool(name="shared", bufs=1))
        psum = ctx.enter_context(tc.psum_pool(name="psum", bufs=1))

        def held(shape, dtype, name, tag=None):
            return keep.tile(shape, dtype, name=name, tag=tag or name, align_bytes=256)

        def placed(shape, dtype, name, place):
            return shared.tile(shape, dtype, name=name, tag=name, align_bytes=256, offset=1024 * place)

        def bank(index, name):
            return psum.tile([P, BANK], F32, name=name, tag="bank%d" % index)

        table_scales = held([P, T], U8, "table_scales")
        nc.vector.memset(table_scales[:].bitcast(I32), 0)
        v_scales = [held([P, HALF], U8, "v_scales%d" % c) for c in range(2)]
        for c in range(2):
            nc.vector.memset(v_scales[c][:].bitcast(I32), 0)
        w2_scale_rows = held([P, 2, N], U8, "w2_scale_rows")
        nc.vector.memset(w2_scale_rows[:].rearrange("p a c -> p (a c)").bitcast(I32), 0)

        def load_list(src, name):
            tile = lists.tile([P, S // 16], U16, name=name)
            nc.sync.dma_start(tile[:], src)
            return tile

        def load_w1(start, stop):
            raw = held([P, PACK, stop - start], F32, "w1_raw%d" % start)[:]
            nc.sync.dma_start(raw, w1[:, start:stop].rearrange("(p j) c -> p j c", j=PACK))
            return raw

        def load_dealt_weights(first, count):
            tile = placed([P, count * S], F32, "wgs_rows%d" % first, WEIGHTS + ROW_KIB * first)
            rows = wgs.rearrange("(q t) j -> q (t j)", t=PACK)[:, S * first : S * (first + count)]
            for q in (0, 2, 1, 3):
                nc.sync.dma_start(tile[32 * q : 32 * (q + 1), :], rows)
            return [tile[:, S * t : S * (t + 1)] for t in range(count)]

        def page_rows(u):
            if u < PACK:
                return page0[P * u : P * (u + 1), :]
            return page0[PASS:, :].rearrange("(p t) c -> t p c", t=PACK)[u - PACK]

        def load_page(u):
            tile = held([P, T2], F32, "page%d" % u)
            nc.sync.dma_start(tile[:], page_rows(u))
            return tile

        def load_pair(u):
            pages[u + 1] = held([P, T2], F32, "page%d" % (u + 1))
            nc.sync.dma_start(pages[u + 1][:, 0 : T2 - TAIL], page_rows(u + 1)[:, 0 : T2 - TAIL])
            pages[u] = load_page(u)

        def load_tail(u):
            nc.sync.dma_start(pages[u + 1][:, T2 - TAIL : T2], page_rows(u + 1)[:, T2 - TAIL : T2])

        def interleave(staged, rows):
            nc.scalar.copy(staged.rearrange("p (c i) t -> p c t i", i=4), rows.rearrange("p t (c i) -> p c t i", i=4))

        def quantise(staged, name, place=None):
            width = staged.shape[1]
            if place is None:
                codes = held([P, width], U32, name + "_codes")
            else:
                codes = placed([P, width], U32, name + "_codes", place)
            scales = held([P, width], U8, name + "_scales")
            nc.vector.quantize_mx(
                out=codes[:].bitcast(FP8X4), scales=scales[:], in_=staged.rearrange("p m t -> p (m t)")
            )
            return codes, scales

        w1_q = {}

        def prepare_w1(raw, start, stop):
            staged = held([P, stop - start, PACK], BF16, "w1_staged%d" % start)
            if start < PASS:
                interleave(staged[:], raw)
            else:
                nc.scalar.copy(
                    staged[:].rearrange("p (t m) j -> p m t j", t=PACK),
                    raw.rearrange("p j (m t) -> p m t j", t=PACK),
                )
            codes, scales = quantise(staged[:], "w1_%d" % start)
            for u in range(start // P, stop // P):
                cols = slice(P * u - start, P * (u + 1) - start)
                w1_q[u] = (codes[:, cols], scales[:, cols])

        def pick_scales(c):
            picked = held([P, HALF], U8, "picked_scales%d" % c)
            nc.vector.tensor_copy(picked[:], table_scales[:].indirect(list_slice(picks, HALF * c, HALF * (c + 1))))
            return picked

        def move_scales(c, picked):
            for r in range(4):
                first = ROW0 + ROW_STEP * r
                rows = picked[first : first + 12 * ROW_STEP + 1 : 4 * ROW_STEP, :]
                nc.sync.dma_start(v_scales[c][r:P:32, :].bitcast(I32), rows.bitcast(I32))

        w1_tile0 = load_w1(0, P)
        picks = load_list(offs, "picks")
        slots = load_list(offs2, "slots")
        table_words = held([P, T], U32, "table_words")
        words = tab_words[0].rearrange("p n t -> p (n t)").bitcast(I32)
        nc.sync.dma_start(table_words[:, 0:LEAD].bitcast(I32), words[:, 0:LEAD])
        rows_end = ROW0 + 15 * ROW_STEP + 1
        nc.sync.dma_start(table_scales[ROW0:rows_end:ROW_STEP, :].bitcast(I32), tab_scales[0].bitcast(I32))
        nc.sync.dma_start(table_words[:, LEAD:T].bitcast(I32), words[:, LEAD:T])
        plain_weights = held([P, S], F32, "wgs_plain")
        nc.sync.dma_start(plain_weights[:, 0:FIRST], wgs[:, 0:FIRST])
        pages = [held([P, T2], F32, "page0")]
        nc.sync.dma_start(pages[0][:, 0:AHEAD], page0[0:P, 0:AHEAD])
        picked = [pick_scales(0)]
        move_scales(0, picked[0])
        prepare_w1(w1_tile0, 0, P)
        picked.append(pick_scales(1))
        nc.sync.dma_start(pages[0][:, AHEAD:T2], page0[0:P, AHEAD:T2])
        w1_tile1 = load_w1(P, 2 * P)
        move_scales(1, picked[1])
        nc.sync.dma_start(plain_weights[:, FIRST:S], wgs[:, FIRST:S])
        w1_tiles23 = load_w1(2 * P, PASS)
        v_words = held([P, S], U32, "v_words")
        for start, stop in ((0, FIRST), (FIRST, S)):
            nc.vector.tensor_copy(v_words[:, start:stop], table_words[:].indirect(list_slice(picks, start, stop)))

        def multiply_h(u, start, stop, index):
            codes, scales = w1_q[u]
            c, at = divmod(start, HALF)
            acc = bank(index, "h_acc")
            nc.tensor.matmul_mx(
                out=acc[:, 0 : stop - start],
                lhsT=codes.bitcast(FP8X4),
                lhsT_scale=scales,
                rhs=v_words[:, start:stop].bitcast(FP8X4),
                rhs_scale=v_scales[c][:, at : at + stop - start],
                start=True,
                stop=True,
            )
            return acc

        def make_h(u, place):
            rows = placed([P, S], F32, "h%d" % u, place)
            for c in range(2):
                acc = multiply_h(u, HALF * c, HALF * (c + 1), (2 * u + 1 + c) % H_BANKS)
                nc.scalar.copy(rows[:, HALF * c : HALF * (c + 1)], acc[:])
            return rows[:]

        def scatter(u, start, stop, h, weights):
            nc.vector.tensor_tensor(
                pages[u][:].indirect(list_slice(slots, start, stop)),
                h,
                weights[:, start:stop],
                MULT,
            )

        first_h = placed([P, S], F32, "h0", H_ROWS + 6)
        for index, (start, stop) in enumerate(((0, QUARTER), (QUARTER, FIRST), (FIRST, HALF), (HALF, S))):
            nc.scalar.copy(first_h[:, start:stop], multiply_h(0, start, stop, index)[:, 0 : stop - start])
        scatter(0, 0, FIRST, first_h[:, 0:FIRST], plain_weights)
        prepare_w1(w1_tile1, P, 2 * P)
        scatter(0, FIRST, S, first_h[:, FIRST:S], plain_weights)
        prepare_w1(w1_tiles23, 2 * P, PASS)

        pages.extend([None] * (TILES - 1))
        pages[1] = load_page(1)
        prepare_w1(load_w1(PASS, H), PASS, H)
        rates = [held([P, PACK], F32, "rates%d" % a) for a in range(2)]
        with nc.allow_non_contiguous_dma(reason="one rate a partition"):
            nc.sync.dma_start(rates[0][:], rate[0:PASS].rearrange("(u p) -> p u", p=P))
        nc.sync.dma_start(rates[1][:], rate[PASS:H].rearrange("(p t) -> p t", t=PACK))
        load_pair(2)
        villains = load_list(offs4, "villains")
        load_tail(2)
        dealt_weights = []
        for t in range(0, PACK, 2):
            dealt_weights.extend(load_dealt_weights(t, 2))
        load_pair(PACK)
        heroes = load_list(offs3, "heroes")
        load_tail(PACK)
        for u in (6, 7):
            pages[u] = load_page(u)
        w3_raw = held([P, 2, PACK, N], F32, "w3_raw", "table_words")
        nc.sync.dma_start(
            w3_raw[:].rearrange("p a j n -> p a (j n)"), w3.rearrange("(a p j) n -> p a (j n)", p=P, j=PACK)
        )
        w2_codes = held([P, 2, 2 * N], U8, "w2_codes")
        nc.sync.dma_start(w2_codes[:].bitcast(I32), w2_words.rearrange("a p c -> p a c").bitcast(I32))
        for q in range(4):
            nc.sync.dma_start(
                w2_scale_rows[32 * q : 32 * q + 4, :, :].bitcast(I32),
                w2_scales[:, 4 * q : 4 * q + 4, :].rearrange("a r c -> r a c").bitcast(I32),
            )

        def read_villain(u, start, stop, raw):
            nc.vector.tensor_copy(raw, pages[u][:].indirect(list_slice(villains, start, stop)))

        def open_gate(gate, raw, rate_column):
            nc.scalar.activation(gate, raw, SIGMOID, scale=rate_column)

        def read_hero(u, start, stop, gate, z):
            nc.vector.tensor_tensor(z, pages[u][:].indirect(list_slice(heroes, start, stop)), gate, MULT)

        gates = [placed([P, PAIRS], F32, "gate%d" % u, GATES + ROW_KIB * u) for u in range(PACK)]
        z0_plain = [placed([P, PAIRS], F32, "z0_plain%d" % u, Z_PLAIN + ROW_KIB * u) for u in range(PACK)]
        z0_dealt = placed([P, PACK, PAIRS], F32, "z0_dealt", Z_DEALT)
        early = WIDTHS[0] + WIDTHS[1]
        early_place = H_ROWS
        raw_rows = placed([P, 6, early], F32, "raw_early", early_place)

        def villain_piece(u, start, stop, gate):
            read_villain(u, start, stop, gate)
            open_gate(gate, gate, rates[0][:, u : u + 1])

        def hero_row(u, start, stop, z):
            read_hero(u, start, stop, gates[u][:], z)
            for t in range(PACK):
                nc.sync.dma_start(z0_dealt[32 * u : 32 * (u + 1), t, :], z0_plain[u][t:P:PACK, :])

        def villain_pieces(u, cuts):
            return [(villain_piece, u, a, b, gates[u][:, a:b], gates[u][:, a:b]) for a, b in zip(cuts, cuts[1:])]

        def hero(u):
            return [(hero_row, u, 0, PAIRS, z0_plain[u][:], z0_plain[u][:])]

        def early_pieces(u, first_row, count):
            width = early // count
            rows = [raw_rows[:, first_row + i, :] for i in range(count)]
            return [(read_villain, u, width * i, width * (i + 1), rows[i][:, 0:width], rows[i]) for i in range(count)]

        second, third = villain_pieces(2, THIRDS), villain_pieces(3, THIRDS)
        reads = villain_pieces(0, QUARTERS) + villain_pieces(1, QUARTERS)
        reads = reads + hero(0) + second[:1] + hero(1) + second[1:] + third
        reads = reads + hero(2) + hero(3) + early_pieces(4, 0, 2) + early_pieces(5, 2, 2)
        reads = reads + early_pieces(7, 5, 1) + early_pieces(6, 4, 1)
        plan = []
        for u in range(2, TILES, 2):
            cuts = QUARTERS if u + 2 < TILES else THIRDS
            others = [(u + 1, a, b) for a, b in zip(cuts, cuts[1:])]
            for i, (a, b) in enumerate(zip(QUARTERS, QUARTERS[1:])):
                plan.append((u, a, b))
                plan.extend(others[i : i + 1])

        scatter(1, 0, S, make_h(1, H_ROWS + 10), plain_weights)
        parked = {}
        for u in range(2, TILES):
            sums = [multiply_h(u, HALF * c, HALF * (c + 1), (2 * u + 1 + c) % H_BANKS) for c in range(2)]
            for step, (tile, start, stop) in enumerate(plan):
                if tile == u:
                    h = reads[step + 1][5][:, 0 : stop - start]
                    for c in range(start // HALF, (stop - 1) // HALF + 1):
                        first, last = max(start, HALF * c), min(stop, HALF * (c + 1))
                        nc.scalar.copy(
                            h[:, first - start : last - start], sums[c][:, first - HALF * c : last - HALF * c]
                        )
                    parked[step] = h
        for step, (read, u, start, stop, row, room) in enumerate(reads):
            if step < len(plan):
                tile, first, last = plan[step]
                scatter(tile, first, last, parked[step], plain_weights if tile < PACK else dealt_weights[tile - PACK])
            read(u, start, stop, row)
        w3_staged = placed([P, 2, N, PACK], BF16, "w3_staged", GATES + ROW_KIB)
        for a in range(2):
            for start in range(0, N, QUARTER):
                cols = slice(start, start + QUARTER)
                interleave(w3_staged[:, a, cols, :], w3_raw[:, a, :, cols])
        w3_q = [quantise(w3_staged[:, 0], "w3_0")]
        z0_staged = held([P, PAIRS, PACK], BF16, "z0_staged")
        for start in reversed(range(0, PAIRS, QUARTER)):
            interleave(z0_staged[:, start : start + QUARTER, :], z0_dealt[:, :, start : start + QUARTER])

        y2_sums = {}
        y1_sums = {}

        def multiply_group(acc, c, a, g, stationary, z_codes, z_scales):
            width = WIDTHS[c]
            per_bank = BANK // width
            for i in range(per_bank):
                codes, scales = stationary(a, per_bank * g + i)
                nc.tensor.matmul_mx(
                    out=acc[:, width * i : width * (i + 1)],
                    lhsT=codes,
                    lhsT_scale=scales,
                    rhs=z_codes.bitcast(FP8X4),
                    rhs_scale=z_scales,
                    start=(a == 0 and i == 0),
                    stop=(a == 1 and i == per_bank - 1),
                )

        def w3_operand(a, n):
            codes, scales = w3_q[a]
            cols = slice(P * n, P * (n + 1))
            return codes[:, cols].bitcast(FP8X4), scales[:, cols]

        def w2_operand(a, n):
            codes = w2_codes[:, a, 2 * P * n : 2 * P * (n + 1)].bitcast(FP4X4)
            return codes, w2_scale_rows[:, a, P * n : P * (n + 1)]

        def multiply_y2(c, a, g, z_codes, z_scales):
            if a == 0:
                y2_sums[c, g] = bank(BANKS[c][2 * g], "y_acc")
            multiply_group(y2_sums[c, g], c, a, g, w3_operand, z_codes, z_scales)

        def multiply_y1(c, a, g, z_codes, z_scales):
            if a == 0:
                y1_sums[c, g] = bank(BANKS[c][2 * g + 1], "y_acc")
            multiply_group(y1_sums[c, g], c, a, g, w2_operand, z_codes, z_scales)

        def multiply(c, a, z_codes, z_scales):
            for g in range(N // P * WIDTHS[c] // BANK):
                multiply_y2(c, a, g, z_codes, z_scales)
                multiply_y1(c, a, g, z_codes, z_scales)

        def store(c, n, count, result):
            nc.sync.dma_start(
                out[P * n : P * (n + count), STARTS[c] : STARTS[c] + WIDTHS[c]].rearrange("(i p) m -> p i m", p=P),
                result.rearrange("p (i m) -> p i m", i=count),
            )

        def squash(c, g, place):
            tanh_y2 = placed([P, BANK], F32, "tanh%d_%d" % (c, g), place)
            nc.scalar.activation(tanh_y2[:], y2_sums[c, g][:], TANH)
            return tanh_y2

        def finish_half(c, g, half, tanh_y2, result):
            per_bank = BANK // WIDTHS[c]
            cols = slice(BANK // 2 * half, BANK // 2 * (half + 1))
            nc.vector.tensor_tensor(result, y1_sums[c, g][:, cols], tanh_y2[:, cols], MULT)
            store(c, per_bank * g + per_bank // 2 * half, per_bank // 2, result)

        def finish(c, g, tanh_y2, place):
            result = placed([P, BANK], F32, "result%d_%d" % (c, g), place)
            for half in range(2):
                finish_half(c, g, half, tanh_y2, result[:, BANK // 2 * half : BANK // 2 * (half + 1)])

        def finish_on_gpsimd(c, g, operands, place, pieces):
            per_bank = BANK // WIDTHS[c]
            tanh_y2 = squash(c, g, operands)
            y1 = placed([P, BANK], F32, "y1_%d_%d" % (c, g), operands + BANK_KIB)
            nc.scalar.copy(y1[:], y1_sums[c, g][:])
            result = placed([P, BANK], F32, "result%d_%d" % (c, g), place)
            nc.gpsimd.tensor_tensor(result[:], y1[:], tanh_y2[:], MULT)
            for i in range(pieces):
                cols = slice(BANK // pieces * i, BANK // pieces * (i + 1))
                store(c, per_bank * g + per_bank // pieces * i, per_bank // pieces, result[:, cols])

        def read_villains(start, stop, name, place):
            raw = placed([P, PACK, stop - start], F32, name, place)
            for t in range(PACK):
                read_villain(PACK + t, start, stop, raw[:, t, :])
            return raw

        def open_gates(raw, name, place):
            opened = placed([P, PACK, raw.shape[2]], F32, name, place)
            for t in range(PACK):
                open_gate(opened[:, t, :], raw[:, t, :], rates[1][:, t : t + 1])
            return opened

        def read_chunk(c, opened, origin, place):
            start, stop = STARTS[c], STARTS[c] + WIDTHS[c]
            z = placed([P, PACK, WIDTHS[c]], F32, "z1_%d" % c, place)
            for t in range(PACK):
                read_hero(PACK + t, start, stop, opened[:, t, start - origin : stop - origin], z[:, t, :])
            return z

        def stage(c, z, tag):
            staged = held([P, WIDTHS[c], PACK], BF16, "z1_staged%d" % c, tag)
            interleave(staged[:], z[:])
            return staged

        def quantise_z1(c, staged):
            codes, scales = quantise(staged[:], "z1_q%d" % c)
            return codes[:], scales[:]

        def z0_operand(quantised, c, origin):
            codes, scales = quantised
            cols = slice(STARTS[c] - origin, STARTS[c] - origin + WIDTHS[c])
            return codes[:, cols], scales[:, cols]

        def multiply_half(acc, a, half, z_codes, z_scales):
            width = WIDTHS[LAST]
            for i in range(2):
                codes, scales = w3_operand(a, 2 * half + i)
                nc.tensor.matmul_mx(
                    out=acc[:, width * i : width * (i + 1)],
                    lhsT=codes,
                    lhsT_scale=scales,
                    rhs=z_codes.bitcast(FP8X4),
                    rhs_scale=z_scales,
                    start=(a == 0 and i == 0),
                    stop=(a == 1 and i == 1),
                )
            return acc

        gates_early = placed([P, PACK, early], F32, "gates_early", Z_DEALT)
        for t in range(2):
            open_gate(
                gates_early[:, t, :].rearrange("p (i m) -> p i m", i=2),
                raw_rows[:, 2 * t : 2 * t + 2, 0 : early // 2],
                rates[1][:, t : t + 1],
            )
        for t in range(2, PACK):
            open_gate(gates_early[:, t, :], raw_rows[:, 2 + t, :], rates[1][:, t : t + 1])
        z0_early = quantise(z0_staged[:, 0:HALF, :], "z0_early")
        for c in (0, 1, 3):
            multiply(c, 0, *z0_operand(z0_early, c, 0))
        z_0 = read_chunk(0, gates_early, 0, Z_PLAIN)
        z_1_place = early_place + 4
        z_1 = read_chunk(1, gates_early, 0, z_1_place)
        w3_q.append(quantise(w3_staged[:, 1], "w3_1", early_place))
        multiply(0, 1, *quantise_z1(0, stage(0, z_0, "w1_raw0")))
        staged1 = stage(1, z_1, "w1_staged0")
        z0_2 = quantise(z0_staged[:, STARTS[2] : STARTS[2] + WIDTHS[2], :], "z0_2", Z_PLAIN)
        multiply(1, 1, *quantise_z1(1, staged1))

        gates_late_place = Z_DEALT + 6
        results_place = Z_PLAIN + ROW_KIB
        finish_on_gpsimd(0, 0, gates_late_place + BANK_KIB, results_place, 2)
        finish_on_gpsimd(0, 1, WEIGHTS, results_place + BANK_KIB, 2)
        finish_on_gpsimd(1, 0, WEIGHTS + 2 * BANK_KIB, results_place + 2 * BANK_KIB, 2)
        multiply(2, 0, *z0_operand(z0_2, 2, STARTS[2]))
        raw_late = read_villains(early, PAIRS, "raw_late", z_1_place)
        gates_late = open_gates(raw_late, "gates_late", gates_late_place)

        even_place = WEIGHTS + 2 * ROW_KIB
        odd_place = z_1_place + 2
        z_2 = read_chunk(2, gates_late, early, even_place)
        z0_45 = quantise(z0_staged[:, STARTS[4] : PAIRS, :], "z0_45", z_1_place)
        multiply(4, 0, *z0_operand(z0_45, 4, STARTS[4]))
        z_3 = read_chunk(3, gates_late, early, odd_place)
        z1_2 = quantise_z1(2, stage(2, z_2, "w1_raw128"))
        for g in range(2):
            multiply_y2(2, 1, g, *z1_2)
        for g in range(2):
            multiply_y1(2, 1, g, *z1_2)
        z_4 = read_chunk(4, gates_late, early, even_place)
        multiply(3, 1, *quantise_z1(3, stage(3, z_3, "w1_staged128")))
        z_5 = read_chunk(LAST, gates_late, early, odd_place)

        tanh_places = [GATES + BANK_KIB * i for i in range(5)]
        tanh_2 = [squash(2, g, tanh_places[g]) for g in range(2)]
        z0_5 = z0_operand(z0_45, LAST, STARTS[4])
        last_y2 = [multiply_half(bank(BANKS[LAST][0], "y_acc"), 0, 0, *z0_5)]
        multiply_y1(LAST, 0, 0, *z0_5)
        staged4 = stage(4, z_4, "w1_raw256")
        tanh_3 = squash(3, 0, tanh_places[2])
        multiply(4, 1, *quantise_z1(4, staged4))
        last_y2.append(multiply_half(bank(BANKS[3][0], "y_acc"), 0, 1, *z0_5))
        staged5 = stage(LAST, z_5, "w1_staged256")

        finish(2, 0, tanh_2[0], even_place - 1)
        finish_half(2, 1, 0, tanh_2[1], placed([P, BANK // 2], F32, "result2_1a", even_place + 1)[:])
        z1_5 = quantise_z1(LAST, staged5)
        for half in range(2):
            multiply_half(last_y2[half], 1, half, *z1_5)
        multiply_y1(LAST, 1, 0, *z1_5)
        finish_half(2, 1, 1, tanh_2[1], placed([P, BANK // 2], F32, "result2_1b", odd_place)[:])
        finish(3, 0, tanh_3, odd_place + 1)
        finish(4, 0, squash(4, 0, tanh_places[3]), tanh_places[4] + BANK_KIB)
        tanh_5 = placed([P, BANK], F32, "tanh5", tanh_places[4])
        for half in range(2):
            cols = slice(BANK // 2 * half, BANK // 2 * (half + 1))
            nc.scalar.activation(tanh_5[:, cols], last_y2[half][:, 0 : BANK // 2], TANH)
        finish(LAST, 0, tanh_5, even_place + ROW_KIB)
